import numpy as np, ml_dtypes
CORES = [66,74,82,90,194,202,210,218]
N = 8
import mx_ref
BF = ml_dtypes.bfloat16
def gcols(t, e):
    v = np.concatenate([t.reshape(8, 16, -1, 4), np.zeros((8, 16, 1, 4), BF)], axis=2)
    return np.ascontiguousarray(np.stack([v[g][:, e[g]] for g in range(8)])).reshape(128, -1)
def tile(rs):
    return np.stack(rs, axis=2).reshape(128, -1).astype(BF)
def pick(q, e):
    c = np.concatenate([q[0].reshape(128, -1, 4), np.zeros((128, 1, 4), np.uint8)], axis=1); s = np.concatenate([q[1], np.ones((16, 1), np.uint8)], axis=1)
    return (np.ascontiguousarray(c[:, e].reshape(128, -1)), np.ascontiguousarray(s[:, e]))
def join(*qs):
    return (np.concatenate([q[0] for q in qs], axis=1), np.concatenate([q[1] for q in qs], axis=1))
def put(q, e, v):
    c, s = q[0].reshape(128, -1, 4).copy(), q[1].copy(); c[:, e] = v[0].reshape(128, -1, 4); s[:, e] = v[1]
    return (c.reshape(128, -1), s)
def pk(c, s):
    return (np.ascontiguousarray(c), mx_ref.live(s))
def emit(q):
    return q[0], q[1]
def packed(v, rng):
    q = [mx_ref.quantize(np.ascontiguousarray(v[r])) for r in range(N)]
    return np.stack([a for a, b in q]), np.stack([mx_ref.plane(b, rng) for a, b in q])
def values_of_codes():
    e, c = np.zeros((128, 128, 4), np.float32), np.zeros((128, 2, 4), np.uint8)
    e[np.arange(128), np.arange(128), 0] = 1
    c[:127, :, 0] = np.arange(256).reshape(2, 128).T[:127]
    return mx_ref.matmul(mx_ref.quantize(e.reshape(128, 512).astype(BF)), (c.reshape(128, 8), np.full((16, 2), 127, np.uint8))).T.reshape(-1).astype(np.float64)
CODE_VALUE, SCALE_VALUE = values_of_codes(), 2.0 ** (np.arange(256) - 127.0)
def decode(q):
    return (CODE_VALUE[q[0]].reshape(16, 8, -1, 4) * SCALE_VALUE[q[1]][:, None, :, None] + 0.0).reshape(128, -1).astype(np.float32)
def f(rng, *shape):
    return mx_ref.flush((rng.standard_normal(shape, dtype=np.float32) * np.exp2(rng.integers(-2, 3, shape[:-1] + (1,)))).astype(BF))
def wide(rng, *shape, cols=0):
    v = rng.standard_normal(shape, dtype=np.float32) * np.exp2(rng.integers(-12, 13, shape)).astype(np.float32)
    if cols: v *= np.repeat(np.exp2(rng.integers(-cols, cols + 1, shape[:-2] + (1, shape[-1] // 4))) * (rng.random(shape[:-2] + (1, shape[-1] // 4)) > 0.0625), 4, axis=-1).astype(np.float32)
    return mx_ref.flush(v.astype(BF))
C, R = 288, 2
def alike(w):
    return np.stack([w] * N)
def layers(rng):
    return f(rng, N, 128, 4096)
def weights(rng, w, still=()):
    w = np.array(w).reshape(N, 8, 16, 8, 8, 16, 4)
    for i in still:
        w[:, :, i] = 0
        w[:, :, :, :, :, i] = 0
    c, p = packed(w.reshape(N, 128, 4096), rng)
    return {"wc": c, "ws": p}
def numbers_of(rng):
    return {"x": np.array(f(rng, N, 128, 4 * C)), "u": alike(f(rng, 128, 512)), "v": np.array(f(rng, N, 128, 512))}
def unscored(rng):
    a = np.array(f(rng, 128, 512)).reshape(128, 128, 4)
    a[:, ::16] = 0
    a[:, 1::16] = 0
    return a
def setup_inputs(rng):
    return {**numbers_of(rng), **weights(rng, layers(rng))}
def setup_inputs_ties(rng):
    d = numbers_of(rng)
    o = rng.permutation(N)
    k = rng.integers(0, 3, (N, 8, C))
    m = np.where((o % 2 == 0)[:, None, None], k, rng.integers(-2, 3, (N, 8, C)))
    k[o == 0] = 0
    m[o == 0] = 0
    k[o == 1] *= -1
    x = d["x"].reshape(N, 8, 16, C, 4)
    x[:, :, 0] = 0
    x[:, :, 0, :, 0] = k.astype(np.float32).astype(BF)
    x[:, :, 0, :, 1] = m.astype(np.float32).astype(BF)
    a = unscored(rng)
    for h in range(0, 128, 16):
        a[h, h, 0] = 1
        a[h, h + 1, 1] = 1
    return {"x": x.reshape(N, 128, 4 * C), "u": alike(a.reshape(128, 512)), "v": d["v"], **weights(rng, layers(rng), [0])}
def setup_inputs_near(rng):
    d = numbers_of(rng)
    x = d["x"].astype(np.float32).reshape(N, 8, 16, C, 4)
    x[:, :, 0] = 0
    x[:, :, 8:] = 0
    a = unscored(rng)
    o = rng.permutation(8) % 4
    for g in range(8):
        h = 16 * g
        for m in range(2):
            s = rng.integers(0, 16, (N, C))
            c = rng.integers(0, 2, (N, C)) * 2.0 - 1.0
            if o[g] < 3: x[:, g, 8 + m] = ((s[:, :, None] >> np.arange(4)) & 1) * np.exp2(np.arange(4) - 23.0)
            if o[g] < 2:
                k = 1.0 if o[g] == 0 else 2.0 ** -30
                x[:, g, 0, :, m] = c
                x[:, g, 11, :, 0] = 2.0 ** -10
                a[h, h + m, m] = k
                a[h + 8 + m, h + m] = k
                a[h + 11, h + m, 0] = k
            elif o[g] == 2:
                for r in range(N): x[r, g, 0, rng.permutation(C)[:2], m] = [1.0, -1.0]
                a[h, h + m, m] = 2.0 ** 30
                a[h + 8 + m, h + m] = 2.0 ** -30
            else:
                x[:, g, 10, :, m] = np.where(s % 2 == 0, 1.125 * 2.0 ** -30 * c, 0.0)
                x[:, g, 12, :, m] = np.where(s % 2 == 0, 0.0, 1.25 * 2.0 ** -30 * c)
                a[h + 10, h + m, m] = 1.125 * 2.0 ** -30
                a[h + 12, h + m, m] = 2.0 ** -30
    return {"x": x.reshape(N, 128, 4 * C).astype(BF), "u": alike(a.reshape(128, 512)), "v": d["v"], **weights(rng, layers(rng), [0, 8, 9, 10, 11, 12, 13, 14, 15])}
def setup_inputs_odd(rng):
    d = numbers_of(rng)
    a = (1.0 + (2 * rng.integers(0, 64, (N, 16, 8, C, 4)) + 1) * 2.0 ** -7) * np.exp2(-rng.integers(8, 15, (N, 16, 8, C, 4)).astype(np.float64))
    a = np.where(np.arange(8)[:, None, None] * 4 + np.arange(4) == rng.integers(0, 32, (N, 16, 1, C, 1)), 1.96875, a)
    a = a * (rng.integers(0, 2, a.shape) * 2.0 - 1.0) * np.exp2(rng.integers(-2, 3, (N, 16, 1, C, 1)).astype(np.float64))
    return {"x": a.astype(np.float32).reshape(N, 128, 4 * C).astype(BF), "u": d["u"], "v": d["v"], **weights(rng, layers(rng), [8, 9, 10, 11, 12, 13, 14, 15])}
def setup_inputs_ends(rng):
    d = numbers_of(rng)
    o = rng.permutation(N) % 4
    x = np.zeros((N, 8, 16, C, 4), np.float32)
    x[:, :, 8:12] = f(rng, N, 8, 4, C, 4).astype(np.float32) * np.float32(1024)
    for r in range(N):
        c = rng.integers(0, 2, C) * 2.0 - 1.0
        w = rng.choice([1.375, 1.5], (8, C))
        a, b = rng.permutation(C)[:2]
        w[:, b] = 1.625
        if o[r] == 0:
            w[:, a] = 1.625
            c[a], c[b] = 1.0, -1.0
        else: w[:, a] = 1.25
        if o[r] == 1: c[:] = -1.0
        if o[r] == 2: c[:] = 1.0
        e = w * c * 2.0 ** 29 if o[r] < 2 else np.ones((8, 1)) * c * 2.0 ** -30
        x[r, :, :8] = e[:, None, :, None]
        k = (rng.integers(0, 2, (128, 512)) * 2.0 - 1.0).astype(np.float32)
        if o[r] == 1: d["v"][r] = (k * np.float32(2.0 ** 30)).astype(BF)
        if o[r] == 2: d["v"][r] = (k * np.float32(2.0 ** -30)).astype(BF)
    u = unscored(rng).reshape(8, 16, 128, 4)
    p = rng.permutation(8)
    for g in range(8):
        k = (2.0 ** 30 if p[g] < 4 else 2.0 ** -29) * (1.0 if p[g] % 2 == 0 else -1.0)
        for m in range(2):
            u[:, :8, 16 * g + m] = 0.75 * k * (1 - 2 * m)
            u[g, :8, 16 * g + m] = k * (1 - 2 * m)
    w = ((rng.integers(0, 2, (N, 128, 4096)) * 2.0 - 1.0) * 2.0 ** -11).astype(np.float32).astype(BF)
    return {"x": x.reshape(N, 128, 4 * C).astype(BF), "u": alike(u.reshape(128, 512)), "v": d["v"], **weights(rng, w, [0, 1, 2, 3, 4, 5, 6, 7])}
def setup_inputs_spread(rng):
    d = numbers_of(rng)
    w = np.array(mx_ref.flush((layers(rng).astype(np.float32) * np.float32(2.0 ** -7)).astype(BF)))
    x = np.array(wide(rng, N, 128, 4 * C, cols=3))
    e = int(rng.integers(N))
    x[e] = ((1.0 + 0.25 * rng.random((128, 4 * C))) * 2.0 ** 24).astype(np.float32).astype(BF)
    w[e ^ 1] = (-0.1875 - 0.0625 * rng.random((128, 4096))).astype(np.float32).astype(BF)
    return {"x": x, "u": d["u"], "v": d["v"], **weights(rng, w)}
def check_inputs(d):
    b = []
    for k in ("x", "u", "v"):
        a = np.abs(d[k].astype(np.float32))
        if not (np.isfinite(a).all() and ((a == 0) | (a >= 2.0 ** -30) & (a <= 2.0 ** 30)).all()): b.append("a value of " + k)
    if (d["u"] != d["u"][:1]).any(): b.append("u isn't the same on all ranks")
    none, least, most = [emit(mx_ref.quantize(np.full((128, 16), k, np.float32).astype(BF)))[1][0, 0] for k in (0.0, 2.0 ** -30, 2.0 ** 30)]
    size = 0.0
    for r in range(N):
        if ((d["wc"][r] == 0x7F) | (d["wc"][r] == 0xFF)).any(): b.append("wc: a code that is no number")
        s = mx_ref.live(d["ws"][r])
        if ((s != none) & ((s < least) | (s > most))).any(): b.append("ws: a scale out of range")
        if (((d["wc"][r].reshape(16, 8, -1, 4) & 0x7F) != 0) & (s == none)[:, None, :, None]).any(): b.append("wc: a code other than zero where the scale is that of zeros")
        size = max(size, float(np.abs(decode(pk(d["wc"][r], d["ws"][r]))).max()))
    if not float(np.abs(d["x"].astype(np.float32)).max()) * (1.0 + 20.0 * size) * (1.0 + 20.0 * size) <= 900000000.0: b.append("the sizes of x and W together")
    return b
def places(s):
    o = np.argsort(-s, axis=1, kind="stable")
    i = np.zeros(s.shape, np.int64)
    np.put_along_axis(i, o, np.broadcast_to(np.arange(C), s.shape), axis=1)
    return o, i
def reference(x, u, v, wc, ws):
    qu = [mx_ref.quantize(u[r]) for r in range(N)]
    lay = [pk(wc[r], ws[r]) for r in range(N)]
    now = [x[r] for r in range(N)]
    total = np.zeros((N, C), np.int64)
    for t in range(R):
        q = [mx_ref.quantize(now[r]) for r in range(N)]
        full = [decode(q[r]).astype(BF) for r in range(N)]
        s = [mx_ref.matmul(qu[r], q[r]) + np.float32(0.0) for r in range(N)]
        first = [places(s[r][::16]) for r in range(N)]
        second = [places(s[r][1::16])[1] for r in range(N)]
        made = [None] * N
        for r in range(N):
            e = r ^ (1 << t)
            total[r] = first[r][1][0]
            took = np.zeros((8, C), np.int64)
            for g in range(8):
                turn = places(total[r][None])[1][0]
                took[g] = first[e][0][g][turn]
                total[r] = total[r] + second[e][g][took[g]]
            z = mx_ref.quantize(gcols(full[e], took))
            p = [mx_ref.matmul(pick(lay[r], np.arange(128 * b, 128 * b + 128)), z) for b in range(8)]
            y = tile([np.maximum(p[b], p[b + 4]) * np.float32(0.03125) for b in range(4)])
            back = gcols(decode(mx_ref.quantize(y)).astype(BF), np.argsort(took, axis=1))
            made[e] = (full[e].astype(np.float32) + back.astype(np.float32)).astype(BF)
        now = made
    y, tot = np.zeros((N, 128, C), np.float32), np.zeros((N, 1, C), np.float32)
    oc, osc = np.zeros((N, 128, 4 * C), np.uint8), np.zeros((N, 16, C), np.uint8)
    for r in range(N):
        q = mx_ref.quantize(now[r])
        y[r] = mx_ref.matmul(mx_ref.quantize(v[r]), q)
        tot[r, 0] = total[r]
        oc[r], osc[r] = emit(q)
    return {"y": y, "tot": tot, "oc": oc, "osc": osc}

@@ -1,0 +1,547 @@
+from concourse.mybir import dt, AluOpType as A, ActivationFunctionType as F
+
+C = 288
+H = 160
+PARTS = ((0, H), (H, C))
+KW = 512
+B16, B96 = 2.0 ** 18, 2.0 ** 21
+BIG, TINY, MAGIC = 1e29, 2.0 ** -119, 1.5 * 2.0 ** 23
+NK = 17
+
+MXC, PL = "float8_e4m3fn_x4", "uint8"
+SCRATCH = {}
+
+
+def _buf(n, cols, d):
+    SCRATCH[n] = ("psum" if n == "ps" else "sbuf", [128, cols], d)
+
+
+_buf("ps", 4096, "float32")
+for _t in range(3):
+    _buf("xt%d" % _t, 4 * C, "bfloat16")
+    _buf("xc%d" % _t, C, MXC)
+    _buf("xs%d" % _t, C, PL)
+for _t in range(2):
+    for _n in ("l", "z", "q", "b"):
+        _buf(_n + "c%d" % _t, C, MXC)
+        _buf(_n + "s%d" % _t, C, PL)
+for _n, _c, _d in (("wk", 1024, MXC), ("wp", 1024, PL), ("ut", 512, "bfloat16"), ("vt", 512, "bfloat16"), ("uq", 128, MXC), ("us", 128, PL),
+                   ("vq", 128, MXC), ("vs", 128, PL), ("up", 640, MXC), ("ups", 640, PL), ("kt", NK * 512, "bfloat16"), ("kc", NK * 128, MXC),
+                   ("ks", NK * 128, PL), ("tm2", 512, "bfloat16"), ("ui", 40, "int32"), ("ul", 40, "uint16"), ("pi", 2, "int32"), ("pj", 4, "int32"),
+                   ("fc", 20, "float32"), ("mk", 4, "float32"), ("bcm", 8, "float32"), ("ij", C, "float32"), ("rowx", C, "float32"),
+                   ("row16", C, "float32"), ("row32", C, "float32"), ("row96", C, "float32"), ("rowog", 128, "float32"), ("hown", C, "float32"),
+                   ("hb", C, "float32"), ("k16", C, "float32"), ("k96", C, "float32"), ("t1", C, "float32"), ("t2", C, "float32"),
+                   ("t3", C, "float32"), ("t4", C, "float32"), ("wo", 4 * C, "bfloat16"), ("qo", C, MXC), ("qos", C, PL), ("om", C, "float32"),
+                   ("wa", 20 * C, "bfloat16"), ("wb", 20 * C, "bfloat16"), ("qa", 5 * C, MXC), ("qas", 5 * C, PL), ("qb", 5 * C, MXC),
+                   ("qbs", 5 * C, PL), ("rm", 4 * C, "float32"), ("tr", 4 * C, "float32"), ("ds", 16 * C, "float32"), ("dd", C, "float32"),
+                   ("de", C, "float32"), ("key0", C, "float32"), ("key1", C, "float32"), ("col", C, "float32"), ("nl", 18, "uint16"),
+                   ("nf", 18, "float32"), ("ne", 18, "float32"), ("no", 18, "float32"), ("nz", 18, "uint16"), ("aw", 18, "uint16"),
+                   ("ow", 18, "uint16"), ("kw", 18, "uint16"), ("bs", C, "float32"), ("cs", C, "float32"), ("of", C, "float32"),
+                   ("nv", C, "float32"), ("kr", C, "float32"), ("cd", 4 * C, "bfloat16"), ("qc", C, MXC), ("qcs", C, PL), ("cw", 8 * C, "float32"),
+                   ("ct", 4 * C, "bfloat16"), ("qt", C, MXC), ("qts", C, PL), ("ff", 4 * C, "bfloat16"), ("fs", 4 * C, "bfloat16"),
+                   ("zt", 4 * C, "bfloat16"), ("y1", 4 * C, "float32"), ("ym", 4 * C, "bfloat16"), ("yt", 4 * C, "bfloat16"),
+                   ("yo", C, "float32"), ("to", C, "float32")):
+    _buf(_n, _c, _d)
+DMAS = ["d%d" % i for i in range(20)]
+SEMAPHORES = ["cv", "cs", "ct", "cg", "sent", "ax0", "ax1", "ay0", "ay1"] + DMAS
+
+
+def rank_program(g, core, T, topo):
+    rank = T.rank_of(core)
+    if rank is None:
+        return
+    Q = {"g": g, "v": g.vector, "s": g.scalar, "t": g.tensor, "y": g.sync}
+    clk = {k: {} for k in Q}
+    cnt = {k: 0 for k in Q}
+    last, readers, ndma, sent = {}, {}, [0], [0]
+
+    def waits(q, toks):
+        for s, v, c, _ in sorted(toks, key=lambda k: -len(k[2])):
+            if clk[q].get(s, 0) < v:
+                Q[q].wait_ge(T.sem[s], max(k[1] for k in toks if k[0] == s))
+                for k in toks:
+                    if k[0] == s:
+                        for a, b in k[2].items():
+                            if clk[q].get(a, 0) < b: clk[q][a] = b
+
+    def op(q, fn, rd=(), wr=(), dma=False):
+        rd = (rd,) if isinstance(rd, str) else rd
+        wr = (wr,) if isinstance(wr, str) else wr
+        me = "dma" if dma else q
+        toks = []
+        for k in rd:
+            if k in last: toks.append(last[k])
+            if k[:2] == "ps": toks += [w for w in readers.get(k, {}).values() if w[3] != me]
+        for k in wr:
+            if k in last and last[k][3] != q: toks.append(last[k])
+            toks += list(readers.get(k, {}).values())
+        waits(q, toks)
+        ins = fn()
+        if dma:
+            s, v = DMAS[ndma[0]], 16
+            ndma[0] += 1
+        else:
+            cnt[q] += 1
+            s, v = "c" + q, cnt[q]
+        ins.then_inc(T.sem[s], 16 if dma else 1)
+        c = dict(clk[q])
+        c[s] = v
+        tok = (s, v, c, me)
+        for k in rd:
+            readers.setdefault(k, {})[s] = tok
+        for k in wr:
+            last[k] = tok
+            readers[k] = {}
+
+    V, S = g.vector, g.scalar
+
+    def ts(out, i, s1, s2, o0, o1, rd, wr):
+        if o1 is None: op("v", lambda: V.tensor_scalar(out, i, s1, None, o0), rd, wr)
+        else: op("v", lambda: V.tensor_scalar(out, i, s1, s2, o0, o1), rd, wr)
+
+    def tt(out, a, b, o, rd, wr):
+        op("v", lambda: V.tensor_tensor(out, a, b, o), rd, wr)
+
+    def cp(out, i, rd, wr):
+        op("v", lambda: V.tensor_copy(out, i), rd, wr)
+
+    def ms(ap, c, wr):
+        op("v", lambda: V.memset(ap, c), (), wr)
+
+    def act(out, i, f, rd, wr, bias=0.0, scale=1.0):
+        op("s", lambda: S.activation(out, i, f, bias=bias, scale=scale), rd, wr)
+
+    def qz(c, s, i, rd, wr):
+        op("v", lambda: V.quantize_mx(c, s, i), rd, wr)
+
+    def iota(out, pat, base, cm, wr, flag=True):
+        op("g", lambda: g.iota(out, pat, base, cm, allow_small_or_imprecise_dtypes=flag), (), wr)
+
+    def ld(q, out, i, wr, rd=()):
+        op(q, lambda: Q[q].dma_start(out, i), rd, wr, dma=True)
+
+    def ps(b, n=C):
+        return T.ps[:, 512 * b:512 * b + n]
+
+    def mm(b, n, lc, ls, rc, rs, rd, start=True, stop=True):
+        op("t", lambda: g.tensor.matmul_mx(ps(b, n), lc, ls, rc, rs, start, stop), rd, "ps%d" % b)
+
+    def kk(i):
+        return T.kc[:, 128 * i:128 * i + 128], T.ks[:, 128 * i:128 * i + 128]
+
+    def kz(k):
+        qz(*kk(k), T.kt[:, k * KW:(k + 1) * KW], "kt%d" % k, "kc%d" % k)
+
+    def scan(out, i, k, rd, wr):
+        op("v", lambda: V.tensor_tensor_scan(out, i, k, -4.0 * B96, A.max, A.add), rd, wr)
+
+    def send(src, dst, sem, peer):
+        waits("g", [last[k] for k in src])
+        rid, pid = topo.addr(peer, core)
+        m = topo.mask(core, peer)
+        g.remote_dma(T[dst[0]][:].bitcast(dt.uint8), T[src[0]][:].bitcast(dt.uint8), T.sem[sem], T.sem.sent, pid, rid, m)
+        g.remote_dma(T[dst[1]][:], T[src[1]][:], T.sem[sem], T.sem.sent, pid, rid, m)
+        n = 2 * len(topo.engines(core, peer))
+        sent[0] += n
+        for k in dst:
+            last[k] = (sem, n, {sem: n}, "r")
+
+    peers = [T.cores[rank ^ (1 << t)] for t in range(2)]
+
+    ld("y", T.xt0[:], T.x[:], "xt0")
+    ld("s", T.ut[:], T.u[:], "ut")
+    ld("y", T.wk[:].bitcast(dt.uint8), T.wc[:], "wk")
+    ld("y", T.wp[:], T.ws[:], "wp")
+    ld("y", T.vt[:], T.v[:], "vt")
+
+    iota(T.pi[:, 0:1], [[1, 1]], 0, 1, "pi", False)
+    iota(T.ui[:, 0:16], [[16, 2], [32, 4], [0, 2]], 0, 0, "ui", False)
+    iota(T.ui[:, 16:32], [[16, 2], [32, 4], [0, 2]], 1, 0, "ui", False)
+    iota(T.rowx[:, 0:256], [[0, 2], [1, 128]], 0, 0, "rowx")
+    iota(T.rowx[:, 256:C], [[1, 32]], 96, 0, "rowx")
+    iota(T.row16[:], [[0, 18], [1, 16]], 0, 0, "row16")
+    iota(T.rowog[:], [[1, 8], [0, 16]], 0, 0, "rowog")
+    iota(T.ij[:], [[1, C]], 0, 0, "ij")
+
+    def col(i):
+        return T.fc[:, i:i + 1]
+
+    def picker(row, rn, c0, c1, step):
+        for t, n, c in ((T.t1, "t1", c0), (T.t2, "t2", c1)):
+            act(t[:], row, F.Abs, (rn, "f%d" % c), n, bias=col(c))
+            act(t[:], t[:], F.Relu, n, n, bias=col(14 if step == B16 else 15), scale=-step)
+
+    for i, x in ((13, TINY), (16, -TINY), (14, B16), (15, B96)):
+        ms(col(i), x, "f%d" % i)
+    ms(T.ui[:, 32:40], 0, "uz")
+    cp(col(0), T.pi[:, 0:1], "pi", "f0")
+    for i, (o, k) in enumerate(((A.bitwise_and, 15), (A.bitwise_and, 31), (A.arith_shift_right, 4), (A.arith_shift_right, 5))):
+        ts(T.pj[:, i:i + 1], T.pi[:, 0:1], k, None, o, None, "pi", "pj")
+    cp(T.fc[:, 1:5], T.pj[:], "pj", "f1")
+    for i, j, a, b in ((10, 0, -BIG, -0.5 * BIG), (5, 1, -1.0, 0.0), (6, 1, -1.0, 1.0), (7, 2, BIG, -0.5 * BIG), (8, 0, -1.0, 0.0),
+                       (9, 0, -1.0, 1.0), (11, 4, 2.0, 0.0), (12, 4, 2.0, 1.0)):
+        ts(col(i), col(j), a, b, A.mult, A.add, ("f0", "f1"), "f%d" % i)
+    act(T.hown[:], T.rowx[:], F.Identity, ("rowx", "f10"), "hown", bias=col(10), scale=BIG)
+    picker(T.row16[:], "row16", 5, 6, B16)
+    for w, (lo, hi, val) in ((0, (0, 128, 512.0)), (1, (0, 128, 512.0)), (3, (0, 128, -512.0)), (2, (0, 96, 0.0)), (2, (96, 128, 512.0))):
+        ms(T.kt[lo:hi, 7 * KW + w:8 * KW:4], val, "kt7")
+    cp(T.ul[:], T.ui[:], ("ui", "uz"), "ul")
+    qz(T.uq[:], T.us[:], T.ut[:], "ut", ("uq", "us"))
+
+    def upick(i):
+        a, b = 128 * i, 128 * i + 128
+        off = T.ul[:, 8 * i:8 * i + 8]
+        op("v", lambda: V.tensor_copy(T.up[:, a:b].bitcast(dt.uint32), T.uq[:, 0:128].bitcast(dt.uint32).indirect(off)), ("uq", "ul"), "up%d" % i)
+        op("s", lambda: S.activation(T.ups[:, a:b], T.us[:, 0:128].indirect(off), F.Copy), ("us", "ul"), "ups%d" % i)
+
+    upick(4)
+    qz(T.xc0[:], T.xs0[:], T.xt0[:], "xt0", ("xc0", "xs0"))
+    send(("xc0", "xs0"), ("lc0", "ls0"), "ax0", peers[0])
+    iota(T.row32[:], [[0, 9], [1, 32]], 0, 0, "row32")
+    iota(T.row96[:], [[0, 3], [1, 96]], 0, 0, "row96")
+    for t in range(4):
+        iota(T.tm2[:, t:512:4], [[0, 128]], 8192 if t < 2 else 0, 0, "tm2")
+    for t in range(2, 4):
+        iota(T.cd[:, t:4 * C:4], [[0, C]], 0, 0, "cdz")
+    iota(T.ct[:, 3:4 * C:4], [[0, C]], 0, 0, "ctz")
+    for k in range(4):
+        iota(T.kt[:, k * KW:(k + 1) * KW], [[0, KW]], 0, 0, "kt%d" % k)
+    kz(7)
+    tt(T.k16[:], T.t1[:], T.t2[:], A.subtract, ("t1", "t2"), "k16")
+    ts(T.k16[:, 15:C:16], T.k16[:, 15:C:16], -2.0 * B16, None, A.add, None, "k16", "k16")
+    ts(T.t3[:, 0:128], T.rowog[:], col(11), None, A.is_equal, None, ("rowog", "f11"), "t3")
+    ts(T.t4[:, 0:128], T.rowog[:], col(12), None, A.is_equal, None, ("rowog", "f12"), "t4")
+    for i in range(4):
+        upick(i)
+    for k, w in ((4, (1.0, 1.0)), (5, (0.5, 0.5)), (6, (1.0, -1.0))):
+        for t in range(4):
+            src, n = (T.t3, "t3") if t < 2 else (T.t4, "t4")
+            act(T.kt[:, k * KW + t:(k + 1) * KW:4], src[:, 0:128], F.Copy, n, "kt%d" % k, scale=w[t % 2])
+    act(T.hb[:], T.row32[:], F.Identity, ("row32", "f7"), "hb", bias=col(7), scale=-BIG)
+
+    def spread(ks):
+        for k in ks:
+            act(T.kt[:, (9 + k) * KW:(10 + k) * KW], T.tm2[:], F.Copy, ("tm2", "bcm"), "kt%d" % (9 + k), scale=T.bcm[:, k:k + 1])
+
+    def late_constants():
+        for m in range(2):
+            ts(T.mk[:, m:m + 1], col(2), 15.5, None, (A.is_lt, A.is_gt)[m], None, "f1", "mk")
+            ts(T.mk[:, m + 2:m + 3], col(2), 15.5, B16 + 48, (A.is_lt, A.is_gt)[m], A.mult, "f1", "mk")
+        ts(T.bcm[:], T.ij[:, 0:8], 16.0, col(0), A.mult, A.is_equal, ("ij", "f0"), "bcm")
+        for t, w in enumerate((1.0, 1.0, 0.5, 0.0)):
+            ms(T.kt[0:96, 8 * KW + t:9 * KW:4], w, "kt8")
+        ms(T.kt[96:128, 8 * KW:9 * KW], 0.0, "kt8")
+        picker(T.row96[:], "row96", 8, 9, B96)
+        spread((0, 1))
+        for k in (4, 5, 6):
+            kz(k)
+
+    def last_constants():
+        for i in (9, 10, 8):
+            kz(i)
+        tt(T.k96[:], T.t1[:], T.t2[:], A.subtract, ("t1", "t2"), "k96")
+        ts(T.k96[:, 95:192:96], T.k96[:, 95:192:96], -2.0 * B96, None, A.add, None, "k96", "k96")
+        ts(T.k96[:, 287:C], T.k96[:, 287:C], -B96 - 0.5, None, A.add, None, "k96", "k96")
+
+    wo, ct, zt = T.wo, T.ct, T.zt
+    D01 = ("dd0", "dd1")
+    for t in range(2):
+        peer = peers[t]
+        dv = T.dd[:, 15:C:16]
+        xc, xs = T["xc%d" % t], T["xs%d" % t]
+        xn = ("xc%d" % t, "xs%d" % t)
+        lc, ls = T["lc%d" % t], T["ls%d" % t]
+        ln = ("lc%d" % t, "ls%d" % t)
+        m0 = (0, 128, 160)
+        mm(3, C, T.up[:, 512:640], T.ups[:, 512:640], xc[:], xs[:], xn + ("up4", "ups4"))
+        for q in range(3):
+            mm(q, 128, xc[:, m0[q]:m0[q] + 128], xs[:, m0[q]:m0[q] + 128], T.uq[:], T.us[:], xn + ("uq", "us"))
+        tt(T.om[:], ps(3), T.hown[:], A.max, ("ps3", "hown"), "om")
+        for q in range(3):
+            sc = T.ps[:, 512 * q:512 * q + 1]
+            rq = ("ps3", "ps%d" % q)
+            e0, e1 = 128 * q, min(128 * q + 128, C)
+            if e0: ts(wo[:, q:4 * e0:4], ps(3, e0), sc, None, A.is_lt, None, rq, "wo")
+            ts(wo[:, 4 * e0 + q:4 * C:4], T.ps[:, 1536 + e0:1536 + C], sc, None, A.is_le, None, rq, "wo")
+            ts(wo[:, 4 * e0 + 3:4 * e1:4], T.om[:, e0:e1], sc, None, A.is_equal, None, ("om", rq[1]), "wo")
+        qz(T.qo[:], T.qos[:], wo[:], "wo", "qo")
+        mm(4, C, *kk(7), T.qo[:], T.qos[:], ("qo", "kc7"))
+        if t == 0:
+            late_constants()
+        scan(T.dd[:], ps(4), T.k16[:], ("ps4", "k16"), D01)
+        tt(T.key0[:], ps(4), T.ij[:], A.subtract, ("ps4", "ij"), ("key0.0", "key0.1"))
+        ts(T.nl[:], dv, -1.0 / 512, 287.0 - B16 / 512, A.mult, A.add, D01, ("nl0", "nl1"))
+        ts(T.nf[:], dv, -1.0 / 512, 287.0 - B16 / 512, A.mult, A.add, D01, "nf")
+        ts(T.ne[0:32, :], T.nf[0:32, :], T.mk[0:32, 0:1], None, A.mult, None, ("nf", "mk"), "ne")
+        banks = ((5, 7), (6, 0), (1, 3), (2, 4))
+        for k in range(4):
+            for b in banks[k]:
+                mm(b, C, T.up[:, 128 * k:128 * k + 128], T.ups[:, 128 * k:128 * k + 128], lc[:], ls[:], ln + ("up%d" % k, "ups%d" % k))
+
+        def side(ty):
+            return (T.wa, "qa", 5) if ty == 0 else (T.wb, "qb", 1)
+
+        def pl(ty, w, p):
+            return "w%d.%d.%d" % (ty, w, p)
+
+        def rows(ty):
+            wt, d0 = side(ty)[0], 8 * C * ty
+            for par in range(2):
+                k = 2 * ty + par
+                o = C * k
+                tt(T.rm[:, o:o + C], ps(banks[k][0]), T.hb[:], A.max, ("ps%d" % banks[k][0], "hb"), "rm%d" % k)
+            for par in range(2):
+                k = 2 * ty + par
+                o = C * k
+                op("v", lambda: V.transpose(T.tr[:, o:o + C], T.rm[:, o:o + C]), "rm%d" % k, "tr%d" % k)
+            for w in range(2):
+                for par in range(2):
+                    k = 2 * ty + par
+                    bw = banks[k][1]
+                    for i in range(2):
+                        b, z = (0, 1, 7, 8)[2 * w + i], 4 * C * w + 2 * par + i
+                        act(T.ds[:, d0 + z:d0 + 4 * C * (w + 1):4], ps(bw), F.Identity, ("ps%d" % bw, "tr%d" % k), "ds%d.%d.%d" % (ty, w, 2 * par + i),
+                            bias=T.tr[:, C * k + 32 * b:C * k + 32 * b + 1], scale=-1.0)
+            for w, st, lo, hi, s in ((0, 1, 32, C, 1), (0, 2, 0, 32, 1), (0, -2, 0, 32, -1),
+                                     (1, 1, 0, 224, -1), (1, 2, 224, 256, 1), (1, -2, 224, 256, -1), (1, 1, 256, C, 1)):
+                f = 4 * C * w + (st < 0)
+                act(wt[:, 12 * C + f + 4 * lo:12 * C + 4 * C * w + 4 * hi:abs(st)], T.ds[:, d0 + f + 4 * lo:d0 + 4 * C * w + 4 * hi:abs(st)], F.Sign,
+                    ["ds%d.%d.%d" % (ty, w, p) for p in range(4)] + ["f13", "f16"], [pl(ty, 3 + w, p) for p in range(4)], bias=col(13 if s > 0 else 16))
+
+        def word(ty, w):
+            wt, qn, pb = side(ty)
+            qc, qs = T[qn], T[qn + "s"]
+            c = (4, 4, 6, 5, 5)[w]
+            qz(qc[:, C * w:C * w + C], qs[:, C * w:C * w + C], wt[:, 4 * C * w:4 * C * w + 4 * C], [pl(ty, w, p) for p in range(4)], qn + "%d" % w)
+            mm(pb, C, *kk(c), qc[:, C * w:C * w + C], qs[:, C * w:C * w + C], (qn + "%d" % w, "kc%d" % c), w == 0, w == 4)
+
+        due = []
+
+        def blocks(ty, par):
+            wt = side(ty)[0]
+            k = 2 * ty + par
+            bv = banks[k][0]
+            rd, o = ("ps%d" % bv, "tr%d" % k), C * k
+            tt(wt[:, 8 * C + 2 * par + 1:12 * C:4], ps(bv), T.tr[:, o:o + C], A.is_equal, rd, pl(ty, 2, 2 * par + 1))
+            for b in range(2, 7):
+                w, p = (b - 2) // 2, 2 * par + b % 2
+                sc = T.tr[:, o + 32 * b:o + 32 * b + 1]
+                z = 4 * C * w + p
+                ts(wt[:, z:z + 128 * b - 3:4], ps(bv, 32 * b), sc, None, A.is_lt, None, rd, pl(ty, w, p))
+                ts(wt[:, z + 128 * b:4 * C * (w + 1):4], T.ps[:, 512 * bv + 32 * b:512 * bv + C], sc, None, A.is_le, None, rd, pl(ty, w, p))
+                while due:
+                    word(*due.pop())
+                if par and (b % 2 or b == 6): due.append((ty, w))
+
+        rows(0)
+        blocks(0, 0)
+        rows(1)
+        blocks(0, 1)
+        blocks(1, 0)
+        word(0, 3)
+        word(0, 4)
+        blocks(1, 1)
+        scan(T.dd[:], ps(5), T.k16[:], ("ps5", "k16"), D01)
+        word(*due.pop())
+        word(1, 3)
+        ts(T.aw[:], dv, B16 + 64, None, A.add, None, D01, "aw")
+        word(1, 4)
+        op("v", lambda: V.tensor_copy(T.of[:].indirect(T.aw[:]), T.ij[:]), ("ij", "aw"), "of")
+        if t == 0:
+            spread(range(2, 8))
+            for k in range(4):
+                ts(T.kt[:, k * KW + k:(k + 1) * KW:4], T.ij[:, 0:128], col(0), None, A.is_equal, None, ("ij", "f0"), "kt%d" % k)
+            last_constants()
+        ts(T.bs[:], ps(1), 0.0625, -5.0, A.mult, A.add, "ps1", "bs")
+        op("v", lambda: V.tensor_copy(T.cs[:].indirect(T.aw[:]), T.bs[:]), ("bs", "aw"), "cs")
+        for h, (a, b) in enumerate(PARTS):
+            ts(T.cd[:, 4 * a:4 * b:4], T.cs[:, a:b], MAGIC, MAGIC, A.add, A.subtract, "cs", "cd0%d" % h)
+        for h, (a, b) in enumerate(PARTS):
+            tt(T.cd[:, 4 * a + 1:4 * b:4], T.cs[:, a:b], T.cd[:, 4 * a:4 * b:4], A.subtract, ("cs", "cd0%d" % h), "cd1%d" % h)
+        for h, (a, b) in enumerate(PARTS):
+            qz(T.qc[:, a:b], T.qcs[:, a:b], T.cd[:, 4 * a:4 * b], ("cd0%d" % h, "cd1%d" % h, "cdz"), "qc")
+        bb = (0, 2, 3, 4, 6, 7, 0, 2)
+
+        def table(k):
+            mm(bb[k], C, *kk(9 + k), T.qc[:], T.qcs[:], ("qc", "kc%d" % (9 + k)))
+
+        def keep(k):
+            if k: act(T.cw[:, C * k:C * k + C], ps(bb[k]), F.Copy, "ps%d" % bb[k], "cw%d" % k)
+            else: cp(T.cw[:, 0:C], ps(bb[0]), "ps%d" % bb[0], "cw0")
+
+        for k in range(2 if t == 0 else 6):
+            table(k)
+        scan(T.kr[:], T.of[:], T.k16[:], ("of", "k16"), "kr")
+        ts(T.ow[:], T.kr[:, 15:C:16], B16, None, A.add, None, "kr", "ow")
+        keep(0)
+        keep(1)
+        keys = ((T.key0, "key0"), (T.key1, "key1"))
+
+        def grow(k, h):
+            (x, xk), (y, yk) = keys[k % 2], keys[1 - k % 2]
+            a, b = PARTS[h]
+            op("v", lambda: V.tensor_tensor(y[:, a:b], T.cw[:, C * k:C * k + C].indirect(T.nl[:, a // 16:b // 16]), x[:, a:b], A.add),
+               ("cw%d" % k, "nl%d" % h, "%s.%d" % (xk, h)), "%s.%d" % (yk, h))
+
+        def turns(h):
+            a, b = PARTS[h]
+            ts(T.nl[:, a // 16:b // 16], dv[:, a // 16:b // 16], B16 + 48, None, A.add, None, "%s%d" % (dn, h), "nl%d" % h)
+
+        fb = (3, 4, 6, 7)
+        dn = "dd"
+        zc, zs = T["zc%d" % t], T["zs%d" % t]
+
+        def z_list(h, i):
+            s = slice(PARTS[h][0] // 16, PARTS[h][1] // 16)
+            if i == 0: ts(T.no[96:128, s], dv[96:128, s], B16 + 48, T.mk[96:128, 1:2], A.add, A.mult, (dn + "%d" % h, "mk"), "no")
+            if i == 1: tt(T.nf[:, s], T.ne[:, s], T.no[:, s], A.add, ("ne", "no"), "nf%d" % h)
+            if i == 2: cp(T.nz[:, s], T.nf[:, s], "nf%d" % h, "nz%d" % h)
+
+        def z_part(b, h, v):
+            a, e = PARTS[h]
+            o, i = zt[:, 4 * a + b:4 * e:4], T.fs[:, C * b:C * b + C].indirect(T.nz[:, a // 16:e // 16])
+            rd, wr = ("fs%d" % b, "nz%d" % h), "zt%d.%d" % (b, h)
+            if v: cp(o, i, rd, wr)
+            else: op("s", lambda: S.activation(o, i, F.Copy), rd, wr)
+
+        def z_codes(h):
+            a, b = PARTS[h]
+            qz(zc[:, a:b], zs[:, a:b], zt[:, 4 * a:4 * b], ["zt%d.%d" % (i, h) for i in range(4)], "zc")
+
+        for k in range(1, 8):
+            kr, kn = keys[k % 2]
+            k0, k1 = kn + ".0", kn + ".1"
+
+            def pick(b, rd):
+                scan(T.col[:, 96 * b:96 * b + 96], kr[:, 96 * b:96 * b + 96], T.k96[:, 96 * b:96 * b + 96], rd + ("k96",), "col%d" % b)
+
+            def less(b, h):
+                a, e = PARTS[h]
+                ts(ct[:, 4 * a + b:4 * e:4], kr[:, a:e], -B96, T.col[:, 96 * b + 95:96 * b + 96], A.add, A.is_lt, ((k0, k1)[h], "col%d" % b), "ct%d.%d" % (b, h))
+
+            grow(k - 1, 0)
+            if k > 1: turns(1)
+            pick(0, (k0,))
+            grow(k - 1, 1)
+            less(0, 0)
+            pick(2, (k1,))
+            for h, (a, b) in enumerate(PARTS):
+                act(ct[:, 4 * a + 2:4 * b:4], kr[:, a:b], F.Sign, ((k0, k1)[h], "col2"), "ct2.%d" % h, bias=T.col[:, 287:288], scale=-1.0)
+            pick(1, (k0, k1))
+            less(0, 1)
+            less(1, 0)
+            less(1, 1)
+            for h, (a, b) in enumerate(PARTS):
+                qz(T.qt[:, a:b], T.qts[:, a:b], ct[:, 4 * a:4 * b], ["ct%d.%d" % (i, h) for i in range(3)] + ["ctz"], "qt%d" % h)
+                mm((5, 1)[h], b - a, *kk(8), T.qt[:, a:b], T.qts[:, a:b], ("qt%d" % h, "kc8"))
+            dx, dn = ((T.dd, "dd"), (T.de, "de"))[k % 2]
+            dv = dx[:, 15:C:16]
+            if t == 0:
+                for i in {1: (11, 12), 2: (13, 14, 0), 3: (15, 16, 1), 4: (2, 3)}.get(k, ()):
+                    kz(i)
+            scan(dx[:, 0:H], ps(5, H), T.k16[:, 0:H], ("ps5", "k16"), dn + "0")
+            if k <= 3:
+                if t == 0:
+                    table(2 * k)
+                    table(2 * k + 1)
+                elif k == 1:
+                    table(6)
+                    table(7)
+                keep(2 * k)
+                keep(2 * k + 1)
+            if k in (4, 5):
+                for b in (2 * k - 8, 2 * k - 7):
+                    mm(fb[b], C, *kk(b), lc[:], ls[:], ln + ("kc%d" % b,))
+                    act(T.ff[:, C * b:C * b + C], ps(fb[b]), F.Copy, "ps%d" % fb[b], "ff%d" % b)
+            if k in (6, 7):
+                for b in (2 * k - 12, 2 * k - 11):
+                    op("s", lambda: S.activation(T.fs[:, C * b:C * b + C], T.ff[:, C * b:C * b + C].indirect(T.ow[:]), F.Copy), ("ff%d" % b, "ow"), "fs%d" % b)
+            if k < 7: turns(0)
+            else:
+                for i in range(3):
+                    z_list(0, i)
+            scan(dx[:, H:C], ps(1, C - H), T.k16[:, H:C], ("ps1", "k16"), dn + "1")
+            p0, m = 32 * (k // 2), k % 2
+            p1 = p0 + 32
+            nb, nn = ((T.ne, "ne"), (T.no, "no"))[m]
+            if k < 7: act(nb[p0:p1, :], dv[p0:p1, :], F.Identity, (dn + "0", dn + "1", "mk"), nn, bias=T.mk[p0:p1, 2 + m:3 + m], scale=T.mk[p0:p1, m:m + 1])
+        z_part(0, 0, True)
+        z_part(3, 0, False)
+        z_list(1, 0)
+        z_part(1, 0, True)
+        z_list(1, 1)
+        z_part(2, 0, True)
+        z_list(1, 2)
+        z_codes(0)
+        z_part(0, 1, True)
+        z_part(2, 1, False)
+        z_part(3, 1, False)
+        z_part(1, 1, True)
+        z_codes(1)
+        if t:
+            turns(0)
+            turns(1)
+        dv = T.dd[:, 15:C:16]
+        for b in range(4):
+            for h in range(2):
+                w = 128 * (b + 4 * h)
+                mm(2 * b + h, C, T.wk[:, w:w + 128], T.wp[:, w:w + 128], zc[:], zs[:], ("zc", "wk", "wp"))
+        op("v", lambda: V.tensor_copy(T.nv[:].indirect(T.nz[:]), T.ij[:]), ("ij", "nz0", "nz1"), "nv")
+        cp(T.kr[:], T.nv[:].indirect(T.aw[:]), ("nv", "aw"), "kr")
+        if t:
+            grow(7, 0)
+            grow(7, 1)
+        scan(T.dd[:], T.kr[:], T.k16[:], ("kr", "k16"), D01)
+        ts(T.kw[:], dv, B16, None, A.add, None, D01, "kw")
+
+        def largest(b):
+            act(T.y1[:, C * b:C * b + C], ps(2 * b), F.Copy, "ps%d" % (2 * b), "y1%d" % b)
+            tt(T.ym[:, C * b:C * b + C], ps(2 * b + 1), T.y1[:, C * b:C * b + C], A.max, ("ps%d" % (2 * b + 1), "y1%d" % b), "ym%d" % b)
+
+        def put(b, v):
+            o, i = T.yt[:, b:4 * C:4], T.ym[:, C * b:C * b + C].indirect(T.kw[:])
+            rd, wr = ("ym%d" % b, "kw"), "yt%d" % b
+            if v: op("v", lambda: V.tensor_scalar(o, i, 0.03125, None, A.mult), rd, wr)
+            else: op("s", lambda: S.activation(o, i, F.Copy, scale=0.03125), rd, wr)
+
+        for b in range(3):
+            largest(b)
+        put(0, True)
+        largest(3)
+        put(1, False)
+        put(2, False)
+        put(3, True)
+        qn = ("qc%d" % t, "qs%d" % t)
+        qz(T[qn[0]][:], T[qn[1]][:], T.yt[:], ["yt%d" % b for b in range(4)], qn)
+        send(qn, ("bc%d" % t, "bs%d" % t), "ay%d" % t, peer)
+        for b in range(4):
+            mm(b, C, *kk(b), xc[:], xs[:], xn + ("kc%d" % b,), True, False)
+        if t == 1:
+            tt(T.to[0:1, :], T.key0[0:1, :], T.ij[0:1, :], A.add, ("key0.0", "key0.1", "ij"), "to")
+            ts(T.to[0:1, :], T.to[0:1, :], 1.0 / 512, 1152.0, A.mult, A.add, "to", "to")
+            ld("y", T.tot[:], T.to[0:1, :], "tot", "to")
+            qz(T.vq[:], T.vs[:], T.vt[:], "vt", "vq")
+        xt = T["xt%d" % (t + 1)]
+        for b in range(4):
+            mm(b, C, *kk(b), T["bc%d" % t][:], T["bs%d" % t][:], ("bc%d" % t, "bs%d" % t, "kc%d" % b), False, True)
+        for b in range(4):
+            if b % 2 == 0: act(xt[:, b:4 * C:4], ps(b), F.Copy, "ps%d" % b, "x%d" % b)
+            else: cp(xt[:, b:4 * C:4], ps(b), "ps%d" % b, "x%d" % b)
+        nx = ("xc%d" % (t + 1), "xs%d" % (t + 1))
+        qz(T[nx[0]][:], T[nx[1]][:], xt[:], ["x%d" % b for b in range(4)], nx)
+        if t == 0:
+            send(nx, ("lc1", "ls1"), "ax1", peers[1])
+    ld("y", T.oc[:], T.xc2[:].bitcast(dt.uint8), "oc", "xc2")
+    for k in range(4):
+        ld("s" if k % 2 else "y", T.osc[4 * k:4 * k + 4, :], T.xs2[32 * k:32 * k + 4, :], "osc%d" % k, "xs2")
+    mm(4, C, T.vq[:], T.vs[:], T.xc2[:], T.xs2[:], ("xc2", "xs2", "vq"))
+    act(T.yo[:], ps(4), F.Copy, "ps4", "yo")
+    ld("s", T.y[:], T.yo[:], "yout", "yo")
+    for q in "vstg":
+        g.wait_ge(T.sem["c" + q], cnt[q])
+    for i in range(ndma[0]):
+        g.wait_ge(T.sem[DMAS[i]], 16)
+    g.wait_ge(T.sem.sent, sent[0])
+    for t in range(2):
+        for s in ("ax", "ay"):
+            g.wait_ge(T.sem[s + "%d" % t], 2 * len(topo.engines(core, peers[t])))

@@ -5,8 +5,12 @@ H = 160
 PARTS = ((0, H), (H, C))
 KW = 512
 B16, B96 = 2.0 ** 18, 2.0 ** 21
-BIG, TINY, MAGIC = 1e29, 2.0 ** -119, 1.5 * 2.0 ** 23
-NK = 17
+BIG, TINY = 1e29, 2.0 ** -119
+NK = 16
+TIE = 9
+WORDS = (((2, 3), (4, 5), (6, TIE), (0, 1), (7, 8)),) * 2
+SCAL = ((6, 0, 1, 7, 8),) * 2
+PLUS = 16.0 * 5 - 32.0
 
 MXC, PL = "float8_e4m3fn_x4", "uint8"
 SCRATCH = {}
@@ -26,17 +30,18 @@ for _t in range(2):
         _buf(_n + "c%d" % _t, C, MXC)
         _buf(_n + "s%d" % _t, C, PL)
 for _n, _c, _d in (("wk", 1024, MXC), ("wp", 1024, PL), ("ut", 512, "bfloat16"), ("vt", 512, "bfloat16"), ("uq", 128, MXC), ("us", 128, PL),
-                   ("vq", 128, MXC), ("vs", 128, PL), ("up", 640, MXC), ("ups", 640, PL), ("kt", NK * 512, "bfloat16"), ("kc", NK * 128, MXC),
-                   ("ks", NK * 128, PL), ("tm2", 512, "bfloat16"), ("ui", 40, "int32"), ("ul", 40, "uint16"), ("pi", 2, "int32"), ("pj", 4, "int32"),
-                   ("fc", 20, "float32"), ("mk", 4, "float32"), ("bcm", 8, "float32"), ("ij", C, "float32"), ("rowx", C, "float32"),
-                   ("row16", C, "float32"), ("row32", C, "float32"), ("row96", C, "float32"), ("rowog", 128, "float32"), ("hown", C, "float32"),
-                   ("hb", C, "float32"), ("k16", C, "float32"), ("k96", C, "float32"), ("t1", C, "float32"), ("t2", C, "float32"),
-                   ("t3", C, "float32"), ("t4", C, "float32"), ("wo", 4 * C, "bfloat16"), ("qo", C, MXC), ("qos", C, PL), ("om", C, "float32"),
+                   ("vq", 128, MXC), ("vs", 128, PL), ("up", 640, MXC), ("ups", 640, PL), ("kt", 4 * KW, "bfloat16"), ("sp", 2 * KW + 8, "bfloat16"),
+                   ("un", KW + 4, "bfloat16"), ("kc", NK * 128, MXC), ("ks", NK * 128, PL), ("tm2", KW + 4, "bfloat16"), ("one", KW + 4, "bfloat16"),
+                   ("ui", 40, "int32"), ("ul", 40, "uint16"), ("pi", 2, "int32"), ("pj", 4, "int32"),
+                   ("fc", 20, "float32"), ("mk", 4, "float32"), ("ij", C, "float32"), ("row32", C, "float32"),
+                   ("rowog", 128, "float32"), ("hown", C, "float32"), ("hb", C, "float32"), ("k16", C, "float32"), ("k96", 96, "float32"),
+                   ("t1", 32, "float32"), ("t2", 128, "float32"), ("t3", 128, "float32"), ("t4", 128, "float32"),
+                   ("wo", 4 * C, "bfloat16"), ("qo", C, MXC), ("qos", C, PL), ("om", C, "float32"),
                    ("wa", 20 * C, "bfloat16"), ("wb", 20 * C, "bfloat16"), ("qa", 5 * C, MXC), ("qas", 5 * C, PL), ("qb", 5 * C, MXC),
-                   ("qbs", 5 * C, PL), ("rm", 4 * C, "float32"), ("tr", 4 * C, "float32"), ("ds", 16 * C, "float32"), ("dd", C, "float32"),
+                   ("qbs", 5 * C, PL), ("rm", 4 * C, "float32"), ("tr", 4 * C, "float32"), ("ds", 40 * C, "float32"), ("dd", C, "float32"),
                    ("de", C, "float32"), ("key0", C, "float32"), ("key1", C, "float32"), ("col", C, "float32"), ("nl", 18, "uint16"),
-                   ("nf", 18, "float32"), ("ne", 18, "float32"), ("no", 18, "float32"), ("nz", 18, "uint16"), ("aw", 18, "uint16"),
-                   ("ow", 18, "uint16"), ("kw", 18, "uint16"), ("bs", C, "float32"), ("cs", C, "float32"), ("of", C, "float32"),
+                   ("nf", 18, "float32"), ("ne", 18, "float32"), ("no", 18, "float32"), ("nr", 18, "float32"), ("nz", 18, "uint16"),
+                   ("aw", 18, "uint16"), ("ow", 18, "uint16"), ("kw", 18, "uint16"), ("bs", C, "float32"), ("of", C, "float32"),
                    ("nv", C, "float32"), ("kr", C, "float32"), ("cd", 4 * C, "bfloat16"), ("qc", C, MXC), ("qcs", C, PL), ("cw", 8 * C, "float32"),
                    ("ct", 4 * C, "bfloat16"), ("qt", C, MXC), ("qts", C, PL), ("ff", 4 * C, "bfloat16"), ("fs", 4 * C, "bfloat16"),
                    ("zt", 4 * C, "bfloat16"), ("y1", 4 * C, "float32"), ("ym", 4 * C, "bfloat16"), ("yt", 4 * C, "bfloat16"),
@@ -130,7 +135,12 @@ def rank_program(g, core, T, topo):
         return T.kc[:, 128 * i:128 * i + 128], T.ks[:, 128 * i:128 * i + 128]
 
     def kz(k):
-        qz(*kk(k), T.kt[:, k * KW:(k + 1) * KW], "kt%d" % k, "kc%d" % k)
+        if k < 4: i, n = T.un[:, 3 - k:3 - k + KW], "un"
+        elif k < 8: i, n = T.kt[:, (k - 4) * KW:(k - 3) * KW], "kt%d" % k
+        else:
+            h, e = divmod(k - 8, 4)
+            i, n = T.sp[:, (KW + 4) * h + e:(KW + 4) * h + e + KW], "sp%d" % h
+        qz(*kk(k), i, n, "kc%d" % k)
 
     def scan(out, i, k, rd, wr):
         op("v", lambda: V.tensor_tensor_scan(out, i, k, -4.0 * B96, A.max, A.add), rd, wr)
@@ -150,98 +160,94 @@ def rank_program(g, core, T, topo):
 
     ld("y", T.xt0[:], T.x[:], "xt0")
     ld("s", T.ut[:], T.u[:], "ut")
-    ld("y", T.wk[:].bitcast(dt.uint8), T.wc[:], "wk")
-    ld("y", T.wp[:], T.ws[:], "wp")
-    ld("y", T.vt[:], T.v[:], "vt")
 
     iota(T.pi[:, 0:1], [[1, 1]], 0, 1, "pi", False)
+    iota(T.ij[:], [[1, C]], 0, 0, "ij")
     iota(T.ui[:, 0:16], [[16, 2], [32, 4], [0, 2]], 0, 0, "ui", False)
     iota(T.ui[:, 16:32], [[16, 2], [32, 4], [0, 2]], 1, 0, "ui", False)
-    iota(T.rowx[:, 0:256], [[0, 2], [1, 128]], 0, 0, "rowx")
-    iota(T.rowx[:, 256:C], [[1, 32]], 96, 0, "rowx")
-    iota(T.row16[:], [[0, 18], [1, 16]], 0, 0, "row16")
+    iota(T.ui[:, 32:40], [[0, 8]], 0, 0, "ui", False)
     iota(T.rowog[:], [[1, 8], [0, 16]], 0, 0, "rowog")
-    iota(T.ij[:], [[1, C]], 0, 0, "ij")
 
     def col(i):
         return T.fc[:, i:i + 1]
 
-    def picker(row, rn, c0, c1, step):
-        for t, n, c in ((T.t1, "t1", c0), (T.t2, "t2", c1)):
-            act(t[:], row, F.Abs, (rn, "f%d" % c), n, bias=col(c))
-            act(t[:], t[:], F.Relu, n, n, bias=col(14 if step == B16 else 15), scale=-step)
-
-    for i, x in ((13, TINY), (16, -TINY), (14, B16), (15, B96)):
+    for i, x in ((13, TINY), (16, -TINY)):
         ms(col(i), x, "f%d" % i)
-    ms(T.ui[:, 32:40], 0, "uz")
     cp(col(0), T.pi[:, 0:1], "pi", "f0")
-    for i, (o, k) in enumerate(((A.bitwise_and, 15), (A.bitwise_and, 31), (A.arith_shift_right, 4), (A.arith_shift_right, 5))):
+    for i, (o, k) in enumerate(((A.bitwise_and, 15), (A.bitwise_and, 31), (A.arith_shift_right, 5))):
         ts(T.pj[:, i:i + 1], T.pi[:, 0:1], k, None, o, None, "pi", "pj")
-    cp(T.fc[:, 1:5], T.pj[:], "pj", "f1")
-    for i, j, a, b in ((10, 0, -BIG, -0.5 * BIG), (5, 1, -1.0, 0.0), (6, 1, -1.0, 1.0), (7, 2, BIG, -0.5 * BIG), (8, 0, -1.0, 0.0),
-                       (9, 0, -1.0, 1.0), (11, 4, 2.0, 0.0), (12, 4, 2.0, 1.0)):
-        ts(col(i), col(j), a, b, A.mult, A.add, ("f0", "f1"), "f%d" % i)
-    act(T.hown[:], T.rowx[:], F.Identity, ("rowx", "f10"), "hown", bias=col(10), scale=BIG)
-    picker(T.row16[:], "row16", 5, 6, B16)
+    ts(col(10), col(0), -BIG, -0.5 * BIG, A.mult, A.add, "f0", "f10")
+    cp(T.fc[:, 1:4], T.pj[:, 0:3], "pj", "f1")
     for w, (lo, hi, val) in ((0, (0, 128, 512.0)), (1, (0, 128, 512.0)), (3, (0, 128, -512.0)), (2, (0, 96, 0.0)), (2, (96, 128, 512.0))):
-        ms(T.kt[lo:hi, 7 * KW + w:8 * KW:4], val, "kt7")
-    cp(T.ul[:], T.ui[:], ("ui", "uz"), "ul")
+        ms(T.kt[lo:hi, 2 * KW + w:3 * KW:4], val, "kt6")
+    for e, (a, b) in zip((0, 128, 256), ((0, 128), (0, 128), (96, 128))):
+        act(T.hown[:, e:e + b - a], T.ij[:, a:b], F.Identity, ("ij", "f10"), "hown", bias=col(10), scale=BIG)
+    ts(T.t1[:, 0:17], T.ij[:, 0:17], col(1), B16, A.is_equal, A.mult, ("ij", "f1"), "t1")
+    for i, j, a, b in ((11, 3, -2.0, 0.0), (12, 3, -2.0, -1.0), (7, 2, BIG, -0.5 * BIG), (5, 1, -18.0, PLUS - 9.0)):
+        ts(col(i), col(j), a, b, A.mult, A.add, "f1", "f%d" % i)
+    tt(T.k16[:, 0:16], T.t1[:, 0:16], T.t1[:, 1:17], A.subtract, "t1", "k16")
+    cp(T.ul[:], T.ui[:], "ui", "ul")
+    ts(T.k16[:, 15:16], T.k16[:, 15:16], -2.0 * B16, None, A.add, None, "k16", "k16")
+    for t, w in enumerate((0.5, 1.0, 0.5, 0.0)):
+        ms(T.kt[0:96, 3 * KW + t:4 * KW:4], w, "kt7")
+    ms(T.kt[96:128, 3 * KW:4 * KW], 0.0, "kt7")
+    kz(6)
     qz(T.uq[:], T.us[:], T.ut[:], "ut", ("uq", "us"))
 
-    def upick(i):
+    def upick(i, v):
         a, b = 128 * i, 128 * i + 128
         off = T.ul[:, 8 * i:8 * i + 8]
-        op("v", lambda: V.tensor_copy(T.up[:, a:b].bitcast(dt.uint32), T.uq[:, 0:128].bitcast(dt.uint32).indirect(off)), ("uq", "ul"), "up%d" % i)
-        op("s", lambda: S.activation(T.ups[:, a:b], T.us[:, 0:128].indirect(off), F.Copy), ("us", "ul"), "ups%d" % i)
+        if v: op("v", lambda: V.tensor_copy(T.up[:, a:b].bitcast(dt.uint32), T.uq[:, 0:128].bitcast(dt.uint32).indirect(off)), ("uq", "ul"), "up%d" % i)
+        else: op("s", lambda: S.activation(T.ups[:, a:b], T.us[:, 0:128].indirect(off), F.Copy), ("us", "ul"), "ups%d" % i)
 
-    upick(4)
+    upick(4, True)
     qz(T.xc0[:], T.xs0[:], T.xt0[:], "xt0", ("xc0", "xs0"))
     send(("xc0", "xs0"), ("lc0", "ls0"), "ax0", peers[0])
+    for x, n, c in ((T.t3, "t3", 11), (T.t4, "t4", 12)):
+        act(x[:], T.rowog[:], F.Abs, ("rowog", "f%d" % c), n, bias=col(c))
+    upick(4, False)
     iota(T.row32[:], [[0, 9], [1, 32]], 0, 0, "row32")
-    iota(T.row96[:], [[0, 3], [1, 96]], 0, 0, "row96")
-    for t in range(4):
-        iota(T.tm2[:, t:512:4], [[0, 128]], 8192 if t < 2 else 0, 0, "tm2")
-    for t in range(2, 4):
-        iota(T.cd[:, t:4 * C:4], [[0, C]], 0, 0, "cdz")
-    iota(T.ct[:, 3:4 * C:4], [[0, C]], 0, 0, "ctz")
-    for k in range(4):
-        iota(T.kt[:, k * KW:(k + 1) * KW], [[0, KW]], 0, 0, "kt%d" % k)
-    kz(7)
-    tt(T.k16[:], T.t1[:], T.t2[:], A.subtract, ("t1", "t2"), "k16")
-    ts(T.k16[:, 15:C:16], T.k16[:, 15:C:16], -2.0 * B16, None, A.add, None, "k16", "k16")
-    ts(T.t3[:, 0:128], T.rowog[:], col(11), None, A.is_equal, None, ("rowog", "f11"), "t3")
-    ts(T.t4[:, 0:128], T.rowog[:], col(12), None, A.is_equal, None, ("rowog", "f12"), "t4")
-    for i in range(4):
-        upick(i)
-    for k, w in ((4, (1.0, 1.0)), (5, (0.5, 0.5)), (6, (1.0, -1.0))):
+    grown = [16, 32, 64, 128, 256]
+    for k in (4, 5):
         for t in range(4):
             src, n = (T.t3, "t3") if t < 2 else (T.t4, "t4")
-            act(T.kt[:, k * KW + t:(k + 1) * KW:4], src[:, 0:128], F.Copy, n, "kt%d" % k, scale=w[t % 2])
+            w = 1.0 if k == 5 and t % 2 else 0.5
+            act(T.kt[:, (k - 4) * KW + t:(k - 3) * KW:4], src[:], F.Relu, n, "kt%d" % k, bias=w, scale=-w)
+            if grown:
+                n = grown.pop(0)
+                m = min(n, C - n)
+                act(T.k16[:, n:n + m], T.k16[:, 0:m], F.Copy, "k16", "k16")
+    for i in range(4):
+        upick(i, True)
+        upick(i, False)
     act(T.hb[:], T.row32[:], F.Identity, ("row32", "f7"), "hb", bias=col(7), scale=-BIG)
-
-    def spread(ks):
-        for k in ks:
-            act(T.kt[:, (9 + k) * KW:(10 + k) * KW], T.tm2[:], F.Copy, ("tm2", "bcm"), "kt%d" % (9 + k), scale=T.bcm[:, k:k + 1])
+    iota(T.tm2[:], [[0, KW + 4]], 512, 0, "tm2")
+    for h in range(2):
+        w = T.sp[:, (KW + 4) * h:(KW + 4) * (h + 1)]
+        op("g", lambda: g.affine_select(w, T.tm2[:], [[0, 129], [-16, 4]], A.is_ge, 0.0, -64 * h, 1), "tm2", "sp%d" % h)
+        op("g", lambda: g.affine_select(w, w, [[0, 129], [16, 4]], A.is_ge, 0.0, 64 * h + 15, -1), "sp%d" % h, "sp%d" % h)
+    for t in range(1, 4):
+        iota(T.cd[:, t:4 * C:4], [[0, C]], 0, 0, "cdz")
+    iota(T.ct[:, 3:4 * C:4], [[0, C]], 0, 0, "ctz")
+    iota(T.one[:], [[0, KW + 4]], 1, 0, "one")
+    op("g", lambda: g.affine_select(T.un[:], T.one[:], [[-1, KW + 4]], A.is_equal, 0.0, 3, 4), "one", "un")
+    for o, i, n in ((T.wk[:].bitcast(dt.uint8), T.wc[:], "wk"), (T.wp[:], T.ws[:], "wp"), (T.vt[:], T.v[:], "vt")):
+        ld("y", o, i, n, "lc0")
 
     def late_constants():
+        for k in (4, 5):
+            kz(k)
+        ts(T.t2[:, 0:97], T.ij[:, 0:97], col(0), B96, A.is_equal, A.mult, ("ij", "f0"), "t2")
         for m in range(2):
             ts(T.mk[:, m:m + 1], col(2), 15.5, None, (A.is_lt, A.is_gt)[m], None, "f1", "mk")
-            ts(T.mk[:, m + 2:m + 3], col(2), 15.5, B16 + 48, (A.is_lt, A.is_gt)[m], A.mult, "f1", "mk")
-        ts(T.bcm[:], T.ij[:, 0:8], 16.0, col(0), A.mult, A.is_equal, ("ij", "f0"), "bcm")
-        for t, w in enumerate((1.0, 1.0, 0.5, 0.0)):
-            ms(T.kt[0:96, 8 * KW + t:9 * KW:4], w, "kt8")
-        ms(T.kt[96:128, 8 * KW:9 * KW], 0.0, "kt8")
-        picker(T.row96[:], "row96", 8, 9, B96)
-        spread((0, 1))
-        for k in (4, 5, 6):
-            kz(k)
 
     def last_constants():
-        for i in (9, 10, 8):
-            kz(i)
-        tt(T.k96[:], T.t1[:], T.t2[:], A.subtract, ("t1", "t2"), "k96")
-        ts(T.k96[:, 95:192:96], T.k96[:, 95:192:96], -2.0 * B96, None, A.add, None, "k96", "k96")
-        ts(T.k96[:, 287:C], T.k96[:, 287:C], -B96 - 0.5, None, A.add, None, "k96", "k96")
+        tt(T.k96[:], T.t2[:, 0:96], T.t2[:, 1:97], A.subtract, "t2", "k96")
+        for m in range(2):
+            ts(T.mk[:, m + 2:m + 3], col(2), 15.5, B16 + 96, (A.is_lt, A.is_gt)[m], A.mult, "f1", "mk2")
+        ts(T.k96[:, 95:96], T.k96[:, 95:96], -B96 - 0.5, None, A.add, None, "k96", "k96")
+        ts(col(6), col(0), 111.5, B16 + 96, A.is_gt, A.mult, "f0", "f6")
+        ts(T.no[96:128, :], T.ij[96:128, 0:18], 0.0, T.mk[96:128, 3:4], A.mult, A.subtract, ("ij", "mk2"), "no7")
 
     wo, ct, zt = T.wo, T.ct, T.zt
     D01 = ("dd0", "dd1")
@@ -265,14 +271,16 @@ def rank_program(g, core, T, topo):
             ts(wo[:, 4 * e0 + q:4 * C:4], T.ps[:, 1536 + e0:1536 + C], sc, None, A.is_le, None, rq, "wo")
             ts(wo[:, 4 * e0 + 3:4 * e1:4], T.om[:, e0:e1], sc, None, A.is_equal, None, ("om", rq[1]), "wo")
         qz(T.qo[:], T.qos[:], wo[:], "wo", "qo")
-        mm(4, C, *kk(7), T.qo[:], T.qos[:], ("qo", "kc7"))
+        mm(4, C, *kk(6), T.qo[:], T.qos[:], ("qo", "kc6"))
         if t == 0:
             late_constants()
         scan(T.dd[:], ps(4), T.k16[:], ("ps4", "k16"), D01)
         tt(T.key0[:], ps(4), T.ij[:], A.subtract, ("ps4", "ij"), ("key0.0", "key0.1"))
         ts(T.nl[:], dv, -1.0 / 512, 287.0 - B16 / 512, A.mult, A.add, D01, ("nl0", "nl1"))
-        ts(T.nf[:], dv, -1.0 / 512, 287.0 - B16 / 512, A.mult, A.add, D01, "nf")
-        ts(T.ne[0:32, :], T.nf[0:32, :], T.mk[0:32, 0:1], None, A.mult, None, ("nf", "mk"), "ne")
+        ts(T.nf[:], dv, -1.0 / 512, 287.0 - B16 / 512, A.mult, A.add, D01, ("nf0", "nf1"))
+        if t == 0:
+            last_constants()
+        ts(T.ne[0:32, :], T.nf[0:32, :], T.mk[0:32, 0:1], None, A.mult, None, ("nf0", "nf1", "mk"), "ne")
         banks = ((5, 7), (6, 0), (1, 3), (2, 4))
         for k in range(4):
             for b in banks[k]:
@@ -285,7 +293,7 @@ def rank_program(g, core, T, topo):
             return "w%d.%d.%d" % (ty, w, p)
 
         def rows(ty):
-            wt, d0 = side(ty)[0], 8 * C * ty
+            wt, d0 = side(ty)[0], 20 * C * ty
             for par in range(2):
                 k = 2 * ty + par
                 o = C * k
@@ -294,85 +302,103 @@ def rank_program(g, core, T, topo):
                 k = 2 * ty + par
                 o = C * k
                 op("v", lambda: V.transpose(T.tr[:, o:o + C], T.rm[:, o:o + C]), "rm%d" % k, "tr%d" % k)
-            for w in range(2):
+            mine = [(w, [i for i in range(2) if x[i] in SCAL[ty]]) for w, x in enumerate(WORDS[ty]) if x[0] in SCAL[ty]]
+
+            def signs(w, sl):
+                cut = [0] + [32 * WORDS[ty][w][i] for i in sl] + [C]
+                for r in range(len(cut) - 1):
+                    lo, hi = cut[r], cut[r + 1]
+                    runs = [(0, 1, r > 0)] if len(sl) == 2 and r != 1 else [(i, 2, r > i) for i in sl]
+                    for f, st, s in runs if hi > lo else ():
+                        z, e = 4 * C * w + f + 4 * lo, 4 * C * w + 4 * hi
+                        act(wt[:, z:e:st], T.ds[:, d0 + z:d0 + e:st], F.Sign, ["ds%d.%d.%d" % (ty, w, p) for p in range(4) if p % 2 in sl] + ["f13", "f16"],
+                            [pl(ty, w, p) for p in range(4) if p % 2 in sl], bias=col(13 if s else 16))
+
+            for n, (w, sl) in enumerate(mine):
                 for par in range(2):
                     k = 2 * ty + par
                     bw = banks[k][1]
-                    for i in range(2):
-                        b, z = (0, 1, 7, 8)[2 * w + i], 4 * C * w + 2 * par + i
+                    for i in sl:
+                        b, z = WORDS[ty][w][i], 4 * C * w + 2 * par + i
                         act(T.ds[:, d0 + z:d0 + 4 * C * (w + 1):4], ps(bw), F.Identity, ("ps%d" % bw, "tr%d" % k), "ds%d.%d.%d" % (ty, w, 2 * par + i),
                             bias=T.tr[:, C * k + 32 * b:C * k + 32 * b + 1], scale=-1.0)
-            for w, st, lo, hi, s in ((0, 1, 32, C, 1), (0, 2, 0, 32, 1), (0, -2, 0, 32, -1),
-                                     (1, 1, 0, 224, -1), (1, 2, 224, 256, 1), (1, -2, 224, 256, -1), (1, 1, 256, C, 1)):
-                f = 4 * C * w + (st < 0)
-                act(wt[:, 12 * C + f + 4 * lo:12 * C + 4 * C * w + 4 * hi:abs(st)], T.ds[:, d0 + f + 4 * lo:d0 + 4 * C * w + 4 * hi:abs(st)], F.Sign,
-                    ["ds%d.%d.%d" % (ty, w, p) for p in range(4)] + ["f13", "f16"], [pl(ty, 3 + w, p) for p in range(4)], bias=col(13 if s > 0 else 16))
+                    if par == 0 and n: signs(*mine[n - 1])
+            signs(*mine[-1])
+
+        made = [0, 0]
 
         def word(ty, w):
             wt, qn, pb = side(ty)
             qc, qs = T[qn], T[qn + "s"]
-            c = (4, 4, 6, 5, 5)[w]
+            c = 5 if TIE in WORDS[ty][w] else 4
             qz(qc[:, C * w:C * w + C], qs[:, C * w:C * w + C], wt[:, 4 * C * w:4 * C * w + 4 * C], [pl(ty, w, p) for p in range(4)], qn + "%d" % w)
-            mm(pb, C, *kk(c), qc[:, C * w:C * w + C], qs[:, C * w:C * w + C], (qn + "%d" % w, "kc%d" % c), w == 0, w == 4)
+            mm(pb, C, *kk(c), qc[:, C * w:C * w + C], qs[:, C * w:C * w + C], (qn + "%d" % w, "kc%d" % c), made[ty] == 0, made[ty] == 4)
+            made[ty] += 1
 
-        due = []
-
-        def blocks(ty, par):
+        def block(ty, par, b):
             wt = side(ty)[0]
             k = 2 * ty + par
             bv = banks[k][0]
             rd, o = ("ps%d" % bv, "tr%d" % k), C * k
-            tt(wt[:, 8 * C + 2 * par + 1:12 * C:4], ps(bv), T.tr[:, o:o + C], A.is_equal, rd, pl(ty, 2, 2 * par + 1))
-            for b in range(2, 7):
-                w, p = (b - 2) // 2, 2 * par + b % 2
-                sc = T.tr[:, o + 32 * b:o + 32 * b + 1]
-                z = 4 * C * w + p
-                ts(wt[:, z:z + 128 * b - 3:4], ps(bv, 32 * b), sc, None, A.is_lt, None, rd, pl(ty, w, p))
-                ts(wt[:, z + 128 * b:4 * C * (w + 1):4], T.ps[:, 512 * bv + 32 * b:512 * bv + C], sc, None, A.is_le, None, rd, pl(ty, w, p))
-                while due:
-                    word(*due.pop())
-                if par and (b % 2 or b == 6): due.append((ty, w))
+            w, i = [(w, x.index(b)) for w, x in enumerate(WORDS[ty]) if b in x][0]
+            p = 2 * par + i
+            z = 4 * C * w + p
+            if b == TIE:
+                tt(wt[:, z:4 * C * (w + 1):4], ps(bv), T.tr[:, o:o + C], A.not_equal, rd, pl(ty, w, p))
+                return
+            sc = T.tr[:, o + 32 * b:o + 32 * b + 1]
+            ts(wt[:, z:z + 128 * b - 3:4], ps(bv, 32 * b), sc, 2.0, A.is_lt, A.mult, rd, pl(ty, w, p))
+            ts(wt[:, z + 128 * b:4 * C * (w + 1):4], T.ps[:, 512 * bv + 32 * b:512 * bv + C], sc, 2.0, A.is_le, A.mult, rd, pl(ty, w, p))
 
         rows(0)
-        blocks(0, 0)
+        for b in (TIE, 2, 3, 4, 5):
+            block(0, 0, b)
+        for b in (TIE, 2, 3, 4):
+            block(0, 1, b)
+        word(0, 0)
+        block(0, 1, 5)
+        word(0, 2)
         rows(1)
-        blocks(0, 1)
-        blocks(1, 0)
+        word(0, 1)
         word(0, 3)
+        block(1, 0, TIE)
+        block(1, 0, 2)
         word(0, 4)
-        blocks(1, 1)
+        block(1, 0, 3)
+        block(1, 0, 4)
         scan(T.dd[:], ps(5), T.k16[:], ("ps5", "k16"), D01)
-        word(*due.pop())
-        word(1, 3)
-        ts(T.aw[:], dv, B16 + 64, None, A.add, None, D01, "aw")
-        word(1, 4)
+        block(1, 0, 5)
+        ts(T.aw[:], dv, B16 + PLUS, None, A.add, None, D01, "aw")
+        block(1, 1, TIE)
         op("v", lambda: V.tensor_copy(T.of[:].indirect(T.aw[:]), T.ij[:]), ("ij", "aw"), "of")
+        block(1, 1, 2)
+        scan(T.kr[:], T.of[:], T.k16[:], ("of", "k16"), "kr")
+        block(1, 1, 3)
+        ts(T.ow[:], T.kr[:, 15:C:16], B16, None, A.add, None, "kr", "ow")
+        block(1, 1, 4)
+        word(1, 0)
+        block(1, 1, 5)
+        for w in (2, 3, 1, 4):
+            word(1, w)
         if t == 0:
-            spread(range(2, 8))
-            for k in range(4):
-                ts(T.kt[:, k * KW + k:(k + 1) * KW:4], T.ij[:, 0:128], col(0), None, A.is_equal, None, ("ij", "f0"), "kt%d" % k)
-            last_constants()
-        ts(T.bs[:], ps(1), 0.0625, -5.0, A.mult, A.add, "ps1", "bs")
-        op("v", lambda: V.tensor_copy(T.cs[:].indirect(T.aw[:]), T.bs[:]), ("bs", "aw"), "cs")
+            for i in (8, 9, 7):
+                kz(i)
+        ts(T.bs[:], ps(1), col(5), None, A.add, None, ("ps1", "f5"), "bs")
         for h, (a, b) in enumerate(PARTS):
-            ts(T.cd[:, 4 * a:4 * b:4], T.cs[:, a:b], MAGIC, MAGIC, A.add, A.subtract, "cs", "cd0%d" % h)
+            op("v", lambda: V.tensor_scalar(T.cd[:, 4 * a:4 * b:4], T.bs[:].indirect(T.ow[:, a // 16:b // 16]), -9.0, 9.0, A.max, A.min), ("bs", "ow"), "cd%d" % h)
         for h, (a, b) in enumerate(PARTS):
-            tt(T.cd[:, 4 * a + 1:4 * b:4], T.cs[:, a:b], T.cd[:, 4 * a:4 * b:4], A.subtract, ("cs", "cd0%d" % h), "cd1%d" % h)
-        for h, (a, b) in enumerate(PARTS):
-            qz(T.qc[:, a:b], T.qcs[:, a:b], T.cd[:, 4 * a:4 * b], ("cd0%d" % h, "cd1%d" % h, "cdz"), "qc")
-        bb = (0, 2, 3, 4, 6, 7, 0, 2)
+            qz(T.qc[:, a:b], T.qcs[:, a:b], T.cd[:, 4 * a:4 * b], ("cd%d" % h, "cdz"), "qc")
+        bb = (0, 2) * 4
 
         def table(k):
-            mm(bb[k], C, *kk(9 + k), T.qc[:], T.qcs[:], ("qc", "kc%d" % (9 + k)))
+            mm(bb[k], C, *kk(8 + k), T.qc[:], T.qcs[:], ("qc", "kc%d" % (8 + k)))
 
         def keep(k):
             if k: act(T.cw[:, C * k:C * k + C], ps(bb[k]), F.Copy, "ps%d" % bb[k], "cw%d" % k)
             else: cp(T.cw[:, 0:C], ps(bb[0]), "ps%d" % bb[0], "cw0")
 
-        for k in range(2 if t == 0 else 6):
-            table(k)
-        scan(T.kr[:], T.of[:], T.k16[:], ("of", "k16"), "kr")
-        ts(T.ow[:], T.kr[:, 15:C:16], B16, None, A.add, None, "kr", "ow")
+        table(0)
+        table(1)
         keep(0)
         keep(1)
         keys = ((T.key0, "key0"), (T.key1, "key1"))
@@ -385,7 +411,7 @@ def rank_program(g, core, T, topo):
 
         def turns(h):
             a, b = PARTS[h]
-            ts(T.nl[:, a // 16:b // 16], dv[:, a // 16:b // 16], B16 + 48, None, A.add, None, "%s%d" % (dn, h), "nl%d" % h)
+            ts(T.nl[:, a // 16:b // 16], dv[:, a // 16:b // 16], B16 + 96, None, A.add, None, "%s%d" % (dn, h), "nl%d" % h)
 
         fb = (3, 4, 6, 7)
         dn = "dd"
@@ -393,9 +419,8 @@ def rank_program(g, core, T, topo):
 
         def z_list(h, i):
             s = slice(PARTS[h][0] // 16, PARTS[h][1] // 16)
-            if i == 0: ts(T.no[96:128, s], dv[96:128, s], B16 + 48, T.mk[96:128, 1:2], A.add, A.mult, (dn + "%d" % h, "mk"), "no")
-            if i == 1: tt(T.nf[:, s], T.ne[:, s], T.no[:, s], A.add, ("ne", "no"), "nf%d" % h)
-            if i == 2: cp(T.nz[:, s], T.nf[:, s], "nf%d" % h, "nz%d" % h)
+            if i == 0: tt(T.nf[:, s], dv[:, s], T.nr[:, s], A.max, (dn + "%d" % h, "nr"), "nf%d" % h)
+            if i == 1: ts(T.nz[:, s], T.nf[:, s], col(6), None, A.add, None, ("nf%d" % h, "f6"), "nz%d" % h)
 
         def z_part(b, h, v):
             a, e = PARTS[h]
@@ -413,89 +438,67 @@ def rank_program(g, core, T, topo):
             k0, k1 = kn + ".0", kn + ".1"
 
             def pick(b, rd):
-                scan(T.col[:, 96 * b:96 * b + 96], kr[:, 96 * b:96 * b + 96], T.k96[:, 96 * b:96 * b + 96], rd + ("k96",), "col%d" % b)
+                scan(T.col[:, 96 * b:96 * b + 96], kr[:, 96 * b:96 * b + 96], T.k96[:], rd + ("k96",), "col%d" % b)
 
             def less(b, h):
                 a, e = PARTS[h]
-                ts(ct[:, 4 * a + b:4 * e:4], kr[:, a:e], -B96, T.col[:, 96 * b + 95:96 * b + 96], A.add, A.is_lt, ((k0, k1)[h], "col%d" % b), "ct%d.%d" % (b, h))
+                o, i, sc = ct[:, 4 * a + b:4 * e:4], kr[:, a:e], T.col[:, 96 * b + 95:96 * b + 96]
+                rd, wr = ((k0, k1)[h], "col%d" % b), "ct%d.%d" % (b, h)
+                if b == 1: ts(o, i, sc, None, A.is_lt, None, rd, wr)
+                else: act(o, i, F.Sign, rd, wr, bias=sc, scale=-1.0)
 
             grow(k - 1, 0)
-            if k > 1: turns(1)
-            pick(0, (k0,))
             grow(k - 1, 1)
-            less(0, 0)
+            pick(0, (k0,))
             pick(2, (k1,))
-            for h, (a, b) in enumerate(PARTS):
-                act(ct[:, 4 * a + 2:4 * b:4], kr[:, a:b], F.Sign, ((k0, k1)[h], "col2"), "ct2.%d" % h, bias=T.col[:, 287:288], scale=-1.0)
             pick(1, (k0, k1))
-            less(0, 1)
-            less(1, 0)
-            less(1, 1)
+            for b, h in ((0, 0), (2, 0), (0, 1), (2, 1), (1, 0), (1, 1)):
+                less(b, h)
             for h, (a, b) in enumerate(PARTS):
                 qz(T.qt[:, a:b], T.qts[:, a:b], ct[:, 4 * a:4 * b], ["ct%d.%d" % (i, h) for i in range(3)] + ["ctz"], "qt%d" % h)
-                mm((5, 1)[h], b - a, *kk(8), T.qt[:, a:b], T.qts[:, a:b], ("qt%d" % h, "kc8"))
+                mm((5, 1)[h], b - a, *kk(7), T.qt[:, a:b], T.qts[:, a:b], ("qt%d" % h, "kc7"))
             dx, dn = ((T.dd, "dd"), (T.de, "de"))[k % 2]
             dv = dx[:, 15:C:16]
-            if t == 0:
-                for i in {1: (11, 12), 2: (13, 14, 0), 3: (15, 16, 1), 4: (2, 3)}.get(k, ()):
-                    kz(i)
+            if t == 0 and k < 7:
+                kz(9 + k)
+                if k < 5: kz(k - 1)
+            if k == 7: tt(T.nr[:], T.ne[:], T.no[:], A.add, ("ne", "no", "no7"), "nr")
             scan(dx[:, 0:H], ps(5, H), T.k16[:, 0:H], ("ps5", "k16"), dn + "0")
-            if k <= 3:
-                if t == 0:
-                    table(2 * k)
-                    table(2 * k + 1)
-                elif k == 1:
-                    table(6)
-                    table(7)
-                keep(2 * k)
-                keep(2 * k + 1)
-            if k in (4, 5):
-                for b in (2 * k - 8, 2 * k - 7):
-                    mm(fb[b], C, *kk(b), lc[:], ls[:], ln + ("kc%d" % b,))
-                    act(T.ff[:, C * b:C * b + C], ps(fb[b]), F.Copy, "ps%d" % fb[b], "ff%d" % b)
-            if k in (6, 7):
-                for b in (2 * k - 12, 2 * k - 11):
-                    op("s", lambda: S.activation(T.fs[:, C * b:C * b + C], T.ff[:, C * b:C * b + C].indirect(T.ow[:]), F.Copy), ("ff%d" % b, "ow"), "fs%d" % b)
-            if k < 7: turns(0)
-            else:
-                for i in range(3):
-                    z_list(0, i)
+            if k <= 6:
+                table(k + 1)
+                keep(k + 1)
+            if 2 <= k <= 5:
+                b = k - 2
+                mm(fb[b], C, *kk(b), lc[:], ls[:], ln + ("kc%d" % b,))
+                act(T.ff[:, C * b:C * b + C], ps(fb[b]), F.Copy, "ps%d" % fb[b], "ff%d" % b)
+            if 3 <= k <= 6:
+                b = k - 3
+                op("s", lambda: S.activation(T.fs[:, C * b:C * b + C], T.ff[:, C * b:C * b + C].indirect(T.ow[:]), F.Copy), ("ff%d" % b, "ow"), "fs%d" % b)
             scan(dx[:, H:C], ps(1, C - H), T.k16[:, H:C], ("ps1", "k16"), dn + "1")
-            p0, m = 32 * (k // 2), k % 2
-            p1 = p0 + 32
-            nb, nn = ((T.ne, "ne"), (T.no, "no"))[m]
-            if k < 7: act(nb[p0:p1, :], dv[p0:p1, :], F.Identity, (dn + "0", dn + "1", "mk"), nn, bias=T.mk[p0:p1, 2 + m:3 + m], scale=T.mk[p0:p1, m:m + 1])
-        z_part(0, 0, True)
-        z_part(3, 0, False)
-        z_list(1, 0)
-        z_part(1, 0, True)
-        z_list(1, 1)
-        z_part(2, 0, True)
-        z_list(1, 2)
+            if k < 7:
+                turns(0)
+                turns(1)
+                p0, m = 32 * (k // 2), k % 2
+                p1 = p0 + 32
+                nb, nn = ((T.ne, "ne"), (T.no, "no"))[m]
+                act(nb[p0:p1, :], dv[p0:p1, :], F.Identity, (dn + "0", dn + "1", "mk", "mk2"), nn, bias=T.mk[p0:p1, 2 + m:3 + m], scale=T.mk[p0:p1, m:m + 1])
+        for i in range(2):
+            z_list(0, i)
+            z_list(1, i)
+        for h in range(2):
+            for b in range(4):
+                z_part(b, h, b < 2)
         z_codes(0)
-        z_part(0, 1, True)
-        z_part(2, 1, False)
-        z_part(3, 1, False)
-        z_part(1, 1, True)
         z_codes(1)
-        if t:
-            turns(0)
-            turns(1)
-        dv = T.dd[:, 15:C:16]
         for b in range(4):
             for h in range(2):
                 w = 128 * (b + 4 * h)
                 mm(2 * b + h, C, T.wk[:, w:w + 128], T.wp[:, w:w + 128], zc[:], zs[:], ("zc", "wk", "wp"))
-        op("v", lambda: V.tensor_copy(T.nv[:].indirect(T.nz[:]), T.ij[:]), ("ij", "nz0", "nz1"), "nv")
-        cp(T.kr[:], T.nv[:].indirect(T.aw[:]), ("nv", "aw"), "kr")
-        if t:
-            grow(7, 0)
-            grow(7, 1)
-        scan(T.dd[:], T.kr[:], T.k16[:], ("kr", "k16"), D01)
-        ts(T.kw[:], dv, B16, None, A.add, None, D01, "kw")
+
+        def copy(b):
+            act(T.y1[:, C * b:C * b + C], ps(2 * b), F.Copy, "ps%d" % (2 * b), "y1%d" % b)
 
         def largest(b):
-            act(T.y1[:, C * b:C * b + C], ps(2 * b), F.Copy, "ps%d" % (2 * b), "y1%d" % b)
             tt(T.ym[:, C * b:C * b + C], ps(2 * b + 1), T.y1[:, C * b:C * b + C], A.max, ("ps%d" % (2 * b + 1), "y1%d" % b), "ym%d" % b)
 
         def put(b, v):
@@ -504,12 +507,21 @@ def rank_program(g, core, T, topo):
             if v: op("v", lambda: V.tensor_scalar(o, i, 0.03125, None, A.mult), rd, wr)
             else: op("s", lambda: S.activation(o, i, F.Copy, scale=0.03125), rd, wr)
 
-        for b in range(3):
-            largest(b)
-        put(0, True)
+        op("v", lambda: V.tensor_copy(T.nv[:].indirect(T.nz[:]), T.ij[:]), ("ij", "nz0", "nz1"), "nv")
+        copy(0)
+        op("s", lambda: S.activation(T.kr[:], T.nv[:].indirect(T.aw[:]), F.Copy), ("nv", "aw"), "kr")
+        largest(0)
+        copy(1)
+        scan(T.dd[:], T.kr[:], T.k16[:], ("kr", "k16"), D01)
+        copy(2)
+        copy(3)
+        largest(1)
+        ts(T.kw[:], T.dd[:, 15:C:16], B16, None, A.add, None, D01, "kw")
+        largest(2)
+        put(0, False)
         largest(3)
         put(1, False)
-        put(2, False)
+        put(2, True)
         put(3, True)
         qn = ("qc%d" % t, "qs%d" % t)
         qz(T[qn[0]][:], T[qn[1]][:], T.yt[:], ["yt%d" % b for b in range(4)], qn)
@@ -517,10 +529,14 @@ def rank_program(g, core, T, topo):
         for b in range(4):
             mm(b, C, *kk(b), xc[:], xs[:], xn + ("kc%d" % b,), True, False)
         if t == 1:
+            turns(0)
+            turns(1)
+            qz(T.vq[:], T.vs[:], T.vt[:], "vt", "vq")
+            grow(7, 0)
+            grow(7, 1)
             tt(T.to[0:1, :], T.key0[0:1, :], T.ij[0:1, :], A.add, ("key0.0", "key0.1", "ij"), "to")
             ts(T.to[0:1, :], T.to[0:1, :], 1.0 / 512, 1152.0, A.mult, A.add, "to", "to")
             ld("y", T.tot[:], T.to[0:1, :], "tot", "to")
-            qz(T.vq[:], T.vs[:], T.vt[:], "vt", "vq")
         xt = T["xt%d" % (t + 1)]
         for b in range(4):
             mm(b, C, *kk(b), T["bc%d" % t][:], T["bs%d" % t][:], ("bc%d" % t, "bs%d" % t, "kc%d" % b), False, True)

@@ -1,16 +1,18 @@
 from concourse.mybir import dt, AluOpType as A, ActivationFunctionType as F
 
 C = 288
-H = 160
+H = 128
 PARTS = ((0, H), (H, C))
+GROWS = ((0, H), (H, 192), (192, C))
 KW = 512
 B16, B96 = 2.0 ** 18, 2.0 ** 21
 BIG, TINY = 1e29, 2.0 ** -119
-NK = 16
+NK = 18
 TIE = 9
-WORDS = (((2, 3), (4, 5), (6, TIE), (0, 1), (7, 8)),) * 2
-SCAL = ((6, 0, 1, 7, 8),) * 2
-PLUS = 16.0 * 5 - 32.0
+WORDS = ((2, 3), (4, 5), (6, TIE), (0, 1), (7, 8))
+BWORDS = ((0, 1, 2, 6), (7, 8, 3, 4), (5, TIE))
+SCAL, BSCAL = (6, 0, 1, 7, 8), ((0, 1, 2, 6, 7, 8), (0, 1, 2, 6, 7, 8, 3, 4))
+PLUS, BPLUS = 16.0 * 5 - 32.0, 16.0 * 6 - 32.0
 
 MXC, PL = "float8_e4m3fn_x4", "uint8"
 SCRATCH = {}
@@ -30,19 +32,20 @@ for _t in range(2):
         _buf(_n + "c%d" % _t, C, MXC)
         _buf(_n + "s%d" % _t, C, PL)
 for _n, _c, _d in (("wk", 1024, MXC), ("wp", 1024, PL), ("ut", 512, "bfloat16"), ("vt", 512, "bfloat16"), ("uq", 128, MXC), ("us", 128, PL),
-                   ("vq", 128, MXC), ("vs", 128, PL), ("up", 640, MXC), ("ups", 640, PL), ("kt", 4 * KW, "bfloat16"), ("sp", 2 * KW + 8, "bfloat16"),
+                   ("vq", 128, MXC), ("vs", 128, PL), ("up", 640, MXC), ("ups", 640, PL), ("kt", 6 * KW, "bfloat16"), ("sp", 2 * KW + 8, "bfloat16"),
                    ("un", KW + 4, "bfloat16"), ("kc", NK * 128, MXC), ("ks", NK * 128, PL), ("tm2", KW + 4, "bfloat16"), ("one", KW + 4, "bfloat16"),
                    ("ui", 40, "int32"), ("ul", 40, "uint16"), ("pi", 2, "int32"), ("pj", 4, "int32"),
-                   ("fc", 20, "float32"), ("mk", 4, "float32"), ("ij", C, "float32"), ("row32", C, "float32"),
+                   ("fc", 20, "float32"), ("mk", 4, "float32"), ("ij", C, "float32"),
                    ("rowog", 128, "float32"), ("hown", C, "float32"), ("hb", C, "float32"), ("k16", C, "float32"), ("k96", 96, "float32"),
-                   ("t1", 32, "float32"), ("t2", 128, "float32"), ("t3", 128, "float32"), ("t4", 128, "float32"),
+                   ("t1", 32, "float32"), ("t2", 128, "float32"), ("t3", 128, "float32"), ("t4", 128, "float32"), ("t5", 128, "float32"),
                    ("wo", 4 * C, "bfloat16"), ("qo", C, MXC), ("qos", C, PL), ("om", C, "float32"),
-                   ("wa", 20 * C, "bfloat16"), ("wb", 20 * C, "bfloat16"), ("qa", 5 * C, MXC), ("qas", 5 * C, PL), ("qb", 5 * C, MXC),
-                   ("qbs", 5 * C, PL), ("rm", 4 * C, "float32"), ("tr", 4 * C, "float32"), ("ds", 40 * C, "float32"), ("dd", C, "float32"),
+                   ("wa", 20 * C, "bfloat16"), ("wb", 24 * C, "bfloat16"), ("qa", 5 * C, MXC), ("qas", 5 * C, PL), ("qb", 6 * C, MXC),
+                   ("qbs", 6 * C, PL), ("rm", 4 * C, "float32"), ("tr", 4 * C, "float32"), ("ds", 44 * C, "float32"), ("dd", C, "float32"),
                    ("de", C, "float32"), ("key0", C, "float32"), ("key1", C, "float32"), ("col", C, "float32"), ("nl", 18, "uint16"),
                    ("nf", 18, "float32"), ("ne", 18, "float32"), ("no", 18, "float32"), ("nr", 18, "float32"), ("nz", 18, "uint16"),
-                   ("aw", 18, "uint16"), ("ow", 18, "uint16"), ("kw", 18, "uint16"), ("bs", C, "float32"), ("of", C, "float32"),
-                   ("nv", C, "float32"), ("kr", C, "float32"), ("cd", 4 * C, "bfloat16"), ("qc", C, MXC), ("qcs", C, PL), ("cw", 8 * C, "float32"),
+                   ("nx", 18, "uint16"), ("ox", 18, "uint16"), ("nid", 18, "float32"), ("aw", 18, "uint16"), ("ow", 18, "uint16"), ("kw", 18, "uint16"), ("bs", 2 * C, "float32"), ("of", C, "float32"),
+                   ("nv", C, "float32"), ("kr", C, "float32"), ("cd", 8 * C, "bfloat16"), ("qc", 2 * C, MXC), ("qcs", 2 * C, PL),
+                   ("cw", 8 * C, "float32"),
                    ("ct", 4 * C, "bfloat16"), ("qt", C, MXC), ("qts", C, PL), ("ff", 4 * C, "bfloat16"), ("fs", 4 * C, "bfloat16"),
                    ("zt", 4 * C, "bfloat16"), ("y1", 4 * C, "float32"), ("ym", 4 * C, "bfloat16"), ("yt", 4 * C, "bfloat16"),
                    ("yo", C, "float32"), ("to", C, "float32")):
@@ -137,6 +140,7 @@ def rank_program(g, core, T, topo):
     def kz(k):
         if k < 4: i, n = T.un[:, 3 - k:3 - k + KW], "un"
         elif k < 8: i, n = T.kt[:, (k - 4) * KW:(k - 3) * KW], "kt%d" % k
+        elif k > 15: i, n = T.kt[:, (k - 12) * KW:(k - 11) * KW], "kt%d" % k
         else:
             h, e = divmod(k - 8, 4)
             i, n = T.sp[:, (KW + 4) * h + e:(KW + 4) * h + e + KW], "sp%d" % h
@@ -164,7 +168,7 @@ def rank_program(g, core, T, topo):
     iota(T.pi[:, 0:1], [[1, 1]], 0, 1, "pi", False)
     iota(T.ij[:], [[1, C]], 0, 0, "ij")
     iota(T.ui[:, 0:16], [[16, 2], [32, 4], [0, 2]], 0, 0, "ui", False)
-    iota(T.ui[:, 16:32], [[16, 2], [32, 4], [0, 2]], 1, 0, "ui", False)
+    iota(T.ui[:, 16:32], [[64, 2], [16, 4], [0, 2]], 1, 0, "ui", False)
     iota(T.ui[:, 32:40], [[0, 8]], 0, 0, "ui", False)
     iota(T.rowog[:], [[1, 8], [0, 16]], 0, 0, "rowog")
 
@@ -183,7 +187,8 @@ def rank_program(g, core, T, topo):
     for e, (a, b) in zip((0, 128, 256), ((0, 128), (0, 128), (96, 128))):
         act(T.hown[:, e:e + b - a], T.ij[:, a:b], F.Identity, ("ij", "f10"), "hown", bias=col(10), scale=BIG)
     ts(T.t1[:, 0:17], T.ij[:, 0:17], col(1), B16, A.is_equal, A.mult, ("ij", "f1"), "t1")
-    for i, j, a, b in ((11, 3, -2.0, 0.0), (12, 3, -2.0, -1.0), (7, 2, BIG, -0.5 * BIG), (5, 1, -18.0, PLUS - 9.0)):
+    for i, j, a, b in ((11, 3, -2.0, 0.0), (12, 3, -2.0, -1.0), (7, 2, BIG, -0.5 * BIG), (5, 1, -18.0, BPLUS - 9.0), (8, 3, -1.0, 0.0),
+                       (9, 1, -18.0, BPLUS + 23.0)):
         ts(col(i), col(j), a, b, A.mult, A.add, "f1", "f%d" % i)
     tt(T.k16[:, 0:16], T.t1[:, 0:16], T.t1[:, 1:17], A.subtract, "t1", "k16")
     cp(T.ul[:], T.ui[:], "ui", "ul")
@@ -205,8 +210,11 @@ def rank_program(g, core, T, topo):
     send(("xc0", "xs0"), ("lc0", "ls0"), "ax0", peers[0])
     for x, n, c in ((T.t3, "t3", 11), (T.t4, "t4", 12)):
         act(x[:], T.rowog[:], F.Abs, ("rowog", "f%d" % c), n, bias=col(c))
+    for e in (0, 64):
+        act(T.t5[:, e:e + 64], T.rowog[:, 0:64], F.Abs, ("rowog", "f8"), "t5", bias=col(8))
+    for e in range(0, C, 32):
+        act(T.hb[:, e:e + 32], T.ij[:, 0:32], F.Identity, ("ij", "f7"), "hb", bias=col(7), scale=-BIG)
     upick(4, False)
-    iota(T.row32[:], [[0, 9], [1, 32]], 0, 0, "row32")
     grown = [16, 32, 64, 128, 256]
     for k in (4, 5):
         for t in range(4):
@@ -220,15 +228,24 @@ def rank_program(g, core, T, topo):
     for i in range(4):
         upick(i, True)
         upick(i, False)
-    act(T.hb[:], T.row32[:], F.Identity, ("row32", "f7"), "hb", bias=col(7), scale=-BIG)
+    for k, ws in ((16, (0.5, 0.5, 0.5, 0.5)), (17, (0.5, 1.0, 0.0, 0.0))):
+        for t, w in enumerate(ws):
+            act(T.kt[:, (k - 12) * KW + t:(k - 11) * KW:4], T.t5[:], F.Relu, "t5", "kt%d" % k, bias=w, scale=-w)
+    for e in range(2):
+        for t in (2, 3):
+            iota(T.wb[:, (12 * e + 8) * C + t:(12 * e + 12) * C:4], [[0, C]], 0, 0, "wbz")
     iota(T.tm2[:], [[0, KW + 4]], 512, 0, "tm2")
-    for h in range(2):
+
+    def groups(h):
         w = T.sp[:, (KW + 4) * h:(KW + 4) * (h + 1)]
         op("g", lambda: g.affine_select(w, T.tm2[:], [[0, 129], [-16, 4]], A.is_ge, 0.0, -64 * h, 1), "tm2", "sp%d" % h)
         op("g", lambda: g.affine_select(w, w, [[0, 129], [16, 4]], A.is_ge, 0.0, 64 * h + 15, -1), "sp%d" % h, "sp%d" % h)
+
+    groups(0)
     for t in range(1, 4):
-        iota(T.cd[:, t:4 * C:4], [[0, C]], 0, 0, "cdz")
+        iota(T.cd[:, t:8 * C:4], [[0, 2 * C]], 0, 0, "cdz")
     iota(T.ct[:, 3:4 * C:4], [[0, C]], 0, 0, "ctz")
+    groups(1)
     iota(T.one[:], [[0, KW + 4]], 1, 0, "one")
     op("g", lambda: g.affine_select(T.un[:], T.one[:], [[-1, KW + 4]], A.is_equal, 0.0, 3, 4), "one", "un")
     for o, i, n in ((T.wk[:].bitcast(dt.uint8), T.wc[:], "wk"), (T.wp[:], T.ws[:], "wp"), (T.vt[:], T.v[:], "vt")):
@@ -240,17 +257,20 @@ def rank_program(g, core, T, topo):
         ts(T.t2[:, 0:97], T.ij[:, 0:97], col(0), B96, A.is_equal, A.mult, ("ij", "f0"), "t2")
         for m in range(2):
             ts(T.mk[:, m:m + 1], col(2), 15.5, None, (A.is_lt, A.is_gt)[m], None, "f1", "mk")
-
-    def last_constants():
-        tt(T.k96[:], T.t2[:, 0:96], T.t2[:, 1:97], A.subtract, "t2", "k96")
-        for m in range(2):
             ts(T.mk[:, m + 2:m + 3], col(2), 15.5, B16 + 96, (A.is_lt, A.is_gt)[m], A.mult, "f1", "mk2")
-        ts(T.k96[:, 95:96], T.k96[:, 95:96], -B96 - 0.5, None, A.add, None, "k96", "k96")
+        tt(T.k96[:], T.t2[:, 0:96], T.t2[:, 1:97], A.subtract, "t2", "k96")
+        ts(col(4), col(0), 15.5, None, A.is_lt, None, "f0", "f4")
+        ts(col(14), col(0), 15.5, None, A.is_gt, None, "f0", "f14")
         ts(col(6), col(0), 111.5, B16 + 96, A.is_gt, A.mult, "f0", "f6")
         ts(T.no[96:128, :], T.ij[96:128, 0:18], 0.0, T.mk[96:128, 3:4], A.mult, A.subtract, ("ij", "mk2"), "no7")
+        for k in (16, 17):
+            kz(k)
+        ts(T.nid[:], T.ij[:, 0:C:16], col(1), col(14), A.add, A.mult, ("ij", "f1", "f14"), "nid")
+        ts(T.k96[:, 95:96], T.k96[:, 95:96], -B96 - 0.5, None, A.add, None, "k96", "k96")
 
     wo, ct, zt = T.wo, T.ct, T.zt
     D01 = ("dd0", "dd1")
+    K3 = ("key0.0", "key0.1", "key0.2")
     for t in range(2):
         peer = peers[t]
         dv = T.dd[:, 15:C:16]
@@ -258,6 +278,11 @@ def rank_program(g, core, T, topo):
         xn = ("xc%d" % t, "xs%d" % t)
         lc, ls = T["lc%d" % t], T["ls%d" % t]
         ln = ("lc%d" % t, "ls%d" % t)
+
+        def first(*ks):
+            for i in ks if t == 0 else ():
+                kz(i)
+
         m0 = (0, 128, 160)
         mm(3, C, T.up[:, 512:640], T.ups[:, 512:640], xc[:], xs[:], xn + ("up4", "ups4"))
         for q in range(3):
@@ -274,146 +299,181 @@ def rank_program(g, core, T, topo):
         mm(4, C, *kk(6), T.qo[:], T.qos[:], ("qo", "kc6"))
         if t == 0:
             late_constants()
-        scan(T.dd[:], ps(4), T.k16[:], ("ps4", "k16"), D01)
-        tt(T.key0[:], ps(4), T.ij[:], A.subtract, ("ps4", "ij"), ("key0.0", "key0.1"))
-        ts(T.nl[:], dv, -1.0 / 512, 287.0 - B16 / 512, A.mult, A.add, D01, ("nl0", "nl1"))
-        ts(T.nf[:], dv, -1.0 / 512, 287.0 - B16 / 512, A.mult, A.add, D01, ("nf0", "nf1"))
-        if t == 0:
-            last_constants()
-        ts(T.ne[0:32, :], T.nf[0:32, :], T.mk[0:32, 0:1], None, A.mult, None, ("nf0", "nf1", "mk"), "ne")
-        banks = ((5, 7), (6, 0), (1, 3), (2, 4))
-        for k in range(4):
-            for b in banks[k]:
-                mm(b, C, T.up[:, 128 * k:128 * k + 128], T.ups[:, 128 * k:128 * k + 128], lc[:], ls[:], ln + ("up%d" % k, "ups%d" % k))
+        banks = ((5, 7), (6, 0), (1, 3), (4, 7))
 
-        def side(ty):
-            return (T.wa, "qa", 5) if ty == 0 else (T.wb, "qb", 1)
+        def scores(k, e):
+            mm(banks[k][e], C, T.up[:, 128 * k:128 * k + 128], T.ups[:, 128 * k:128 * k + 128], lc[:], ls[:], ln + ("up%d" % k, "ups%d" % k))
 
-        def pl(ty, w, p):
-            return "w%d.%d.%d" % (ty, w, p)
+        for k, e in ((0, 0), (1, 0), (0, 1), (1, 1), (2, 0), (2, 1)):
+            scores(k, e)
 
-        def rows(ty):
-            wt, d0 = side(ty)[0], 20 * C * ty
-            for par in range(2):
-                k = 2 * ty + par
-                o = C * k
-                tt(T.rm[:, o:o + C], ps(banks[k][0]), T.hb[:], A.max, ("ps%d" % banks[k][0], "hb"), "rm%d" % k)
-            for par in range(2):
-                k = 2 * ty + par
-                o = C * k
-                op("v", lambda: V.transpose(T.tr[:, o:o + C], T.rm[:, o:o + C]), "rm%d" % k, "tr%d" % k)
-            mine = [(w, [i for i in range(2) if x[i] in SCAL[ty]]) for w, x in enumerate(WORDS[ty]) if x[0] in SCAL[ty]]
+        def mask(k):
+            tt(T.rm[:, C * k:C * k + C], ps(banks[k][0]), T.hb[:], A.max, ("ps%d" % banks[k][0], "hb"), "rm%d" % k)
 
-            def signs(w, sl):
-                cut = [0] + [32 * WORDS[ty][w][i] for i in sl] + [C]
-                for r in range(len(cut) - 1):
-                    lo, hi = cut[r], cut[r + 1]
-                    runs = [(0, 1, r > 0)] if len(sl) == 2 and r != 1 else [(i, 2, r > i) for i in sl]
-                    for f, st, s in runs if hi > lo else ():
-                        z, e = 4 * C * w + f + 4 * lo, 4 * C * w + 4 * hi
-                        act(wt[:, z:e:st], T.ds[:, d0 + z:d0 + e:st], F.Sign, ["ds%d.%d.%d" % (ty, w, p) for p in range(4) if p % 2 in sl] + ["f13", "f16"],
-                            [pl(ty, w, p) for p in range(4) if p % 2 in sl], bias=col(13 if s else 16))
+        def turn(k):
+            op("v", lambda: V.transpose(T.tr[:, C * k:C * k + C], T.rm[:, C * k:C * k + C]), "rm%d" % k, "tr%d" % k)
 
-            for n, (w, sl) in enumerate(mine):
-                for par in range(2):
-                    k = 2 * ty + par
-                    bw = banks[k][1]
-                    for i in sl:
-                        b, z = WORDS[ty][w][i], 4 * C * w + 2 * par + i
-                        act(T.ds[:, d0 + z:d0 + 4 * C * (w + 1):4], ps(bw), F.Identity, ("ps%d" % bw, "tr%d" % k), "ds%d.%d.%d" % (ty, w, 2 * par + i),
-                            bias=T.tr[:, C * k + 32 * b:C * k + 32 * b + 1], scale=-1.0)
-                    if par == 0 and n: signs(*mine[n - 1])
-            signs(*mine[-1])
+        def plane(k, b):
+            if k < 2:
+                w = [b in x for x in WORDS].index(True)
+                return T.wa, 4 * C * w, 2 * k + WORDS[w].index(b), "a%d" % w
+            w = [b in x for x in BWORDS].index(True)
+            return T.wb, 4 * C * (3 * k - 6 + w), BWORDS[w].index(b), "b%d" % (3 * k - 6 + w)
 
-        made = [0, 0]
+        def diff(k, b):
+            _, z, p, n = plane(k, b)
+            z += 20 * C * (k > 1)
+            bw = banks[k][1]
+            act(T.ds[:, z + p:z + 4 * C:4], ps(bw), F.Identity, ("ps%d" % bw, "tr%d" % k), "d%s.%d" % (n, p), bias=T.tr[:, C * k + 32 * b:C * k + 32 * b + 1], scale=-1.0)
 
-        def word(ty, w):
-            wt, qn, pb = side(ty)
-            qc, qs = T[qn], T[qn + "s"]
-            c = 5 if TIE in WORDS[ty][w] else 4
-            qz(qc[:, C * w:C * w + C], qs[:, C * w:C * w + C], wt[:, 4 * C * w:4 * C * w + 4 * C], [pl(ty, w, p) for p in range(4)], qn + "%d" % w)
-            mm(pb, C, *kk(c), qc[:, C * w:C * w + C], qs[:, C * w:C * w + C], (qn + "%d" % w, "kc%d" % c), made[ty] == 0, made[ty] == 4)
-            made[ty] += 1
+        def sign(k, b):
+            wt, z, p, n = plane(k, b)
+            d = 20 * C * (k > 1)
+            for lo, hi, c in ((0, 32 * b, 16), (32 * b, C, 13)):
+                if hi > lo:
+                    act(wt[:, z + 4 * lo + p:z + 4 * hi:4], T.ds[:, d + z + 4 * lo + p:d + z + 4 * hi:4], F.Sign, ("d%s.%d" % (n, p), "f13", "f16"),
+                        "w%s.%d" % (n, p), bias=col(c))
 
-        def block(ty, par, b):
-            wt = side(ty)[0]
-            k = 2 * ty + par
+        def chain(jobs):
+            calls = []
+            for i, j in enumerate(jobs):
+                calls.append((diff, j))
+                if i: calls.append((sign, jobs[i - 1]))
+            return calls + [(sign, jobs[-1])]
+
+        def run(calls, n):
+            for f, j in calls[:n]:
+                f(*j)
+            del calls[:n]
+
+        def block(k, b):
+            wt, z, p, n = plane(k, b)
             bv = banks[k][0]
-            rd, o = ("ps%d" % bv, "tr%d" % k), C * k
-            w, i = [(w, x.index(b)) for w, x in enumerate(WORDS[ty]) if b in x][0]
-            p = 2 * par + i
-            z = 4 * C * w + p
+            rd, wr, o = ("ps%d" % bv, "tr%d" % k), "w%s.%d" % (n, p), C * k
+            z += p
             if b == TIE:
-                tt(wt[:, z:4 * C * (w + 1):4], ps(bv), T.tr[:, o:o + C], A.not_equal, rd, pl(ty, w, p))
+                tt(wt[:, z:z - p + 4 * C:4], ps(bv), T.tr[:, o:o + C], A.not_equal, rd, wr)
                 return
             sc = T.tr[:, o + 32 * b:o + 32 * b + 1]
-            ts(wt[:, z:z + 128 * b - 3:4], ps(bv, 32 * b), sc, 2.0, A.is_lt, A.mult, rd, pl(ty, w, p))
-            ts(wt[:, z + 128 * b:4 * C * (w + 1):4], T.ps[:, 512 * bv + 32 * b:512 * bv + C], sc, 2.0, A.is_le, A.mult, rd, pl(ty, w, p))
+            ts(wt[:, z:z + 128 * b - 3:4], ps(bv, 32 * b), sc, 2.0, A.is_lt, A.mult, rd, wr)
+            ts(wt[:, z + 128 * b:z - p + 4 * C:4], T.ps[:, 512 * bv + 32 * b:512 * bv + C], sc, 2.0, A.is_le, A.mult, rd, wr)
 
-        rows(0)
-        for b in (TIE, 2, 3, 4, 5):
-            block(0, 0, b)
-        for b in (TIE, 2, 3, 4):
-            block(0, 1, b)
-        word(0, 0)
-        block(0, 1, 5)
-        word(0, 2)
-        rows(1)
-        word(0, 1)
-        word(0, 3)
-        block(1, 0, TIE)
-        block(1, 0, 2)
-        word(0, 4)
-        block(1, 0, 3)
-        block(1, 0, 4)
-        scan(T.dd[:], ps(5), T.k16[:], ("ps5", "k16"), D01)
-        block(1, 0, 5)
-        ts(T.aw[:], dv, B16 + PLUS, None, A.add, None, D01, "aw")
-        block(1, 1, TIE)
-        op("v", lambda: V.tensor_copy(T.of[:].indirect(T.aw[:]), T.ij[:]), ("ij", "aw"), "of")
-        block(1, 1, 2)
-        scan(T.kr[:], T.of[:], T.k16[:], ("of", "k16"), "kr")
-        block(1, 1, 3)
-        ts(T.ow[:], T.kr[:, 15:C:16], B16, None, A.add, None, "kr", "ow")
-        block(1, 1, 4)
-        word(1, 0)
-        block(1, 1, 5)
-        for w in (2, 3, 1, 4):
-            word(1, w)
-        if t == 0:
-            for i in (8, 9, 7):
-                kz(i)
-        ts(T.bs[:], ps(1), col(5), None, A.add, None, ("ps1", "f5"), "bs")
-        for h, (a, b) in enumerate(PARTS):
-            op("v", lambda: V.tensor_scalar(T.cd[:, 4 * a:4 * b:4], T.bs[:].indirect(T.ow[:, a // 16:b // 16]), -9.0, 9.0, A.max, A.min), ("bs", "ow"), "cd%d" % h)
-        for h, (a, b) in enumerate(PARTS):
-            qz(T.qc[:, a:b], T.qcs[:, a:b], T.cd[:, 4 * a:4 * b], ("cd%d" % h, "cdz"), "qc")
-        bb = (0, 2) * 4
+        made, held = [0, 0, 0], []
+
+        def word(ty, w):
+            wt, qn, pb, x, all_ = (T.wa, "qa", 5, WORDS[w], 5) if ty == 0 else (T.wb, "qb", (2, 6)[ty - 1], BWORDS[w], 3)
+            qc, qs = T[qn], T[qn + "s"]
+            c = (4 if ty == 0 else 16) + (TIE in x)
+            w += 3 * (ty == 2)
+            n = qn[1] + "%d" % w
+            qz(qc[:, C * w:C * w + C], qs[:, C * w:C * w + C], wt[:, 4 * C * w:4 * C * w + 4 * C], ["w%s.%d" % (n, p) for p in range(4)] + ["wbz"] * (ty > 0), "q" + n)
+            held.append((pb, C, *kk(c), qc[:, C * w:C * w + C], qs[:, C * w:C * w + C], ("q" + n, "kc%d" % c), made[ty] == 0, made[ty] == all_ - 1))
+            made[ty] += 1
+            if ty < 2: mm(*held.pop())
+
+        def steps(e, i):
+            o = C * e
+            if i == 0 and e == 0: ts(T.bs[:, 0:C], ps(2), col(5), None, A.add, None, ("ps2", "f5"), "bt0")
+            if i == 0 and e == 1: act(T.bs[:, C:2 * C], ps(6), F.Identity, ("ps6", "f9"), "bt1", bias=col(9))
+            if i in (1, 2):
+                a, b = PARTS[i - 1]
+                op("v", lambda: V.tensor_scalar(T.cd[:, 4 * (o + a):4 * (o + b):4], T.bs[:, o:o + C].indirect(T.ox[:, a // 16:b // 16]), -9.0, 9.0, A.max, A.min),
+                   ("bt%d" % e, "ox"), "cd%d.%d" % (e, i - 1))
+            if i in (3, 4):
+                a, b = PARTS[i - 3]
+                qz(T.qc[:, o + a:o + b], T.qcs[:, o + a:o + b], T.cd[:, 4 * (o + a):4 * (o + b)], ("cd%d.%d" % (e, i - 3), "cdz"), "qc%d." % e)
 
         def table(k):
-            mm(bb[k], C, *kk(8 + k), T.qc[:], T.qcs[:], ("qc", "kc%d" % (8 + k)))
+            o = C * (k // 4)
+            mm((0, 3)[k % 2], C, *kk(8 + k), T.qc[:, o:o + C], T.qcs[:, o:o + C], ("qc%d." % (k // 4), "kc%d" % (8 + k)))
 
         def keep(k):
-            if k: act(T.cw[:, C * k:C * k + C], ps(bb[k]), F.Copy, "ps%d" % bb[k], "cw%d" % k)
-            else: cp(T.cw[:, 0:C], ps(bb[0]), "ps%d" % bb[0], "cw0")
+            b = (0, 3)[k % 2]
+            act(T.cw[:, C * k:C * k + C], ps(b), F.Copy, "ps%d" % b, "cw%d" % k)
 
+        scan(T.dd[:], ps(4), T.k16[:], ("ps4", "k16"), D01)
+        tt(T.key0[:], ps(4), T.ij[:], A.subtract, ("ps4", "ij"), K3)
+        mask(0)
+        ts(T.nf[:], dv, -1.0 / 512, 287.0 - B16 / 512, A.mult, A.add, D01, ("nf0", "nf1"))
+        turn(0)
+        mask(1)
+        ts(T.ne[:], T.nf[:], col(4), None, A.mult, None, ("nf0", "nf1", "f4"), "ne")
+        block(0, TIE)
+        tt(T.nf[:], T.ne[:], T.nid[:], A.add, ("ne", "nid"), ("nf0", "nf1"))
+        turn(1)
+        run(chain([(k, b) for x in ((6, 0, 1), (7, 8)) for k in range(2) for b in x]), 99)
+        block(0, 2)
+        cp(T.nx[:], T.nf[:], ("nf0", "nf1"), "nx")
+        for b in (3, 4, 5):
+            block(0, b)
+        for b in (TIE, 2, 3, 4):
+            block(1, b)
+        word(0, 0)
+        block(1, 5)
+        word(0, 2)
+        mask(2)
+        word(0, 1)
+        turn(2)
+        word(0, 3)
+        run(chain([(2, b) for b in BSCAL[0]]), 99)
+        scores(3, 0)
+        for b in (TIE, 5, 3):
+            block(2, b)
+        word(0, 4)
+        scores(3, 1)
+        block(2, 4)
+        word(1, 2)
+        scan(T.dd[:], ps(5), T.k16[:], ("ps5", "k16"), D01)
+        mask(3)
+        ts(T.aw[:], dv, B16 + PLUS, None, A.add, None, D01, "aw")
+        turn(3)
+        op("v", lambda: V.tensor_copy(T.of[:].indirect(T.aw[:]), T.ij[:]), ("ij", "aw"), "of")
+        word(1, 0)
+        op("s", lambda: S.activation(T.nv[:], T.of[:].indirect(T.nx[:]), F.Copy), ("of", "nx"), "nv")
+        late = chain([(3, b) for b in BSCAL[1]])
+        run(late, 11)
+        block(3, TIE)
+        word(1, 1)
+        scan(T.kr[:], T.nv[:], T.k16[:], ("nv", "k16"), "kr")
+        block(3, 5)
+        ts(T.ox[:], T.kr[:, 15:C:16], B16, None, A.add, None, "kr", "ox")
+        steps(0, 0)
+        first(8)
+        for i in range(1, 5):
+            steps(0, i)
         table(0)
-        table(1)
-        keep(0)
-        keep(1)
+        word(2, 2)
+        first(7, 9)
         keys = ((T.key0, "key0"), (T.key1, "key1"))
 
         def grow(k, h):
             (x, xk), (y, yk) = keys[k % 2], keys[1 - k % 2]
-            a, b = PARTS[h]
+            a, b = GROWS[h]
+            if k == 0:
+                tt(y[:, a:b], T.ps[:, a:b], x[:, a:b], A.add, ("ps0", "%s.%d" % (xk, h)), "%s.%d" % (yk, h))
+                return
             op("v", lambda: V.tensor_tensor(y[:, a:b], T.cw[:, C * k:C * k + C].indirect(T.nl[:, a // 16:b // 16]), x[:, a:b], A.add),
-               ("cw%d" % k, "nl%d" % h, "%s.%d" % (xk, h)), "%s.%d" % (yk, h))
+               ("cw%d" % k, "nl%d" % min(h, 1), "%s.%d" % (xk, h)), "%s.%d" % (yk, h))
 
         def turns(h):
             a, b = PARTS[h]
             ts(T.nl[:, a // 16:b // 16], dv[:, a // 16:b // 16], B16 + 96, None, A.add, None, "%s%d" % (dn, h), "nl%d" % h)
 
-        fb = (3, 4, 6, 7)
+        def unpack(b):
+            mm((2, 7)[b % 2], C, *kk(b), lc[:], ls[:], ln + ("kc%d" % b,))
+            act(T.ff[:, C * b:C * b + C], ps((2, 7)[b % 2]), F.Copy, "ps%d" % (2, 7)[b % 2], "ff%d" % b)
+
+        def order(b):
+            op("s", lambda: S.activation(T.fs[:, C * b:C * b + C], T.ff[:, C * b:C * b + C].indirect(T.ow[:]), F.Copy), ("ff%d" % b, "ow"), "fs%d" % b)
+
+        def listed(i):
+            if i == 0: scan(T.kr[:], T.of[:], T.k16[:], ("of", "k16"), "kr")
+            if i == 1: ts(T.ow[:], T.kr[:, 15:C:16], B16, None, A.add, None, "kr", "ow")
+
+        def spread(k):
+            table(k)
+            keep(k)
+
         dn = "dd"
         zc, zs = T["zc%d" % t], T["zs%d" % t]
 
@@ -433,48 +493,53 @@ def rank_program(g, core, T, topo):
             a, b = PARTS[h]
             qz(zc[:, a:b], zs[:, a:b], zt[:, 4 * a:4 * b], ["zt%d.%d" % (i, h) for i in range(4)], "zc")
 
+        beside = {1: ([(spread, 1), (run, late, 99)], [(word, 2, 0)], [(listed, 0), (first, 10), (spread, 2)]),
+                  2: ([], [(word, 2, 1)], [(listed, 1), (first, 11), (spread, 3)]),
+                  3: ([(steps, 1, 0)], [(first, 12, 13)], [(steps, 1, 1), (steps, 1, 2)]),
+                  4: ([], [(steps, 1, 3), (steps, 1, 4), (spread, 4)], [(first, 0, 1), (spread, 5), (unpack, 0), (unpack, 1)]),
+                  5: ([(order, 0), (order, 1)], [(first, 2, 3)], [(first, 14), (spread, 6), (unpack, 2), (unpack, 3)]),
+                  6: ([(order, 2), (order, 3)], [(first, 15)], [(spread, 7)] * t),
+                  7: ([], [], [(tt, T.nr[:], T.ne[:], T.no[:], A.add, ("ne", "no", "no7"), "nr")])}
+
         for k in range(1, 8):
             kr, kn = keys[k % 2]
-            k0, k1 = kn + ".0", kn + ".1"
+            k0, k1, k2 = kn + ".0", kn + ".1", kn + ".2"
 
-            def pick(b, rd):
-                scan(T.col[:, 96 * b:96 * b + 96], kr[:, 96 * b:96 * b + 96], T.k96[:], rd + ("k96",), "col%d" % b)
+            def pick(b):
+                scan(T.col[:, 96 * b:96 * b + 96], kr[:, 96 * b:96 * b + 96], T.k96[:], ((k0,), (k0, k1), (k2,))[b] + ("k96",), "col%d" % b)
 
             def less(b, h):
                 a, e = PARTS[h]
                 o, i, sc = ct[:, 4 * a + b:4 * e:4], kr[:, a:e], T.col[:, 96 * b + 95:96 * b + 96]
-                rd, wr = ((k0, k1)[h], "col%d" % b), "ct%d.%d" % (b, h)
+                rd, wr = ((k0,), (k1, k2))[h] + ("col%d" % b,), "ct%d.%d" % (b, h)
                 if b == 1: ts(o, i, sc, None, A.is_lt, None, rd, wr)
                 else: act(o, i, F.Sign, rd, wr, bias=sc, scale=-1.0)
 
-            grow(k - 1, 0)
-            grow(k - 1, 1)
-            pick(0, (k0,))
-            pick(2, (k1,))
-            pick(1, (k0, k1))
-            for b, h in ((0, 0), (2, 0), (0, 1), (2, 1), (1, 0), (1, 1)):
-                less(b, h)
+            def fill(i):
+                for f in beside[k][i]:
+                    f[0](*f[1:])
+
+            for h in range(3):
+                grow(k - 1, h)
+            for b in range(3):
+                pick(b)
+            for b in range(3):
+                less(b, 0)
+                less(b, 1)
+            fill(0)
+            fill(1)
             for h, (a, b) in enumerate(PARTS):
                 qz(T.qt[:, a:b], T.qts[:, a:b], ct[:, 4 * a:4 * b], ["ct%d.%d" % (i, h) for i in range(3)] + ["ctz"], "qt%d" % h)
                 mm((5, 1)[h], b - a, *kk(7), T.qt[:, a:b], T.qts[:, a:b], ("qt%d" % h, "kc7"))
             dx, dn = ((T.dd, "dd"), (T.de, "de"))[k % 2]
             dv = dx[:, 15:C:16]
-            if t == 0 and k < 7:
-                kz(9 + k)
-                if k < 5: kz(k - 1)
-            if k == 7: tt(T.nr[:], T.ne[:], T.no[:], A.add, ("ne", "no", "no7"), "nr")
-            scan(dx[:, 0:H], ps(5, H), T.k16[:, 0:H], ("ps5", "k16"), dn + "0")
-            if k <= 6:
-                table(k + 1)
-                keep(k + 1)
-            if 2 <= k <= 5:
-                b = k - 2
-                mm(fb[b], C, *kk(b), lc[:], ls[:], ln + ("kc%d" % b,))
-                act(T.ff[:, C * b:C * b + C], ps(fb[b]), F.Copy, "ps%d" % fb[b], "ff%d" % b)
-            if 3 <= k <= 6:
-                b = k - 3
-                op("s", lambda: S.activation(T.fs[:, C * b:C * b + C], T.ff[:, C * b:C * b + C].indirect(T.ow[:]), F.Copy), ("ff%d" % b, "ow"), "fs%d" % b)
-            scan(dx[:, H:C], ps(1, C - H), T.k16[:, H:C], ("ps1", "k16"), dn + "1")
+            while held:
+                mm(*held.pop(0))
+            fill(2)
+            while held:
+                mm(*held.pop(0))
+            for h, (a, b) in enumerate(PARTS):
+                scan(dx[:, a:b], ps((5, 1)[h], b - a), T.k16[:, a:b], ("ps%d" % (5, 1)[h], "k16"), dn + "%d" % h)
             if k < 7:
                 turns(0)
                 turns(1)
@@ -532,9 +597,9 @@ def rank_program(g, core, T, topo):
             turns(0)
             turns(1)
             qz(T.vq[:], T.vs[:], T.vt[:], "vt", "vq")
-            grow(7, 0)
-            grow(7, 1)
-            tt(T.to[0:1, :], T.key0[0:1, :], T.ij[0:1, :], A.add, ("key0.0", "key0.1", "ij"), "to")
+            for h in range(3):
+                grow(7, h)
+            tt(T.to[0:1, :], T.key0[0:1, :], T.ij[0:1, :], A.add, K3 + ("ij",), "to")
             ts(T.to[0:1, :], T.to[0:1, :], 1.0 / 512, 1152.0, A.mult, A.add, "to", "to")
             ld("y", T.tot[:], T.to[0:1, :], "tot", "to")
         xt = T["xt%d" % (t + 1)]

@@ -7,12 +7,13 @@ GROWS = ((0, H), (H, 192), (192, C))
 KW = 512
 B16, B96 = 2.0 ** 18, 2.0 ** 21
 BIG, TINY = 1e29, 2.0 ** -119
-NK = 18
+NK = 19
 TIE = 9
 WORDS = ((2, 3), (4, 5), (6, TIE), (0, 1), (7, 8))
 BWORDS = ((0, 1, 2, 6), (7, 8, 3, 4), (5, TIE))
-SCAL, BSCAL = (6, 0, 1, 7, 8), ((0, 1, 2, 6, 7, 8), (0, 1, 2, 6, 7, 8, 3, 4))
-PLUS, BPLUS = 16.0 * 5 - 32.0, 16.0 * 6 - 32.0
+SCAL = ((0, 1, 6, 7, 8), (0, 1, 7, 8), (0, 1, 2, 6, 7, 8, 3), (0, 1, 2, 6, 7, 8, 3, 4))
+PLUS = [16.0 * len(x) - 32.0 for x in SCAL]
+RAW = (4, 1, 5, 3)
 
 MXC, PL = "float8_e4m3fn_x4", "uint8"
 SCRATCH = {}
@@ -31,19 +32,21 @@ for _t in range(2):
     for _n in ("l", "z", "q", "b"):
         _buf(_n + "c%d" % _t, C, MXC)
         _buf(_n + "s%d" % _t, C, PL)
+    _buf("aw%d" % _t, 18, "uint16")
+    _buf("al%d" % _t, 18, "uint16")
 for _n, _c, _d in (("wk", 1024, MXC), ("wp", 1024, PL), ("ut", 512, "bfloat16"), ("vt", 512, "bfloat16"), ("uq", 128, MXC), ("us", 128, PL),
-                   ("vq", 128, MXC), ("vs", 128, PL), ("up", 640, MXC), ("ups", 640, PL), ("kt", 6 * KW, "bfloat16"), ("sp", 2 * KW + 8, "bfloat16"),
+                   ("vq", 128, MXC), ("vs", 128, PL), ("up", 512, MXC), ("ups", 512, PL), ("kt", 7 * KW, "bfloat16"), ("sp", 2 * KW + 8, "bfloat16"),
                    ("un", KW + 4, "bfloat16"), ("kc", NK * 128, MXC), ("ks", NK * 128, PL), ("tm2", KW + 4, "bfloat16"), ("one", KW + 4, "bfloat16"),
-                   ("ui", 40, "int32"), ("ul", 40, "uint16"), ("pi", 2, "int32"), ("pj", 4, "int32"),
+                   ("ui", 32, "int32"), ("ul", 32, "uint16"), ("pi", 2, "int32"), ("pj", 4, "int32"),
                    ("fc", 20, "float32"), ("mk", 4, "float32"), ("ij", C, "float32"),
-                   ("rowog", 128, "float32"), ("hown", C, "float32"), ("hb", C, "float32"), ("k16", C, "float32"), ("k96", 96, "float32"),
+                   ("rowog", 128, "float32"), ("hb", C, "float32"), ("k16", C, "float32"), ("k96", 96, "float32"),
                    ("t1", 32, "float32"), ("t2", 128, "float32"), ("t3", 128, "float32"), ("t4", 128, "float32"), ("t5", 128, "float32"),
-                   ("wo", 4 * C, "bfloat16"), ("qo", C, MXC), ("qos", C, PL), ("om", C, "float32"),
-                   ("wa", 20 * C, "bfloat16"), ("wb", 24 * C, "bfloat16"), ("qa", 5 * C, MXC), ("qas", 5 * C, PL), ("qb", 6 * C, MXC),
-                   ("qbs", 6 * C, PL), ("rm", 4 * C, "float32"), ("tr", 4 * C, "float32"), ("ds", 44 * C, "float32"), ("dd", C, "float32"),
+                   ("wa", 20 * C, "bfloat16"), ("wb", 16 * C, "bfloat16"), ("qa", 5 * C, MXC), ("qas", 5 * C, PL), ("qb", 6 * C, MXC),
+                   ("qbs", 6 * C, PL), ("rm", 4 * C, "float32"), ("tr", 6 * C, "float32"), ("ds", 36 * C, "float32"), ("dd", C, "float32"),
                    ("de", C, "float32"), ("key0", C, "float32"), ("key1", C, "float32"), ("col", C, "float32"), ("nl", 18, "uint16"),
                    ("nf", 18, "float32"), ("ne", 18, "float32"), ("no", 18, "float32"), ("nr", 18, "float32"), ("nz", 18, "uint16"),
-                   ("nx", 18, "uint16"), ("ox", 18, "uint16"), ("nid", 18, "float32"), ("aw", 18, "uint16"), ("ow", 18, "uint16"), ("kw", 18, "uint16"), ("bs", 2 * C, "float32"), ("of", C, "float32"),
+                   ("nx", 18, "uint16"), ("ox", 18, "uint16"), ("nid", 18, "float32"),
+                   ("ow", 18, "uint16"), ("kw", 18, "uint16"), ("bs", 2 * C, "float32"), ("of", C, "float32"),
                    ("nv", C, "float32"), ("kr", C, "float32"), ("cd", 8 * C, "bfloat16"), ("qc", 2 * C, MXC), ("qcs", 2 * C, PL),
                    ("cw", 8 * C, "float32"),
                    ("ct", 4 * C, "bfloat16"), ("qt", C, MXC), ("qts", C, PL), ("ff", 4 * C, "bfloat16"), ("fs", 4 * C, "bfloat16"),
@@ -51,7 +54,7 @@ for _n, _c, _d in (("wk", 1024, MXC), ("wp", 1024, PL), ("ut", 512, "bfloat16"),
                    ("yo", C, "float32"), ("to", C, "float32")):
     _buf(_n, _c, _d)
 DMAS = ["d%d" % i for i in range(20)]
-SEMAPHORES = ["cv", "cs", "ct", "cg", "sent", "ax0", "ax1", "ay0", "ay1"] + DMAS
+SEMAPHORES = ["cv", "cs", "ct", "cg", "sent", "ax0", "ax1", "ay0", "ay1", "aa0", "aa1"] + DMAS
 
 
 def rank_program(g, core, T, topo):
@@ -61,7 +64,7 @@ def rank_program(g, core, T, topo):
     Q = {"g": g, "v": g.vector, "s": g.scalar, "t": g.tensor, "y": g.sync}
     clk = {k: {} for k in Q}
     cnt = {k: 0 for k in Q}
-    last, readers, ndma, sent = {}, {}, [0], [0]
+    last, readers, ndma, sent, due = {}, {}, [0], [0], {}
 
     def waits(q, toks):
         for s, v, c, _ in sorted(toks, key=lambda k: -len(k[2])):
@@ -113,8 +116,8 @@ def rank_program(g, core, T, topo):
     def cp(out, i, rd, wr):
         op("v", lambda: V.tensor_copy(out, i), rd, wr)
 
-    def ms(ap, c, wr):
-        op("v", lambda: V.memset(ap, c), (), wr)
+    def ms(ap, c, wr, rd=()):
+        op("v", lambda: V.memset(ap, c), rd, wr)
 
     def act(out, i, f, rd, wr, bias=0.0, scale=1.0):
         op("s", lambda: S.activation(out, i, f, bias=bias, scale=scale), rd, wr)
@@ -152,11 +155,12 @@ def rank_program(g, core, T, topo):
     def send(src, dst, sem, peer):
         waits("g", [last[k] for k in src])
         rid, pid = topo.addr(peer, core)
-        m = topo.mask(core, peer)
-        g.remote_dma(T[dst[0]][:].bitcast(dt.uint8), T[src[0]][:].bitcast(dt.uint8), T.sem[sem], T.sem.sent, pid, rid, m)
-        g.remote_dma(T[dst[1]][:], T[src[1]][:], T.sem[sem], T.sem.sent, pid, rid, m)
-        n = 2 * len(topo.engines(core, peer))
+        for a, b in zip(src, dst):
+            o, i = (T[k][:].bitcast(dt.uint8) if SCRATCH[k][2] == MXC else T[k][:] for k in (b, a))
+            g.remote_dma(o, i, T.sem[sem], T.sem.sent, pid, rid, topo.mask(core, peer))
+        n = len(src) * len(topo.engines(core, peer))
         sent[0] += n
+        due[sem] = n
         for k in dst:
             last[k] = (sem, n, {sem: n}, "r")
 
@@ -167,36 +171,47 @@ def rank_program(g, core, T, topo):
 
     iota(T.pi[:, 0:1], [[1, 1]], 0, 1, "pi", False)
     iota(T.ij[:], [[1, C]], 0, 0, "ij")
+    iota(T.rowog[:], [[1, 8], [0, 16]], 0, 0, "rowog")
     iota(T.ui[:, 0:16], [[16, 2], [32, 4], [0, 2]], 0, 0, "ui", False)
     iota(T.ui[:, 16:32], [[64, 2], [16, 4], [0, 2]], 1, 0, "ui", False)
-    iota(T.ui[:, 32:40], [[0, 8]], 0, 0, "ui", False)
-    iota(T.rowog[:], [[1, 8], [0, 16]], 0, 0, "rowog")
 
     def col(i):
         return T.fc[:, i:i + 1]
 
-    for i, x in ((13, TINY), (16, -TINY)):
-        ms(col(i), x, "f%d" % i)
+    firsts = ((6, 2, (256.0, 256.0)), (18, 6, (256.0, 512.0)))
+    ms(T.kt[:, 2 * KW:3 * KW], 0.0, "kz6")
     cp(col(0), T.pi[:, 0:1], "pi", "f0")
     for i, (o, k) in enumerate(((A.bitwise_and, 15), (A.bitwise_and, 31), (A.arith_shift_right, 5))):
         ts(T.pj[:, i:i + 1], T.pi[:, 0:1], k, None, o, None, "pi", "pj")
-    ts(col(10), col(0), -BIG, -0.5 * BIG, A.mult, A.add, "f0", "f10")
+    ms(T.kt[:, 6 * KW:7 * KW], 0.0, "kz18")
     cp(T.fc[:, 1:4], T.pj[:, 0:3], "pj", "f1")
-    for w, (lo, hi, val) in ((0, (0, 128, 512.0)), (1, (0, 128, 512.0)), (3, (0, 128, -512.0)), (2, (0, 96, 0.0)), (2, (96, 128, 512.0))):
-        ms(T.kt[lo:hi, 2 * KW + w:3 * KW:4], val, "kt6")
-    for e, (a, b) in zip((0, 128, 256), ((0, 128), (0, 128), (96, 128))):
-        act(T.hown[:, e:e + b - a], T.ij[:, a:b], F.Identity, ("ij", "f10"), "hown", bias=col(10), scale=BIG)
-    ts(T.t1[:, 0:17], T.ij[:, 0:17], col(1), B16, A.is_equal, A.mult, ("ij", "f1"), "t1")
-    for i, j, a, b in ((11, 3, -2.0, 0.0), (12, 3, -2.0, -1.0), (7, 2, BIG, -0.5 * BIG), (5, 1, -18.0, BPLUS - 9.0), (8, 3, -1.0, 0.0),
-                       (9, 1, -18.0, BPLUS + 23.0)):
+    for i, x in ((13, TINY), (16, -TINY)):
+        ms(col(i), x, "f%d" % i)
+    for k, e, ws in firsts[:1]:
+        for t, w in enumerate(ws):
+            ms(T.kt[0:32, e * KW + t:(e + 1) * KW:4], w, "kt%d" % k, "kz%d" % k)
+    for i, j, a, b in ((7, 2, BIG, -0.5 * BIG), (11, 3, -2.0, 0.0), (12, 3, -2.0, -1.0), (8, 3, -1.0, 0.0)):
         ts(col(i), col(j), a, b, A.mult, A.add, "f1", "f%d" % i)
+    ts(T.t1[:, 0:17], T.ij[:, 0:17], col(1), B16, A.is_equal, A.mult, ("ij", "f1"), "t1")
+    for k, e, ws in firsts[1:]:
+        for t, w in enumerate(ws):
+            ms(T.kt[0:32, e * KW + t:(e + 1) * KW:4], w, "kt%d" % k, "kz%d" % k)
+    for i, a in ((5, PLUS[2]), (9, PLUS[3])):
+        ts(col(i), col(1), -18.0, a - 9.0, A.mult, A.add, "f1", "f%d" % i)
     tt(T.k16[:, 0:16], T.t1[:, 0:16], T.t1[:, 1:17], A.subtract, "t1", "k16")
     cp(T.ul[:], T.ui[:], "ui", "ul")
-    ts(T.k16[:, 15:16], T.k16[:, 15:16], -2.0 * B16, None, A.add, None, "k16", "k16")
     for t, w in enumerate((0.5, 1.0, 0.5, 0.0)):
         ms(T.kt[0:96, 3 * KW + t:4 * KW:4], w, "kt7")
+    ts(T.k16[:, 15:16], T.k16[:, 15:16], -2.0 * B16, None, A.add, None, "k16", "k16")
     ms(T.kt[96:128, 3 * KW:4 * KW], 0.0, "kt7")
+    for m in range(2):
+        ts(T.mk[:, m:m + 1], col(2), 15.5, None, (A.is_lt, A.is_gt)[m], None, "f1", "mk")
+    ts(col(4), col(0), 15.5, None, A.is_lt, None, "f0", "f4")
+    ts(col(14), col(0), 15.5, None, A.is_gt, None, "f0", "f14")
     kz(6)
+    kz(18)
+    ts(col(15), T.mk[:, 1:2], PLUS[1] - PLUS[0], B16 + PLUS[0], A.mult, A.add, "mk", "f15")
+    ts(T.nid[:], T.ij[:, 0:C:16], col(1), col(14), A.add, A.mult, ("ij", "f1", "f14"), "nid")
     qz(T.uq[:], T.us[:], T.ut[:], "ut", ("uq", "us"))
 
     def upick(i, v):
@@ -205,35 +220,36 @@ def rank_program(g, core, T, topo):
         if v: op("v", lambda: V.tensor_copy(T.up[:, a:b].bitcast(dt.uint32), T.uq[:, 0:128].bitcast(dt.uint32).indirect(off)), ("uq", "ul"), "up%d" % i)
         else: op("s", lambda: S.activation(T.ups[:, a:b], T.us[:, 0:128].indirect(off), F.Copy), ("us", "ul"), "ups%d" % i)
 
-    upick(4, True)
-    qz(T.xc0[:], T.xs0[:], T.xt0[:], "xt0", ("xc0", "xs0"))
-    send(("xc0", "xs0"), ("lc0", "ls0"), "ax0", peers[0])
+    for e in range(0, C, 32):
+        act(T.hb[:, e:e + 32], T.ij[:, 0:32], F.Identity, ("ij", "f7"), "hb", bias=col(7), scale=-BIG)
     for x, n, c in ((T.t3, "t3", 11), (T.t4, "t4", 12)):
         act(x[:], T.rowog[:], F.Abs, ("rowog", "f%d" % c), n, bias=col(c))
     for e in (0, 64):
         act(T.t5[:, e:e + 64], T.rowog[:, 0:64], F.Abs, ("rowog", "f8"), "t5", bias=col(8))
-    for e in range(0, C, 32):
-        act(T.hb[:, e:e + 32], T.ij[:, 0:32], F.Identity, ("ij", "f7"), "hb", bias=col(7), scale=-BIG)
-    upick(4, False)
     grown = [16, 32, 64, 128, 256]
+
+    def weights(k, t, w, src, n):
+        e = k - 4 if k < 8 else k - 12
+        act(T.kt[:, e * KW + t:(e + 1) * KW:4], src[:], F.Relu, n, "kt%d" % k, bias=w, scale=-w)
+
+    def longer():
+        n = grown.pop(0)
+        m = min(n, C - n)
+        act(T.k16[:, n:n + m], T.k16[:, 0:m], F.Copy, "k16", "k16")
+
     for k in (4, 5):
         for t in range(4):
-            src, n = (T.t3, "t3") if t < 2 else (T.t4, "t4")
-            w = 1.0 if k == 5 and t % 2 else 0.5
-            act(T.kt[:, (k - 4) * KW + t:(k - 3) * KW:4], src[:], F.Relu, n, "kt%d" % k, bias=w, scale=-w)
-            if grown:
-                n = grown.pop(0)
-                m = min(n, C - n)
-                act(T.k16[:, n:n + m], T.k16[:, 0:m], F.Copy, "k16", "k16")
-    for i in range(4):
+            weights(k, t, 1.0 if k == 5 and t % 2 else 0.5, *((T.t3, "t3") if t < 2 else (T.t4, "t4")))
+            if t % 2: longer()
+    for i in range(2):
         upick(i, True)
         upick(i, False)
-    for k, ws in ((16, (0.5, 0.5, 0.5, 0.5)), (17, (0.5, 1.0, 0.0, 0.0))):
-        for t, w in enumerate(ws):
-            act(T.kt[:, (k - 12) * KW + t:(k - 11) * KW:4], T.t5[:], F.Relu, "t5", "kt%d" % k, bias=w, scale=-w)
-    for e in range(2):
-        for t in (2, 3):
-            iota(T.wb[:, (12 * e + 8) * C + t:(12 * e + 12) * C:4], [[0, C]], 0, 0, "wbz")
+    longer()
+    qz(T.xc0[:], T.xs0[:], T.xt0[:], "xt0", ("xc0", "xs0"))
+    send(("xc0", "xs0"), ("lc0", "ls0"), "ax0", peers[0])
+    for i in range(2, 4):
+        upick(i, True)
+        upick(i, False)
     iota(T.tm2[:], [[0, KW + 4]], 512, 0, "tm2")
 
     def groups(h):
@@ -242,33 +258,35 @@ def rank_program(g, core, T, topo):
         op("g", lambda: g.affine_select(w, w, [[0, 129], [16, 4]], A.is_ge, 0.0, 64 * h + 15, -1), "sp%d" % h, "sp%d" % h)
 
     groups(0)
-    for t in range(1, 4):
-        iota(T.cd[:, t:8 * C:4], [[0, 2 * C]], 0, 0, "cdz")
-    iota(T.ct[:, 3:4 * C:4], [[0, C]], 0, 0, "ctz")
-    groups(1)
-    iota(T.one[:], [[0, KW + 4]], 1, 0, "one")
-    op("g", lambda: g.affine_select(T.un[:], T.one[:], [[-1, KW + 4]], A.is_equal, 0.0, 3, 4), "one", "un")
-    for o, i, n in ((T.wk[:].bitcast(dt.uint8), T.wc[:], "wk"), (T.wp[:], T.ws[:], "wp"), (T.vt[:], T.v[:], "vt")):
-        ld("y", o, i, n, "lc0")
 
-    def late_constants():
-        for k in (4, 5):
-            kz(k)
-        ts(T.t2[:, 0:97], T.ij[:, 0:97], col(0), B96, A.is_equal, A.mult, ("ij", "f0"), "t2")
-        for m in range(2):
-            ts(T.mk[:, m:m + 1], col(2), 15.5, None, (A.is_lt, A.is_gt)[m], None, "f1", "mk")
-            ts(T.mk[:, m + 2:m + 3], col(2), 15.5, B16 + 96, (A.is_lt, A.is_gt)[m], A.mult, "f1", "mk2")
-        tt(T.k96[:], T.t2[:, 0:96], T.t2[:, 1:97], A.subtract, "t2", "k96")
-        ts(col(4), col(0), 15.5, None, A.is_lt, None, "f0", "f4")
-        ts(col(14), col(0), 15.5, None, A.is_gt, None, "f0", "f14")
-        ts(col(6), col(0), 111.5, B16 + 96, A.is_gt, A.mult, "f0", "f6")
-        ts(T.no[96:128, :], T.ij[96:128, 0:18], 0.0, T.mk[96:128, 3:4], A.mult, A.subtract, ("ij", "mk2"), "no7")
-        for k in (16, 17):
-            kz(k)
-        ts(T.nid[:], T.ij[:, 0:C:16], col(1), col(14), A.add, A.mult, ("ij", "f1", "f14"), "nid")
-        ts(T.k96[:, 95:96], T.k96[:, 95:96], -B96 - 0.5, None, A.add, None, "k96", "k96")
+    def late_constants(i):
+        if i == 0:
+            for k, ws in ((17, (0.5, 1.0, 0.0, 0.0)), (16, (0.5, 0.5, 0.5, 0.5))):
+                for t, w in enumerate(ws):
+                    weights(k, t, w, T.t5, "t5")
+        if i == 1:
+            ts(T.t2[:, 0:97], T.ij[:, 0:97], col(0), B96, A.is_equal, A.mult, ("ij", "f0"), "t2")
+            for m in range(2):
+                ts(T.mk[:, m + 2:m + 3], col(2), 15.5, B16 + 96, (A.is_lt, A.is_gt)[m], A.mult, "f1", "mk2")
+            ts(col(6), col(0), 111.5, B16 + 96, A.is_gt, A.mult, "f0", "f6")
+            tt(T.k96[:], T.t2[:, 0:96], T.t2[:, 1:97], A.subtract, "t2", "k96")
+        if i == 2:
+            ts(T.no[96:128, :], T.ij[96:128, 0:18], 0.0, T.mk[96:128, 3:4], A.mult, A.subtract, ("ij", "mk2"), "no7")
+            ts(T.k96[:, 95:96], T.k96[:, 95:96], -B96 - 0.5, None, A.add, None, "k96", "k96")
 
-    wo, ct, zt = T.wo, T.ct, T.zt
+    def last_constants():
+        for t in range(1, 4):
+            iota(T.cd[:, t:4 * C:4], [[0, C]], 0, 0, "cdz0")
+        iota(T.ct[:, 3:4 * C:4], [[0, C]], 0, 0, "ctz")
+        groups(1)
+        for t in range(1, 4):
+            iota(T.cd[:, 4 * C + t:8 * C:4], [[0, C]], 0, 0, "cdz1")
+        iota(T.one[:], [[0, KW + 4]], 1, 0, "one")
+        op("g", lambda: g.affine_select(T.un[:], T.one[:], [[-1, KW + 4]], A.is_equal, 0.0, 3, 4), "one", "un")
+        for o, i, n in ((T.wk[:].bitcast(dt.uint8), T.wc[:], "wk"), (T.wp[:], T.ws[:], "wp"), (T.vt[:], T.v[:], "vt")):
+            ld("y", o, i, n, "al0")
+
+    ct, zt = T.ct, T.zt
     D01 = ("dd0", "dd1")
     K3 = ("key0.0", "key0.1", "key0.2")
     for t in range(2):
@@ -278,34 +296,17 @@ def rank_program(g, core, T, topo):
         xn = ("xc%d" % t, "xs%d" % t)
         lc, ls = T["lc%d" % t], T["ls%d" % t]
         ln = ("lc%d" % t, "ls%d" % t)
+        aw, al = "aw%d" % t, "al%d" % t
 
         def first(*ks):
             for i in ks if t == 0 else ():
                 kz(i)
 
-        m0 = (0, 128, 160)
-        mm(3, C, T.up[:, 512:640], T.ups[:, 512:640], xc[:], xs[:], xn + ("up4", "ups4"))
-        for q in range(3):
-            mm(q, 128, xc[:, m0[q]:m0[q] + 128], xs[:, m0[q]:m0[q] + 128], T.uq[:], T.us[:], xn + ("uq", "us"))
-        tt(T.om[:], ps(3), T.hown[:], A.max, ("ps3", "hown"), "om")
-        for q in range(3):
-            sc = T.ps[:, 512 * q:512 * q + 1]
-            rq = ("ps3", "ps%d" % q)
-            e0, e1 = 128 * q, min(128 * q + 128, C)
-            if e0: ts(wo[:, q:4 * e0:4], ps(3, e0), sc, None, A.is_lt, None, rq, "wo")
-            ts(wo[:, 4 * e0 + q:4 * C:4], T.ps[:, 1536 + e0:1536 + C], sc, None, A.is_le, None, rq, "wo")
-            ts(wo[:, 4 * e0 + 3:4 * e1:4], T.om[:, e0:e1], sc, None, A.is_equal, None, ("om", rq[1]), "wo")
-        qz(T.qo[:], T.qos[:], wo[:], "wo", "qo")
-        mm(4, C, *kk(6), T.qo[:], T.qos[:], ("qo", "kc6"))
-        if t == 0:
-            late_constants()
         banks = ((5, 7), (6, 0), (1, 3), (4, 7))
 
         def scores(k, e):
-            mm(banks[k][e], C, T.up[:, 128 * k:128 * k + 128], T.ups[:, 128 * k:128 * k + 128], lc[:], ls[:], ln + ("up%d" % k, "ups%d" % k))
-
-        for k, e in ((0, 0), (1, 0), (0, 1), (1, 1), (2, 0), (2, 1)):
-            scores(k, e)
+            c, s, n = (xc, xs, xn) if k < 2 else (lc, ls, ln)
+            mm(banks[k][e], C, T.up[:, 128 * k:128 * k + 128], T.ups[:, 128 * k:128 * k + 128], c[:], s[:], n + ("up%d" % k, "ups%d" % k))
 
         def mask(k):
             tt(T.rm[:, C * k:C * k + C], ps(banks[k][0]), T.hb[:], A.max, ("ps%d" % banks[k][0], "hb"), "rm%d" % k)
@@ -318,13 +319,15 @@ def rank_program(g, core, T, topo):
                 w = [b in x for x in WORDS].index(True)
                 return T.wa, 4 * C * w, 2 * k + WORDS[w].index(b), "a%d" % w
             w = [b in x for x in BWORDS].index(True)
-            return T.wb, 4 * C * (3 * k - 6 + w), BWORDS[w].index(b), "b%d" % (3 * k - 6 + w)
+            if w == 2: return T.wa, 4 * C * (6 - 2 * k), BWORDS[w].index(b), "a%d" % (6 - 2 * k)
+            return T.wb, 4 * C * (2 * k - 4 + w), BWORDS[w].index(b), "b%d" % (2 * k - 4 + w)
 
         def diff(k, b):
             _, z, p, n = plane(k, b)
             z += 20 * C * (k > 1)
             bw = banks[k][1]
-            act(T.ds[:, z + p:z + 4 * C:4], ps(bw), F.Identity, ("ps%d" % bw, "tr%d" % k), "d%s.%d" % (n, p), bias=T.tr[:, C * k + 32 * b:C * k + 32 * b + 1], scale=-1.0)
+            act(T.ds[:, z + p:z + 4 * C:4], ps(bw), F.Identity, ("ps%d" % bw, "tr%d" % RAW[k]), "d%s.%d" % (n, p),
+                bias=T.tr[:, C * RAW[k] + 32 * b:C * RAW[k] + 32 * b + 1], scale=-1.0)
 
         def sign(k, b):
             wt, z, p, n = plane(k, b)
@@ -341,35 +344,39 @@ def rank_program(g, core, T, topo):
                 if i: calls.append((sign, jobs[i - 1]))
             return calls + [(sign, jobs[-1])]
 
-        def run(calls, n):
+        def run(calls, n=99):
             for f, j in calls[:n]:
                 f(*j)
             del calls[:n]
 
-        def block(k, b):
-            wt, z, p, n = plane(k, b)
-            bv = banks[k][0]
-            rd, wr, o = ("ps%d" % bv, "tr%d" % k), "w%s.%d" % (n, p), C * k
-            z += p
-            if b == TIE:
-                tt(wt[:, z:z - p + 4 * C:4], ps(bv), T.tr[:, o:o + C], A.not_equal, rd, wr)
-                return
-            sc = T.tr[:, o + 32 * b:o + 32 * b + 1]
-            ts(wt[:, z:z + 128 * b - 3:4], ps(bv, 32 * b), sc, 2.0, A.is_lt, A.mult, rd, wr)
-            ts(wt[:, z + 128 * b:z - p + 4 * C:4], T.ps[:, 512 * bv + 32 * b:512 * bv + C], sc, 2.0, A.is_le, A.mult, rd, wr)
+        def block(k, *bs):
+            for b in bs:
+                wt, z, p, n = plane(k, b)
+                bv = banks[k][0]
+                rd, wr, o = ("ps%d" % bv, "tr%d" % k), "w%s.%d" % (n, p), C * k
+                z += p
+                if b == TIE:
+                    tt(wt[:, z:z - p + 4 * C:4], ps(bv), T.tr[:, o:o + C], A.not_equal, rd, wr)
+                    continue
+                sc = T.tr[:, o + 32 * b:o + 32 * b + 1]
+                ts(wt[:, z:z + 128 * b - 3:4], ps(bv, 32 * b), sc, 2.0, A.is_lt, A.mult, rd, wr)
+                ts(wt[:, z + 128 * b:z - p + 4 * C:4], T.ps[:, 512 * bv + 32 * b:512 * bv + C], sc, 2.0, A.is_le, A.mult, rd, wr)
 
         made, held = [0, 0, 0], []
 
         def word(ty, w):
-            wt, qn, pb, x, all_ = (T.wa, "qa", 5, WORDS[w], 5) if ty == 0 else (T.wb, "qb", (2, 6)[ty - 1], BWORDS[w], 3)
-            qc, qs = T[qn], T[qn + "s"]
+            qn, pb, x, all_ = ("qa", 5, WORDS[w], 5) if ty == 0 else ("qb", (2, 6)[ty - 1], BWORDS[w], 3)
+            wt, z, _, n = plane(ty + 1 if ty else 0, x[0])
+            o = C * (w + 3 * (ty == 2))
+            qc, qs, qn = T[qn][:, o:o + C], T[qn + "s"][:, o:o + C], "%s%d" % (qn, o)
             c = (4 if ty == 0 else 16) + (TIE in x)
-            w += 3 * (ty == 2)
-            n = qn[1] + "%d" % w
-            qz(qc[:, C * w:C * w + C], qs[:, C * w:C * w + C], wt[:, 4 * C * w:4 * C * w + 4 * C], ["w%s.%d" % (n, p) for p in range(4)] + ["wbz"] * (ty > 0), "q" + n)
-            held.append((pb, C, *kk(c), qc[:, C * w:C * w + C], qs[:, C * w:C * w + C], ("q" + n, "kc%d" % c), made[ty] == 0, made[ty] == all_ - 1))
-            made[ty] += 1
+            qz(qc, qs, wt[:, z:z + 4 * C], ["w%s.%d" % (n, p) for p in range(4)], qn)
+            held.append((pb, C, *kk(c), qc, qs, (qn, "kc%d" % c), made[ty] == 0, made[ty] == all_ - 1))
             if ty < 2: mm(*held.pop())
+            if ty == 0:
+                c = 18 if TIE in x else 6
+                held.append((4, C, *kk(c), qc, qs, (qn, "kc%d" % c), made[0] == 0, made[0] == 4))
+            made[ty] += 1
 
         def steps(e, i):
             o = C * e
@@ -381,7 +388,7 @@ def rank_program(g, core, T, topo):
                    ("bt%d" % e, "ox"), "cd%d.%d" % (e, i - 1))
             if i in (3, 4):
                 a, b = PARTS[i - 3]
-                qz(T.qc[:, o + a:o + b], T.qcs[:, o + a:o + b], T.cd[:, 4 * (o + a):4 * (o + b)], ("cd%d.%d" % (e, i - 3), "cdz"), "qc%d." % e)
+                qz(T.qc[:, o + a:o + b], T.qcs[:, o + a:o + b], T.cd[:, 4 * (o + a):4 * (o + b)], ("cd%d.%d" % (e, i - 3), "cdz%d" % e), "qc%d." % e)
 
         def table(k):
             o = C * (k // 4)
@@ -391,53 +398,83 @@ def rank_program(g, core, T, topo):
             b = (0, 3)[k % 2]
             act(T.cw[:, C * k:C * k + C], ps(b), F.Copy, "ps%d" % b, "cw%d" % k)
 
-        scan(T.dd[:], ps(4), T.k16[:], ("ps4", "k16"), D01)
-        tt(T.key0[:], ps(4), T.ij[:], A.subtract, ("ps4", "ij"), K3)
+        def release():
+            while held:
+                mm(*held.pop(0))
+
+        def raw(k):
+            op("v", lambda: V.transpose(T.tr[:, C * RAW[k]:C * RAW[k] + C], ps(banks[k][0])), "ps%d" % banks[k][0], "tr%d" % RAW[k])
+
+        for k, e in ((0, 0), (0, 1), (1, 0), (1, 1)):
+            scores(k, e)
+        raw(0)
         mask(0)
-        ts(T.nf[:], dv, -1.0 / 512, 287.0 - B16 / 512, A.mult, A.add, D01, ("nf0", "nf1"))
-        turn(0)
         mask(1)
-        ts(T.ne[:], T.nf[:], col(4), None, A.mult, None, ("nf0", "nf1", "f4"), "ne")
-        block(0, TIE)
-        tt(T.nf[:], T.ne[:], T.nid[:], A.add, ("ne", "nid"), ("nf0", "nf1"))
+        turn(0)
         turn(1)
-        run(chain([(k, b) for x in ((6, 0, 1), (7, 8)) for k in range(2) for b in x]), 99)
-        block(0, 2)
-        cp(T.nx[:], T.nf[:], ("nf0", "nf1"), "nx")
-        for b in (3, 4, 5):
-            block(0, b)
-        for b in (TIE, 2, 3, 4):
-            block(1, b)
+        first(4)
+        run(chain([(0, 0), (0, 1), (0, 6), (1, 0), (1, 1), (0, 7), (0, 8), (1, 7), (1, 8)]))
+        if t == 0: late_constants(0)
+        block(0, TIE, 2, 3, 4, 5)
+        block(1, 2, 3)
+        block(1, TIE)
         word(0, 0)
-        block(1, 5)
-        word(0, 2)
-        mask(2)
-        word(0, 1)
-        turn(2)
+        block(1, 6)
         word(0, 3)
-        run(chain([(2, b) for b in BSCAL[0]]), 99)
-        scores(3, 0)
-        for b in (TIE, 5, 3):
-            block(2, b)
+        release()
+        first(5)
+        block(1, 4, 5)
+        if t:
+            scores(2, 0)
+            scores(2, 1)
+        word(0, 2)
+        word(0, 1)
         word(0, 4)
-        scores(3, 1)
-        block(2, 4)
-        word(1, 2)
+        if t == 0:
+            scores(2, 0)
+            scores(2, 1)
+            first(17, 16)
+        else:
+            raw(2)
+            mask(2)
+        release()
         scan(T.dd[:], ps(5), T.k16[:], ("ps5", "k16"), D01)
+        if t == 0: raw(2)
+        else: turn(2)
+        ts(T[aw][:], dv, col(15), None, A.add, None, D01 + ("f15",), aw)
+        send((aw,), (al,), "aa%d" % t, peer)
+        run(chain([(2, b) for b in SCAL[2]]))
+        ts(T.nf[:], dv, -1.0, 287.0 - B16 - PLUS[0], A.mult, A.add, D01, ("nf0", "nf1"))
+        if t == 0:
+            last_constants()
+            mask(2)
+        tt(T.key0[:], ps(4), T.ij[:], A.subtract, ("ps4", "ij"), K3)
+        scores(3, 0)
+        scores(3, 1)
+        ts(T.ne[:], T.nf[:], col(4), None, A.mult, None, ("nf0", "nf1", "f4"), "ne")
+        if t == 0:
+            turn(2)
+            late_constants(1)
+        block(2, TIE, 5)
+        tt(T.nf[:], T.ne[:], T.nid[:], A.add, ("ne", "nid"), ("nf0", "nf1"))
+        block(2, 4)
+        cp(T.nx[:], T.nf[:], ("nf0", "nf1"), "nx")
         mask(3)
-        ts(T.aw[:], dv, B16 + PLUS, None, A.add, None, D01, "aw")
-        turn(3)
-        op("v", lambda: V.tensor_copy(T.of[:].indirect(T.aw[:]), T.ij[:]), ("ij", "aw"), "of")
-        word(1, 0)
+        word(1, 2)
+        rest = [(turn, (3,)), (word, (1, 0)), (block, (3, TIE))]
+        run(rest, 3 if t else 1)
+        op("v", lambda: V.tensor_copy(T.of[:].indirect(T[al][:]), T.ij[:]), ("ij", al), "of")
+        run(rest)
+        late = chain([(3, b) for b in SCAL[3]])
+        run(late, 1)
         op("s", lambda: S.activation(T.nv[:], T.of[:].indirect(T.nx[:]), F.Copy), ("of", "nx"), "nv")
-        late = chain([(3, b) for b in BSCAL[1]])
         run(late, 11)
-        block(3, TIE)
         word(1, 1)
-        scan(T.kr[:], T.nv[:], T.k16[:], ("nv", "k16"), "kr")
         block(3, 5)
-        ts(T.ox[:], T.kr[:, 15:C:16], B16, None, A.add, None, "kr", "ox")
+        if t == 0: late_constants(2)
+        scan(T.kr[:], T.nv[:], T.k16[:], ("nv", "k16"), "kr")
         steps(0, 0)
+        ts(T.ox[:], T.kr[:, 15:C:16], B16, None, A.add, None, "kr", "ox")
         first(8)
         for i in range(1, 5):
             steps(0, i)
@@ -493,7 +530,7 @@ def rank_program(g, core, T, topo):
             a, b = PARTS[h]
             qz(zc[:, a:b], zs[:, a:b], zt[:, 4 * a:4 * b], ["zt%d.%d" % (i, h) for i in range(4)], "zc")
 
-        beside = {1: ([(spread, 1), (run, late, 99)], [(word, 2, 0)], [(listed, 0), (first, 10), (spread, 2)]),
+        beside = {1: ([(spread, 1), (run, late)], [(word, 2, 0)], [(listed, 0), (first, 10), (spread, 2)]),
                   2: ([], [(word, 2, 1)], [(listed, 1), (first, 11), (spread, 3)]),
                   3: ([(steps, 1, 0)], [(first, 12, 13)], [(steps, 1, 1), (steps, 1, 2)]),
                   4: ([], [(steps, 1, 3), (steps, 1, 4), (spread, 4)], [(first, 0, 1), (spread, 5), (unpack, 0), (unpack, 1)]),
@@ -533,11 +570,8 @@ def rank_program(g, core, T, topo):
                 mm((5, 1)[h], b - a, *kk(7), T.qt[:, a:b], T.qts[:, a:b], ("qt%d" % h, "kc7"))
             dx, dn = ((T.dd, "dd"), (T.de, "de"))[k % 2]
             dv = dx[:, 15:C:16]
-            while held:
-                mm(*held.pop(0))
+            release()
             fill(2)
-            while held:
-                mm(*held.pop(0))
             for h, (a, b) in enumerate(PARTS):
                 scan(dx[:, a:b], ps((5, 1)[h], b - a), T.k16[:, a:b], ("ps%d" % (5, 1)[h], "k16"), dn + "%d" % h)
             if k < 7:
@@ -574,7 +608,7 @@ def rank_program(g, core, T, topo):
 
         op("v", lambda: V.tensor_copy(T.nv[:].indirect(T.nz[:]), T.ij[:]), ("ij", "nz0", "nz1"), "nv")
         copy(0)
-        op("s", lambda: S.activation(T.kr[:], T.nv[:].indirect(T.aw[:]), F.Copy), ("nv", "aw"), "kr")
+        op("s", lambda: S.activation(T.kr[:], T.nv[:].indirect(T[al][:]), F.Copy), ("nv", al), "kr")
         largest(0)
         copy(1)
         scan(T.dd[:], T.kr[:], T.k16[:], ("kr", "k16"), D01)
@@ -600,7 +634,7 @@ def rank_program(g, core, T, topo):
             for h in range(3):
                 grow(7, h)
             tt(T.to[0:1, :], T.key0[0:1, :], T.ij[0:1, :], A.add, K3 + ("ij",), "to")
-            ts(T.to[0:1, :], T.to[0:1, :], 1.0 / 512, 1152.0, A.mult, A.add, "to", "to")
+            ts(T.to[0:1, :], T.to[0:1, :], 1.0 / 512, 1152.0 + PLUS[0], A.mult, A.add, "to", "to")
             ld("y", T.tot[:], T.to[0:1, :], "tot", "to")
         xt = T["xt%d" % (t + 1)]
         for b in range(4):
@@ -623,6 +657,5 @@ def rank_program(g, core, T, topo):
     for i in range(ndma[0]):
         g.wait_ge(T.sem[DMAS[i]], 16)
     g.wait_ge(T.sem.sent, sent[0])
-    for t in range(2):
-        for s in ("ax", "ay"):
-            g.wait_ge(T.sem[s + "%d" % t], 2 * len(topo.engines(core, peers[t])))
+    for s, n in due.items():
+        g.wait_ge(T.sem[s], n)

@@ -4,10 +4,12 @@ C = 288
 H = 128
 PARTS = ((0, H), (H, C))
 GROWS = ((0, H), (H, 192), (192, C))
+BACK = ((0, C - H), (C - H, C))
 KW = 512
 B16, B96 = 2.0 ** 18, 2.0 ** 21
+HIGH = 2.0 ** 22
 BIG, TINY = 1e29, 2.0 ** -119
-NK = 19
+NK = 18
 TIE = 9
 WORDS = ((2, 3), (4, 5), (6, TIE), (0, 1), (7, 8))
 BWORDS = ((0, 1, 2, 6), (7, 8, 3, 4), (5, TIE))
@@ -35,16 +37,16 @@ for _t in range(2):
     _buf("aw%d" % _t, 18, "uint16")
     _buf("al%d" % _t, 18, "uint16")
 for _n, _c, _d in (("wk", 1024, MXC), ("wp", 1024, PL), ("ut", 512, "bfloat16"), ("vt", 512, "bfloat16"), ("uq", 128, MXC), ("us", 128, PL),
-                   ("vq", 128, MXC), ("vs", 128, PL), ("up", 512, MXC), ("ups", 512, PL), ("kt", 7 * KW, "bfloat16"), ("sp", 2 * KW + 8, "bfloat16"),
+                   ("vq", 128, MXC), ("vs", 128, PL), ("up", 512, MXC), ("ups", 512, PL), ("kt", 6 * KW, "bfloat16"), ("sp", 2 * KW + 8, "bfloat16"),
                    ("un", KW + 4, "bfloat16"), ("kc", NK * 128, MXC), ("ks", NK * 128, PL), ("tm2", KW + 4, "bfloat16"), ("one", KW + 4, "bfloat16"),
                    ("ui", 32, "int32"), ("ul", 32, "uint16"), ("pi", 2, "int32"), ("pj", 4, "int32"),
-                   ("fc", 20, "float32"), ("mk", 4, "float32"), ("ij", C, "float32"),
-                   ("rowog", 128, "float32"), ("hb", C, "float32"), ("k16", C, "float32"), ("k96", 96, "float32"),
+                   ("fc", 24, "float32"), ("mk", 4, "float32"), ("ij", C, "float32"),
+                   ("rowog", 128, "float32"), ("hb", C, "float32"), ("k16", C, "float32"), ("k7", C, "float32"), ("k96", 96, "float32"),
                    ("t1", 32, "float32"), ("t2", 128, "float32"), ("t3", 128, "float32"), ("t4", 128, "float32"), ("t5", 128, "float32"),
                    ("wa", 20 * C, "bfloat16"), ("wb", 16 * C, "bfloat16"), ("qa", 5 * C, MXC), ("qas", 5 * C, PL), ("qb", 6 * C, MXC),
                    ("qbs", 6 * C, PL), ("rm", 4 * C, "float32"), ("tr", 6 * C, "float32"), ("ds", 36 * C, "float32"), ("dd", C, "float32"),
                    ("de", C, "float32"), ("key0", C, "float32"), ("key1", C, "float32"), ("col", C, "float32"), ("nl", 18, "uint16"),
-                   ("nf", 18, "float32"), ("ne", 18, "float32"), ("no", 18, "float32"), ("nr", 18, "float32"), ("nz", 18, "uint16"),
+                   ("nf", 18, "float32"), ("ne", 18, "float32"), ("no", 18, "float32"), ("nr", 20, "float32"), ("nz", 18, "uint16"),
                    ("nx", 18, "uint16"), ("ox", 18, "uint16"), ("nid", 18, "float32"),
                    ("ow", 18, "uint16"), ("kw", 18, "uint16"), ("bs", 2 * C, "float32"), ("of", C, "float32"),
                    ("nv", C, "float32"), ("kr", C, "float32"), ("cd", 8 * C, "bfloat16"), ("qc", 2 * C, MXC), ("qcs", 2 * C, PL),
@@ -54,7 +56,7 @@ for _n, _c, _d in (("wk", 1024, MXC), ("wp", 1024, PL), ("ut", 512, "bfloat16"),
                    ("yo", C, "float32"), ("to", C, "float32")):
     _buf(_n, _c, _d)
 DMAS = ["d%d" % i for i in range(20)]
-SEMAPHORES = ["cv", "cs", "ct", "cg", "sent", "ax0", "ax1", "ay0", "ay1", "aa0", "aa1"] + DMAS
+SEMAPHORES = ["cv", "cs", "ct", "cg", "sent", "ax0", "ax1", "ay00", "ay01", "ay10", "ay11", "aa0", "aa1"] + DMAS
 
 
 def rank_program(g, core, T, topo):
@@ -116,8 +118,8 @@ def rank_program(g, core, T, topo):
     def cp(out, i, rd, wr):
         op("v", lambda: V.tensor_copy(out, i), rd, wr)
 
-    def ms(ap, c, wr, rd=()):
-        op("v", lambda: V.memset(ap, c), rd, wr)
+    def ms(ap, c, wr):
+        op("v", lambda: V.memset(ap, c), (), wr)
 
     def act(out, i, f, rd, wr, bias=0.0, scale=1.0):
         op("s", lambda: S.activation(out, i, f, bias=bias, scale=scale), rd, wr)
@@ -149,20 +151,20 @@ def rank_program(g, core, T, topo):
             i, n = T.sp[:, (KW + 4) * h + e:(KW + 4) * h + e + KW], "sp%d" % h
         qz(*kk(k), i, n, "kc%d" % k)
 
-    def scan(out, i, k, rd, wr):
-        op("v", lambda: V.tensor_tensor_scan(out, i, k, -4.0 * B96, A.max, A.add), rd, wr)
+    def scan(out, i, k, rd, wr, first=-4.0 * B96):
+        op("v", lambda: V.tensor_tensor_scan(out, i, k, first, A.max, A.add), rd, wr)
 
-    def send(src, dst, sem, peer):
-        waits("g", [last[k] for k in src])
+    def send(src, dst, sem, peer, cols=slice(None), part=""):
+        waits("g", [last[k + part] for k in src])
         rid, pid = topo.addr(peer, core)
         for a, b in zip(src, dst):
-            o, i = (T[k][:].bitcast(dt.uint8) if SCRATCH[k][2] == MXC else T[k][:] for k in (b, a))
+            o, i = (T[k][:, cols].bitcast(dt.uint8) if SCRATCH[k][2] == MXC else T[k][:, cols] for k in (b, a))
             g.remote_dma(o, i, T.sem[sem], T.sem.sent, pid, rid, topo.mask(core, peer))
         n = len(src) * len(topo.engines(core, peer))
         sent[0] += n
         due[sem] = n
         for k in dst:
-            last[k] = (sem, n, {sem: n}, "r")
+            last[k + part] = (sem, n, {sem: n}, "r")
 
     peers = [T.cores[rank ^ (1 << t)] for t in range(2)]
 
@@ -178,39 +180,29 @@ def rank_program(g, core, T, topo):
     def col(i):
         return T.fc[:, i:i + 1]
 
-    firsts = ((6, 2, (256.0, 256.0)), (18, 6, (256.0, 512.0)))
-    ms(T.kt[:, 2 * KW:3 * KW], 0.0, "kz6")
-    cp(col(0), T.pi[:, 0:1], "pi", "f0")
-    for i, (o, k) in enumerate(((A.bitwise_and, 15), (A.bitwise_and, 31), (A.arith_shift_right, 5))):
-        ts(T.pj[:, i:i + 1], T.pi[:, 0:1], k, None, o, None, "pi", "pj")
-    ms(T.kt[:, 6 * KW:7 * KW], 0.0, "kz18")
-    cp(T.fc[:, 1:4], T.pj[:, 0:3], "pj", "f1")
     for i, x in ((13, TINY), (16, -TINY)):
         ms(col(i), x, "f%d" % i)
-    for k, e, ws in firsts[:1]:
-        for t, w in enumerate(ws):
-            ms(T.kt[0:32, e * KW + t:(e + 1) * KW:4], w, "kt%d" % k, "kz%d" % k)
+    ms(T.no[96:128, :], 0.0, "no7")
+    ms(T.nr[:, 0:1], 0.0, "nr0")
+    for i, (o, k) in enumerate(((A.bitwise_and, 15), (A.bitwise_and, 31), (A.arith_shift_right, 5))):
+        ts(T.pj[:, i:i + 1], T.pi[:, 0:1], k, None, o, None, "pi", "pj")
+    cp(col(0), T.pi[:, 0:1], "pi", "f0")
+    cp(T.fc[:, 1:4], T.pj[:, 0:3], "pj", "f1")
+    for t, w in enumerate((0.5, 1.0, 0.5, 0.0)):
+        ms(T.kt[0:96, 3 * KW + t:4 * KW:4], w, "kt7")
     for i, j, a, b in ((7, 2, BIG, -0.5 * BIG), (11, 3, -2.0, 0.0), (12, 3, -2.0, -1.0), (8, 3, -1.0, 0.0)):
         ts(col(i), col(j), a, b, A.mult, A.add, "f1", "f%d" % i)
     ts(T.t1[:, 0:17], T.ij[:, 0:17], col(1), B16, A.is_equal, A.mult, ("ij", "f1"), "t1")
-    for k, e, ws in firsts[1:]:
-        for t, w in enumerate(ws):
-            ms(T.kt[0:32, e * KW + t:(e + 1) * KW:4], w, "kt%d" % k, "kz%d" % k)
-    for i, a in ((5, PLUS[2]), (9, PLUS[3])):
-        ts(col(i), col(1), -18.0, a - 9.0, A.mult, A.add, "f1", "f%d" % i)
-    tt(T.k16[:, 0:16], T.t1[:, 0:16], T.t1[:, 1:17], A.subtract, "t1", "k16")
-    cp(T.ul[:], T.ui[:], "ui", "ul")
-    for t, w in enumerate((0.5, 1.0, 0.5, 0.0)):
-        ms(T.kt[0:96, 3 * KW + t:4 * KW:4], w, "kt7")
-    ts(T.k16[:, 15:16], T.k16[:, 15:16], -2.0 * B16, None, A.add, None, "k16", "k16")
-    ms(T.kt[96:128, 3 * KW:4 * KW], 0.0, "kt7")
     for m in range(2):
         ts(T.mk[:, m:m + 1], col(2), 15.5, None, (A.is_lt, A.is_gt)[m], None, "f1", "mk")
-    ts(col(4), col(0), 15.5, None, A.is_lt, None, "f0", "f4")
-    ts(col(14), col(0), 15.5, None, A.is_gt, None, "f0", "f14")
-    kz(6)
-    kz(18)
-    ts(col(15), T.mk[:, 1:2], PLUS[1] - PLUS[0], B16 + PLUS[0], A.mult, A.add, "mk", "f15")
+    for i, x, o in ((4, 15.5, A.is_lt), (14, 15.5, A.is_gt), (10, 111.5, A.is_gt)):
+        ts(col(i), col(0), x, None, o, None, "f0", "f%d" % i)
+    tt(T.k16[:, 0:16], T.t1[:, 0:16], T.t1[:, 1:17], A.subtract, "t1", "k16")
+    cp(T.ul[:], T.ui[:], "ui", "ul")
+    for i, a in ((5, PLUS[2]), (9, PLUS[3])):
+        ts(col(i), col(1), -18.0, a - 9.0, A.mult, A.add, "f1", "f%d" % i)
+    ts(col(15), T.mk[:, 1:2], 512.0 * (PLUS[1] - PLUS[0]), B16 + 512.0 * PLUS[0], A.mult, A.add, "mk", "f15")
+    ts(T.k16[:, 15:16], T.k16[:, 15:16], -2.0 * B16, None, A.add, None, "k16", "k16")
     ts(T.nid[:], T.ij[:, 0:C:16], col(1), col(14), A.add, A.mult, ("ij", "f1", "f14"), "nid")
     qz(T.uq[:], T.us[:], T.ut[:], "ut", ("uq", "us"))
 
@@ -237,19 +229,22 @@ def rank_program(g, core, T, topo):
         m = min(n, C - n)
         act(T.k16[:, n:n + m], T.k16[:, 0:m], F.Copy, "k16", "k16")
 
-    for k in (4, 5):
+    def places(k):
         for t in range(4):
-            weights(k, t, 1.0 if k == 5 and t % 2 else 0.5, *((T.t3, "t3") if t < 2 else (T.t4, "t4")))
+            weights(k, t, 512.0 if k == 5 and t % 2 else 256.0, *((T.t3, "t3") if t < 2 else (T.t4, "t4")))
             if t % 2: longer()
+
+    places(4)
     for i in range(2):
         upick(i, True)
         upick(i, False)
-    longer()
     qz(T.xc0[:], T.xs0[:], T.xt0[:], "xt0", ("xc0", "xs0"))
     send(("xc0", "xs0"), ("lc0", "ls0"), "ax0", peers[0])
+    places(5)
     for i in range(2, 4):
         upick(i, True)
         upick(i, False)
+    longer()
     iota(T.tm2[:], [[0, KW + 4]], 512, 0, "tm2")
 
     def groups(h):
@@ -265,14 +260,18 @@ def rank_program(g, core, T, topo):
                 for t, w in enumerate(ws):
                     weights(k, t, w, T.t5, "t5")
         if i == 1:
+            ms(T.kt[96:128, 3 * KW:4 * KW], 0.0, "kt7")
             ts(T.t2[:, 0:97], T.ij[:, 0:97], col(0), B96, A.is_equal, A.mult, ("ij", "f0"), "t2")
             for m in range(2):
                 ts(T.mk[:, m + 2:m + 3], col(2), 15.5, B16 + 96, (A.is_lt, A.is_gt)[m], A.mult, "f1", "mk2")
-            ts(col(6), col(0), 111.5, B16 + 96, A.is_gt, A.mult, "f0", "f6")
+            ts(col(6), col(10), HIGH + B16 + 96, -HIGH, A.mult, A.add, "f10", "f6")
             tt(T.k96[:], T.t2[:, 0:96], T.t2[:, 1:97], A.subtract, "t2", "k96")
         if i == 2:
-            ts(T.no[96:128, :], T.ij[96:128, 0:18], 0.0, T.mk[96:128, 3:4], A.mult, A.subtract, ("ij", "mk2"), "no7")
+            ts(col(17), col(10), -HIGH - 4.0 * B96, HIGH, A.mult, A.add, "f10", "f17")
             ts(T.k96[:, 95:96], T.k96[:, 95:96], -B96 - 0.5, None, A.add, None, "k96", "k96")
+        if i == 3:
+            act(T.k7[:], T.k16[:], F.Copy, ("k16", "f10"), "k7", scale=col(10))
+            act(col(18), T.k16[:, 15:16], F.Copy, ("k16", "f10"), "f18", scale=col(10))
 
     def last_constants():
         for t in range(1, 4):
@@ -296,13 +295,14 @@ def rank_program(g, core, T, topo):
         xn = ("xc%d" % t, "xs%d" % t)
         lc, ls = T["lc%d" % t], T["ls%d" % t]
         ln = ("lc%d" % t, "ls%d" % t)
+        plus = PLUS[t]
         aw, al = "aw%d" % t, "al%d" % t
 
         def first(*ks):
             for i in ks if t == 0 else ():
                 kz(i)
 
-        banks = ((5, 7), (6, 0), (1, 3), (4, 7))
+        banks = ((5, 7), (6, 0), (1, 3), (6, 7))
 
         def scores(k, e):
             c, s, n = (xc, xs, xn) if k < 2 else (lc, ls, ln)
@@ -313,6 +313,14 @@ def rank_program(g, core, T, topo):
 
         def turn(k):
             op("v", lambda: V.transpose(T.tr[:, C * k:C * k + C], T.rm[:, C * k:C * k + C]), "rm%d" % k, "tr%d" % k)
+
+        def raw(k):
+            op("v", lambda: V.transpose(T.tr[:, C * RAW[k]:C * RAW[k] + C], ps(banks[k][0])), "ps%d" % banks[k][0], "tr%d" % RAW[k])
+
+        def hide(k):
+            for a in range(0, 128, 32):
+                op("g", lambda: g.affine_select(T.tr[a:a + 32, C * k:C * k + C], T.tr[a:a + 32, C * RAW[k]:C * RAW[k] + C], [[0, 9], [-1, 32]], A.is_ge, BIG, 0, 1),
+                   "tr%d" % RAW[k], "tr%d" % k)
 
         def plane(k, b):
             if k < 2:
@@ -358,6 +366,7 @@ def rank_program(g, core, T, topo):
                 if b == TIE:
                     tt(wt[:, z:z - p + 4 * C:4], ps(bv), T.tr[:, o:o + C], A.not_equal, rd, wr)
                     continue
+                if t and k == 0: rd, o = (rd[0], "tr%d" % RAW[0]), C * RAW[0]
                 sc = T.tr[:, o + 32 * b:o + 32 * b + 1]
                 ts(wt[:, z:z + 128 * b - 3:4], ps(bv, 32 * b), sc, 2.0, A.is_lt, A.mult, rd, wr)
                 ts(wt[:, z + 128 * b:z - p + 4 * C:4], T.ps[:, 512 * bv + 32 * b:512 * bv + C], sc, 2.0, A.is_le, A.mult, rd, wr)
@@ -365,7 +374,7 @@ def rank_program(g, core, T, topo):
         made, held = [0, 0, 0], []
 
         def word(ty, w):
-            qn, pb, x, all_ = ("qa", 5, WORDS[w], 5) if ty == 0 else ("qb", (2, 6)[ty - 1], BWORDS[w], 3)
+            qn, pb, x, all_ = ("qa", 4, WORDS[w], 5) if ty == 0 else ("qb", (2, 4)[ty - 1], BWORDS[w], 3)
             wt, z, _, n = plane(ty + 1 if ty else 0, x[0])
             o = C * (w + 3 * (ty == 2))
             qc, qs, qn = T[qn][:, o:o + C], T[qn + "s"][:, o:o + C], "%s%d" % (qn, o)
@@ -373,113 +382,135 @@ def rank_program(g, core, T, topo):
             qz(qc, qs, wt[:, z:z + 4 * C], ["w%s.%d" % (n, p) for p in range(4)], qn)
             held.append((pb, C, *kk(c), qc, qs, (qn, "kc%d" % c), made[ty] == 0, made[ty] == all_ - 1))
             if ty < 2: mm(*held.pop())
-            if ty == 0:
-                c = 18 if TIE in x else 6
-                held.append((4, C, *kk(c), qc, qs, (qn, "kc%d" % c), made[0] == 0, made[0] == 4))
             made[ty] += 1
-
-        def steps(e, i):
-            o = C * e
-            if i == 0 and e == 0: ts(T.bs[:, 0:C], ps(2), col(5), None, A.add, None, ("ps2", "f5"), "bt0")
-            if i == 0 and e == 1: act(T.bs[:, C:2 * C], ps(6), F.Identity, ("ps6", "f9"), "bt1", bias=col(9))
-            if i in (1, 2):
-                a, b = PARTS[i - 1]
-                op("v", lambda: V.tensor_scalar(T.cd[:, 4 * (o + a):4 * (o + b):4], T.bs[:, o:o + C].indirect(T.ox[:, a // 16:b // 16]), -9.0, 9.0, A.max, A.min),
-                   ("bt%d" % e, "ox"), "cd%d.%d" % (e, i - 1))
-            if i in (3, 4):
-                a, b = PARTS[i - 3]
-                qz(T.qc[:, o + a:o + b], T.qcs[:, o + a:o + b], T.cd[:, 4 * (o + a):4 * (o + b)], ("cd%d.%d" % (e, i - 3), "cdz%d" % e), "qc%d." % e)
-
-        def table(k):
-            o = C * (k // 4)
-            mm((0, 3)[k % 2], C, *kk(8 + k), T.qc[:, o:o + C], T.qcs[:, o:o + C], ("qc%d." % (k // 4), "kc%d" % (8 + k)))
-
-        def keep(k):
-            b = (0, 3)[k % 2]
-            act(T.cw[:, C * k:C * k + C], ps(b), F.Copy, "ps%d" % b, "cw%d" % k)
 
         def release():
             while held:
                 mm(*held.pop(0))
 
-        def raw(k):
-            op("v", lambda: V.transpose(T.tr[:, C * RAW[k]:C * RAW[k] + C], ps(banks[k][0])), "ps%d" % banks[k][0], "tr%d" % RAW[k])
+        def steps(e, i):
+            o = C * e
+            if i == 0 and e == 0: ts(T.bs[:, 0:C], ps(2), col(5), None, A.add, None, ("ps2", "f5"), "bt0")
+            if i == 0 and e == 1: act(T.bs[:, C:2 * C], ps(4), F.Identity, ("ps4", "f9"), "bt1", bias=col(9))
+            if i in (1, 2):
+                a, b = PARTS[i - 1]
+                op("v", lambda: V.tensor_scalar(T.cd[:, 4 * (o + a):4 * (o + b):4], T.bs[:, o:o + C].indirect(T.ox[:, a // 16:b // 16]), -9.0, 9.0, A.max, A.min),
+                   ("bt%d" % e, "ox%d" % (i - 1)), "cd%d.%d" % (e, i - 1))
+            if i in (3, 4):
+                a, b = PARTS[i - 3]
+                qz(T.qc[:, o + a:o + b], T.qcs[:, o + a:o + b], T.cd[:, 4 * (o + a):4 * (o + b)], ("cd%d.%d" % (e, i - 3), "cdz%d" % e), "qc%d.%d" % (e, i - 3))
+
+        def table(k):
+            o = C * (k // 4)
+            mm((0, 3)[k % 2], C, *kk(8 + k), T.qc[:, o:o + C], T.qcs[:, o:o + C], ("qc%d.0" % (k // 4), "qc%d.1" % (k // 4), "kc%d" % (8 + k)))
+
+        def keep(k):
+            b = (0, 3)[k % 2]
+            act(T.cw[:, C * k:C * k + C], ps(b), F.Copy, "ps%d" % b, "cw%d" % k)
+
+        def picked(i, h):
+            a, e = PARTS[h]
+            if i == 0: op("s", lambda: S.activation(T.nv[:, a:e], T.of[:].indirect(T.nx[:, a // 16:e // 16]), F.Copy), ("of", "nx"), ("nv%d" % h, "nv"))
+            if i == 1: scan(T.kr[:, a:e], T.nv[:, a:e], T.k16[:, a:e], ("nv%d" % h, "k16"), ("kr%d" % h, "kr"))
+            if i == 2: ts(T.ox[:, a // 16:e // 16], T.kr[:, a + 15:e:16], B16, None, A.add, None, "kr%d" % h, "ox%d" % h)
+
+        def gains(h):
+            a, e = PARTS[h]
+            mm((0, 4)[h], e - a, *kk(8), T.qc[:, a:e], T.qcs[:, a:e], ("qc0.%d" % h, "kc8"))
 
         for k, e in ((0, 0), (0, 1), (1, 0), (1, 1)):
             scores(k, e)
         raw(0)
-        mask(0)
-        mask(1)
-        turn(0)
-        turn(1)
-        first(4)
-        run(chain([(0, 0), (0, 1), (0, 6), (1, 0), (1, 1), (0, 7), (0, 8), (1, 7), (1, 8)]))
-        if t == 0: late_constants(0)
-        block(0, TIE, 2, 3, 4, 5)
+        if t == 0:
+            mask(0)
+            mask(1)
+            turn(0)
+            turn(1)
+            kz(4)
+            run(chain([(0, 0), (0, 1), (0, 6), (1, 0), (1, 1), (0, 7), (0, 8), (1, 7), (1, 8)]))
+            late_constants(0)
+            block(0, TIE, 2, 3, 4, 5)
+        else:
+            hide(0)
+            mask(1)
+            block(0, 2)
+            turn(1)
+            run(chain([(0, 0), (0, 1), (0, 7), (1, 0), (1, 1), (0, 8), (1, 7), (1, 8)]))
+            block(0, 3, 4, 5, 6)
         block(1, 2, 3)
         block(1, TIE)
         word(0, 0)
         block(1, 6)
+        if t: block(1, 4)
         word(0, 3)
-        release()
         first(5)
-        block(1, 4, 5)
         if t:
             scores(2, 0)
             scores(2, 1)
+            block(0, TIE)
+            block(1, 5)
+        else: block(1, 4, 5)
         word(0, 2)
         word(0, 1)
         word(0, 4)
         if t == 0:
             scores(2, 0)
             scores(2, 1)
-            first(17, 16)
+            late_constants(1)
         else:
             raw(2)
             mask(2)
-        release()
-        scan(T.dd[:], ps(5), T.k16[:], ("ps5", "k16"), D01)
+        scores(3, 0)
+        scores(3, 1)
+        scan(T.dd[:], ps(4), T.k16[:], ("ps4", "k16"), D01)
         if t == 0: raw(2)
         else: turn(2)
-        ts(T[aw][:], dv, col(15), None, A.add, None, D01 + ("f15",), aw)
+        ts(T[aw][:], dv, B16 + 512.0 * plus if t else col(15), 1.0 / 512, A.add, A.mult, D01 + ("f15",), aw)
         send((aw,), (al,), "aa%d" % t, peer)
+        tt(T.to[0:1, :], T.ps[0:1, 4 * 512:4 * 512 + C], T.ij[0:1, :], A.subtract, ("ps4", "ij"), "to")
+        op("g", lambda: g.partition_broadcast(T.key0[:], T.to[0:1, :], 128), "to", K3)
         run(chain([(2, b) for b in SCAL[2]]))
-        ts(T.nf[:], dv, -1.0, 287.0 - B16 - PLUS[0], A.mult, A.add, D01, ("nf0", "nf1"))
+        ts(T.nf[:], dv, -1.0 / 512, 287.0 - B16 / 512 - plus, A.mult, A.add, D01, "nf")
         if t == 0:
             last_constants()
             mask(2)
-        tt(T.key0[:], ps(4), T.ij[:], A.subtract, ("ps4", "ij"), K3)
-        scores(3, 0)
-        scores(3, 1)
-        ts(T.ne[:], T.nf[:], col(4), None, A.mult, None, ("nf0", "nf1", "f4"), "ne")
-        if t == 0:
+            first(17, 16)
             turn(2)
-            late_constants(1)
-        block(2, TIE, 5)
-        tt(T.nf[:], T.ne[:], T.nid[:], A.add, ("ne", "nid"), ("nf0", "nf1"))
-        block(2, 4)
-        cp(T.nx[:], T.nf[:], ("nf0", "nf1"), "nx")
+        else: block(2, TIE)
+        ts(T.ne[:], T.nf[:], col(4), None, A.mult, None, ("nf", "f4"), "ne")
         mask(3)
+        tt(T.nf[:], T.ne[:], T.nid[:], A.add, ("ne", "nid"), "nf")
+        if t == 0: block(2, TIE)
+        block(2, 5)
+        cp(T.nx[:], T.nf[:], "nf", "nx")
+        turn(3)
+        block(2, 4)
         word(1, 2)
-        rest = [(turn, (3,)), (word, (1, 0)), (block, (3, TIE))]
-        run(rest, 3 if t else 1)
+        word(1, 0)
+        block(3, TIE)
+        if t: block(3, 5)
         op("v", lambda: V.tensor_copy(T.of[:].indirect(T[al][:]), T.ij[:]), ("ij", al), "of")
-        run(rest)
         late = chain([(3, b) for b in SCAL[3]])
-        run(late, 1)
-        op("s", lambda: S.activation(T.nv[:], T.of[:].indirect(T.nx[:]), F.Copy), ("of", "nx"), "nv")
-        run(late, 11)
+        run(late, 3 if t else 1)
+        picked(0, 0)
+        picked(0, 1)
+        run(late, 9 if t else 10)
         word(1, 1)
-        block(3, 5)
-        if t == 0: late_constants(2)
-        scan(T.kr[:], T.nv[:], T.k16[:], ("nv", "k16"), "kr")
-        steps(0, 0)
-        ts(T.ox[:], T.kr[:, 15:C:16], B16, None, A.add, None, "kr", "ox")
+        if t: word(2, 2)
         first(8)
-        for i in range(1, 5):
-            steps(0, i)
-        table(0)
-        word(2, 2)
+        picked(1, 0)
+        if t == 0: late_constants(2)
+        picked(1, 1)
+        picked(2, 0)
+        steps(0, 0)
+        picked(2, 1)
+        steps(0, 1)
+        steps(0, 2)
+        steps(0, 3)
+        gains(0)
+        steps(0, 4)
+        gains(1)
+        if t == 0: block(3, 5)
         first(7, 9)
         keys = ((T.key0, "key0"), (T.key1, "key1"))
 
@@ -487,10 +518,12 @@ def rank_program(g, core, T, topo):
             (x, xk), (y, yk) = keys[k % 2], keys[1 - k % 2]
             a, b = GROWS[h]
             if k == 0:
-                tt(y[:, a:b], T.ps[:, a:b], x[:, a:b], A.add, ("ps0", "%s.%d" % (xk, h)), "%s.%d" % (yk, h))
+                bank, o = (4, 4 * 512 - H) if h else (0, 0)
+                tt(y[:, a:b], T.ps[:, o + a:o + b], x[:, a:b], A.add, ("ps%d" % bank, "%s.%d" % (xk, h)), "%s.%d" % (yk, h))
                 return
-            op("v", lambda: V.tensor_tensor(y[:, a:b], T.cw[:, C * k:C * k + C].indirect(T.nl[:, a // 16:b // 16]), x[:, a:b], A.add),
-               ("cw%d" % k, "nl%d" % min(h, 1), "%s.%d" % (xk, h)), "%s.%d" % (yk, h))
+            l, n = (T.nl, "nl") if k < 7 else (T.nz, "nz")
+            op("v", lambda: V.tensor_tensor(y[:, a:b], T.cw[:, C * k:C * k + C].indirect(l[:, a // 16:b // 16]), x[:, a:b], A.add),
+               ("cw%d" % k, n + "%d" % min(h, 1), "%s.%d" % (xk, h)), "%s.%d" % (yk, h))
 
         def turns(h):
             a, b = PARTS[h]
@@ -504,20 +537,22 @@ def rank_program(g, core, T, topo):
             op("s", lambda: S.activation(T.fs[:, C * b:C * b + C], T.ff[:, C * b:C * b + C].indirect(T.ow[:]), F.Copy), ("ff%d" % b, "ow"), "fs%d" % b)
 
         def listed(i):
-            if i == 0: scan(T.kr[:], T.of[:], T.k16[:], ("of", "k16"), "kr")
+            if i == 0: scan(T.kr[:], T.of[:], T.k16[:], ("of", "k16"), ("kr", "kr0", "kr1"))
             if i == 1: ts(T.ow[:], T.kr[:, 15:C:16], B16, None, A.add, None, "kr", "ow")
 
         def spread(k):
             table(k)
             keep(k)
 
+        def earlier(i):
+            if i == 0: tt(T.nr[:, 1:19], T.ne[:], T.no[:], A.add, ("ne", "no", "no7"), "nr")
+            if i == 1: tt(T.nf[:], T.nr[:, 1:19], T.nr[:, 0:18], A.subtract, ("nr", "nr0"), "nf")
+            if i == 2:
+                ts(T.k7[:, 15:C:16], T.nf[:], col(18), None, A.add, None, ("nf", "f18"), "k7")
+                ts(col(19), T.nr[:, H // 16:H // 16 + 1], col(17), None, A.add, None, ("nr", "f17"), "f19")
+
         dn = "dd"
         zc, zs = T["zc%d" % t], T["zs%d" % t]
-
-        def z_list(h, i):
-            s = slice(PARTS[h][0] // 16, PARTS[h][1] // 16)
-            if i == 0: tt(T.nf[:, s], dv[:, s], T.nr[:, s], A.max, (dn + "%d" % h, "nr"), "nf%d" % h)
-            if i == 1: ts(T.nz[:, s], T.nf[:, s], col(6), None, A.add, None, ("nf%d" % h, "f6"), "nz%d" % h)
 
         def z_part(b, h, v):
             a, e = PARTS[h]
@@ -530,13 +565,20 @@ def rank_program(g, core, T, topo):
             a, b = PARTS[h]
             qz(zc[:, a:b], zs[:, a:b], zt[:, 4 * a:4 * b], ["zt%d.%d" % (i, h) for i in range(4)], "zc")
 
-        beside = {1: ([(spread, 1), (run, late)], [(word, 2, 0)], [(listed, 0), (first, 10), (spread, 2)]),
-                  2: ([], [(word, 2, 1)], [(listed, 1), (first, 11), (spread, 3)]),
-                  3: ([(steps, 1, 0)], [(first, 12, 13)], [(steps, 1, 1), (steps, 1, 2)]),
-                  4: ([], [(steps, 1, 3), (steps, 1, 4), (spread, 4)], [(first, 0, 1), (spread, 5), (unpack, 0), (unpack, 1)]),
-                  5: ([(order, 0), (order, 1)], [(first, 2, 3)], [(first, 14), (spread, 6), (unpack, 2), (unpack, 3)]),
-                  6: ([(order, 2), (order, 3)], [(first, 15)], [(spread, 7)] * t),
-                  7: ([], [], [(tt, T.nr[:], T.ne[:], T.no[:], A.add, ("ne", "no", "no7"), "nr")])}
+        beside = {1: ([(spread, 1), (run, late)], [(word, 2, 0)], [(word, 2, 2)] * (1 - t) + [(first, 10), (spread, 2)]),
+                  2: ([], [(word, 2, 1)], [(first, 11, 12), (spread, 3), (steps, 1, 0)]),
+                  3: ([(late_constants, 3)], [(steps, 1, 1)], [(steps, 1, 2)]),
+                  4: ([], [(steps, 1, 3), (steps, 1, 4), (spread, 4)], [(first, 13, 0), (spread, 5), (unpack, 0)]),
+                  5: ([], [(listed, 0)], [(listed, 1), (first, 14, 1), (spread, 6), (unpack, 1)]),
+                  6: ([(order, 0), (order, 1)], [(first, 2, 3)], [(unpack, 2), (unpack, 3)]),
+                  7: ([(order, 2), (order, 3)], [(earlier, 1)], [(earlier, 2)])}
+        if t:
+            beside.update({2: ([], [(word, 2, 1)], [(listed, 0), (spread, 3), (steps, 1, 0)]),
+                           3: ([(unpack, 0), (unpack, 1)], [(steps, 1, 1)], [(listed, 1), (steps, 1, 2)]),
+                           4: ([(order, 0)], [(steps, 1, 3), (steps, 1, 4), (spread, 4)], [(spread, 5), (unpack, 2)]),
+                           5: ([(order, 1), (order, 2)], [], [(spread, 6), (unpack, 3)]),
+                           6: ([(order, 3)], [], [(spread, 7)]),
+                           7: ([], [(earlier, 1)], [(earlier, 2)])})
 
         for k in range(1, 8):
             kr, kn = keys[k % 2]
@@ -560,11 +602,14 @@ def rank_program(g, core, T, topo):
                 grow(k - 1, h)
             for b in range(3):
                 pick(b)
-            for b in range(3):
+            if k == 7: earlier(0)
+            for b in (0, 2):
                 less(b, 0)
                 less(b, 1)
             fill(0)
             fill(1)
+            less(1, 0)
+            less(1, 1)
             for h, (a, b) in enumerate(PARTS):
                 qz(T.qt[:, a:b], T.qts[:, a:b], ct[:, 4 * a:4 * b], ["ct%d.%d" % (i, h) for i in range(3)] + ["ctz"], "qt%d" % h)
                 mm((5, 1)[h], b - a, *kk(7), T.qt[:, a:b], T.qts[:, a:b], ("qt%d" % h, "kc7"))
@@ -572,8 +617,11 @@ def rank_program(g, core, T, topo):
             dv = dx[:, 15:C:16]
             release()
             fill(2)
+            release()
             for h, (a, b) in enumerate(PARTS):
-                scan(dx[:, a:b], ps((5, 1)[h], b - a), T.k16[:, a:b], ("ps%d" % (5, 1)[h], "k16"), dn + "%d" % h)
+                rd, wr = ("ps%d" % (5, 1)[h],), dn + "%d" % h
+                if k < 7: scan(dx[:, a:b], ps((5, 1)[h], b - a), T.k16[:, a:b], rd + ("k16",), wr)
+                else: scan(dx[:, a:b], ps((5, 1)[h], b - a), T.k7[:, a:b], rd + ("k7", "f17", "f19"), wr, col((17, 19)[h]))
             if k < 7:
                 turns(0)
                 turns(1)
@@ -581,9 +629,8 @@ def rank_program(g, core, T, topo):
                 p1 = p0 + 32
                 nb, nn = ((T.ne, "ne"), (T.no, "no"))[m]
                 act(nb[p0:p1, :], dv[p0:p1, :], F.Identity, (dn + "0", dn + "1", "mk", "mk2"), nn, bias=T.mk[p0:p1, 2 + m:3 + m], scale=T.mk[p0:p1, m:m + 1])
-        for i in range(2):
-            z_list(0, i)
-            z_list(1, i)
+        for h, (a, b) in enumerate(PARTS):
+            ts(T.nz[:, a // 16:b // 16], dv[:, a // 16:b // 16], col(6), None, A.add, None, (dn + "%d" % h, "f6"), "nz%d" % h)
         for h in range(2):
             for b in range(4):
                 z_part(b, h, b < 2)
@@ -600,13 +647,21 @@ def rank_program(g, core, T, topo):
         def largest(b):
             tt(T.ym[:, C * b:C * b + C], ps(2 * b + 1), T.y1[:, C * b:C * b + C], A.max, ("ps%d" % (2 * b + 1), "y1%d" % b), "ym%d" % b)
 
-        def put(b, v):
-            o, i = T.yt[:, b:4 * C:4], T.ym[:, C * b:C * b + C].indirect(T.kw[:])
-            rd, wr = ("ym%d" % b, "kw"), "yt%d" % b
+        qn, bn = ("qc%d" % t, "qs%d" % t), ("bc%d" % t, "bs%d" % t)
+
+        def put(b, h, v):
+            a, e = BACK[h]
+            o, i = T.yt[:, 4 * a + b:4 * e:4], T.ym[:, C * b:C * b + C].indirect(T.kw[:, a // 16:e // 16])
+            rd, wr = ("ym%d" % b, "kw"), "yt%d.%d" % (b, h)
             if v: op("v", lambda: V.tensor_scalar(o, i, 0.03125, None, A.mult), rd, wr)
             else: op("s", lambda: S.activation(o, i, F.Copy, scale=0.03125), rd, wr)
 
-        op("v", lambda: V.tensor_copy(T.nv[:].indirect(T.nz[:]), T.ij[:]), ("ij", "nz0", "nz1"), "nv")
+        def y_codes(h):
+            a, e = BACK[h]
+            qz(T[qn[0]][:, a:e], T[qn[1]][:, a:e], T.yt[:, 4 * a:4 * e], ["yt%d.%d" % (b, h) for b in range(4)], [k + "/%d" % h for k in qn])
+            send(qn, bn, "ay%d%d" % (t, h), peer, slice(a, e), "/%d" % h)
+
+        op("v", lambda: V.tensor_copy(T.nv[:].indirect(T.nz[:]), T.ij[:]), ("ij", "nz0", "nz1"), ("nv", "nv0", "nv1"))
         copy(0)
         op("s", lambda: S.activation(T.kr[:], T.nv[:].indirect(T[al][:]), F.Copy), ("nv", al), "kr")
         largest(0)
@@ -617,41 +672,60 @@ def rank_program(g, core, T, topo):
         largest(1)
         ts(T.kw[:], T.dd[:, 15:C:16], B16, None, A.add, None, D01, "kw")
         largest(2)
-        put(0, False)
+        put(0, 0, False)
+        put(1, 0, False)
         largest(3)
-        put(1, False)
-        put(2, True)
-        put(3, True)
-        qn = ("qc%d" % t, "qs%d" % t)
-        qz(T[qn[0]][:], T[qn[1]][:], T.yt[:], ["yt%d" % b for b in range(4)], qn)
-        send(qn, ("bc%d" % t, "bs%d" % t), "ay%d" % t, peer)
-        for b in range(4):
-            mm(b, C, *kk(b), xc[:], xs[:], xn + ("kc%d" % b,), True, False)
+        put(0, 1, False)
+        put(1, 1, False)
+        put(2, 0, True)
+        put(3, 0, True)
+        put(2, 1, True)
+        y_codes(0)
+        put(3, 1, True)
+        y_codes(1)
+        for back in (False, True):
+            for h, (a, e) in enumerate(BACK):
+                c, s, n = (T[bn[0]], T[bn[1]], tuple(k + "/%d" % h for k in bn)) if back else (xc, xs, xn)
+                for b in range(4):
+                    mm(4 * h + b, e - a, *kk(b), c[:, a:e], s[:, a:e], n + ("kc%d" % b,), not back, back)
+        first(15)
         if t == 1:
-            turns(0)
-            turns(1)
             qz(T.vq[:], T.vs[:], T.vt[:], "vt", "vq")
             for h in range(3):
                 grow(7, h)
-            tt(T.to[0:1, :], T.key0[0:1, :], T.ij[0:1, :], A.add, K3 + ("ij",), "to")
-            ts(T.to[0:1, :], T.to[0:1, :], 1.0 / 512, 1152.0 + PLUS[0], A.mult, A.add, "to", "to")
-            ld("y", T.tot[:], T.to[0:1, :], "tot", "to")
+            tt(T.to[96:128, :], T.key0[96:128, :], T.ij[96:128, :], A.add, K3 + ("ij",), "to")
+            ts(T.to[96:128, :], T.to[96:128, :], 1.0 / 512, 1152.0 + plus, A.mult, A.add, "to", "to")
+            ld("y", T.tot[:], T.to[127:128, :], "tot", "to")
         xt = T["xt%d" % (t + 1)]
-        for b in range(4):
-            mm(b, C, *kk(b), T["bc%d" % t][:], T["bs%d" % t][:], ("bc%d" % t, "bs%d" % t, "kc%d" % b), False, True)
-        for b in range(4):
-            if b % 2 == 0: act(xt[:, b:4 * C:4], ps(b), F.Copy, "ps%d" % b, "x%d" % b)
-            else: cp(xt[:, b:4 * C:4], ps(b), "ps%d" % b, "x%d" % b)
         nx = ("xc%d" % (t + 1), "xs%d" % (t + 1))
-        qz(T[nx[0]][:], T[nx[1]][:], xt[:], ["x%d" % b for b in range(4)], nx)
+
+        def new(h, b):
+            a, e = BACK[h]
+            o, i, n = xt[:, 4 * a + b:4 * e:4], ps(4 * h + b, e - a), "ps%d" % (4 * h + b)
+            if b % 2 == 0: act(o, i, F.Copy, n, "x%d.%d" % (b, h))
+            else: cp(o, i, n, "x%d.%d" % (b, h))
+
+        def x_codes(h):
+            a, e = BACK[h]
+            qz(T[nx[0]][:, a:e], T[nx[1]][:, a:e], xt[:, 4 * a:4 * e], ["x%d.%d" % (b, h) for b in range(4)], nx + ("xq%d" % h,))
+
+        for b in range(4):
+            new(0, b)
+        for b in range(3):
+            new(1, b)
+        x_codes(0)
+        new(1, 3)
+        x_codes(1)
         if t == 0:
             send(nx, ("lc1", "ls1"), "ax1", peers[1])
     ld("y", T.oc[:], T.xc2[:].bitcast(dt.uint8), "oc", "xc2")
     for k in range(4):
         ld("s" if k % 2 else "y", T.osc[4 * k:4 * k + 4, :], T.xs2[32 * k:32 * k + 4, :], "osc%d" % k, "xs2")
-    mm(4, C, T.vq[:], T.vs[:], T.xc2[:], T.xs2[:], ("xc2", "xs2", "vq"))
-    act(T.yo[:], ps(4), F.Copy, "ps4", "yo")
-    ld("s", T.y[:], T.yo[:], "yout", "yo")
+    for h, (a, e) in enumerate(BACK):
+        mm(h, e - a, T.vq[:], T.vs[:], T.xc2[:, a:e], T.xs2[:, a:e], ("xq%d" % h, "vq"))
+        if h: cp(T.yo[:, a:e], ps(h, e - a), "ps%d" % h, "yo%d" % h)
+        else: act(T.yo[:, a:e], ps(h, e - a), F.Copy, "ps%d" % h, "yo%d" % h)
+        ld("sy"[h], T.y[:, a:e], T.yo[:, a:e], "y%d" % h, "yo%d" % h)
     for q in "vstg":
         g.wait_ge(T.sem["c" + q], cnt[q])
     for i in range(ndma[0]):

from concourse.mybir import dt, AluOpType as A, ActivationFunctionType as F

C = 288
H = 128
PARTS = ((0, H), (H, C))
GROWS = ((0, H), (H, 192), (192, C))
BACK = ((0, C - H), (C - H, C))
KW = 512
B16, B96 = 2.0 ** 18, 2.0 ** 21
HIGH = 2.0 ** 22
BIG, TINY = 1e29, 2.0 ** -119
NK = 18
TIE = 9
WORDS = ((2, 3), (4, 5), (6, TIE), (0, 1), (7, 8))
BWORDS = ((0, 1, 2, 6), (7, 8, 3, 4), (5, TIE))
SCAL = ((0, 1, 6, 7, 8), (0, 1, 7, 8), (0, 1, 2, 6, 7, 8, 3), (0, 1, 2, 6, 7, 8, 3, 4))
PLUS = [16.0 * len(x) - 32.0 for x in SCAL]
RAW = (4, 1, 5, 3)

MXC, PL = "float8_e4m3fn_x4", "uint8"
SCRATCH = {}


def _buf(n, cols, d):
    SCRATCH[n] = ("psum" if n == "ps" else "sbuf", [128, cols], d)


_buf("ps", 4096, "float32")
for _t in range(3):
    _buf("xt%d" % _t, 4 * C, "bfloat16")
    _buf("xc%d" % _t, C, MXC)
    _buf("xs%d" % _t, C, PL)
for _t in range(2):
    for _n in ("l", "z", "q", "b"):
        _buf(_n + "c%d" % _t, C, MXC)
        _buf(_n + "s%d" % _t, C, PL)
    _buf("aw%d" % _t, 18, "uint16")
    _buf("al%d" % _t, 18, "uint16")
for _n, _c, _d in (("wk", 1024, MXC), ("wp", 1024, PL), ("ut", 512, "bfloat16"), ("vt", 512, "bfloat16"), ("uq", 128, MXC), ("us", 128, PL),
                   ("vq", 128, MXC), ("vs", 128, PL), ("up", 512, MXC), ("ups", 512, PL), ("kt", 6 * KW, "bfloat16"), ("sp", 2 * KW + 8, "bfloat16"),
                   ("un", KW + 4, "bfloat16"), ("kc", NK * 128, MXC), ("ks", NK * 128, PL), ("tm2", KW + 4, "bfloat16"), ("one", KW + 4, "bfloat16"),
                   ("ui", 32, "int32"), ("ul", 32, "uint16"), ("pi", 2, "int32"), ("pj", 4, "int32"),
                   ("fc", 24, "float32"), ("mk", 4, "float32"), ("ij", C, "float32"),
                   ("rowog", 128, "float32"), ("hb", C, "float32"), ("k16", C, "float32"), ("k7", C, "float32"), ("k96", 96, "float32"),
                   ("t1", 32, "float32"), ("t2", 128, "float32"), ("t3", 128, "float32"), ("t4", 128, "float32"), ("t5", 128, "float32"),
                   ("wa", 20 * C, "bfloat16"), ("wb", 16 * C, "bfloat16"), ("qa", 5 * C, MXC), ("qas", 5 * C, PL), ("qb", 6 * C, MXC),
                   ("qbs", 6 * C, PL), ("rm", 4 * C, "float32"), ("tr", 6 * C, "float32"), ("ds", 36 * C, "float32"), ("dd", C, "float32"),
                   ("de", C, "float32"), ("key0", C, "float32"), ("key1", C, "float32"), ("col", C, "float32"), ("nl", 18, "uint16"),
                   ("nf", 18, "float32"), ("ne", 18, "float32"), ("no", 18, "float32"), ("nr", 20, "float32"), ("nz", 18, "uint16"),
                   ("nx", 18, "uint16"), ("ox", 18, "uint16"), ("nid", 18, "float32"),
                   ("ow", 18, "uint16"), ("kw", 18, "uint16"), ("bs", 2 * C, "float32"), ("of", C, "float32"),
                   ("nv", C, "float32"), ("kr", C, "float32"), ("cd", 8 * C, "bfloat16"), ("qc", 2 * C, MXC), ("qcs", 2 * C, PL),
                   ("cw", 8 * C, "float32"),
                   ("ct", 4 * C, "bfloat16"), ("qt", C, MXC), ("qts", C, PL), ("ff", 4 * C, "bfloat16"), ("fs", 4 * C, "bfloat16"),
                   ("zt", 4 * C, "bfloat16"), ("y1", 4 * C, "float32"), ("ym", 4 * C, "bfloat16"), ("yt", 4 * C, "bfloat16"),
                   ("yo", C, "float32"), ("to", C, "float32")):
    _buf(_n, _c, _d)
DMAS = ["d%d" % i for i in range(20)]
SEMAPHORES = ["cv", "cs", "ct", "cg", "sent", "ax0", "ax1", "ay00", "ay01", "ay10", "ay11", "aa0", "aa1"] + DMAS


def rank_program(g, core, T, topo):
    rank = T.rank_of(core)
    if rank is None:
        return
    Q = {"g": g, "v": g.vector, "s": g.scalar, "t": g.tensor, "y": g.sync}
    clk = {k: {} for k in Q}
    cnt = {k: 0 for k in Q}
    last, readers, ndma, sent, due = {}, {}, [0], [0], {}

    def waits(q, toks):
        for s, v, c, _ in sorted(toks, key=lambda k: -len(k[2])):
            if clk[q].get(s, 0) < v:
                Q[q].wait_ge(T.sem[s], max(k[1] for k in toks if k[0] == s))
                for k in toks:
                    if k[0] == s:
                        for a, b in k[2].items():
                            if clk[q].get(a, 0) < b: clk[q][a] = b

    def op(q, fn, rd=(), wr=(), dma=False):
        rd = (rd,) if isinstance(rd, str) else rd
        wr = (wr,) if isinstance(wr, str) else wr
        me = "dma" if dma else q
        toks = []
        for k in rd:
            if k in last: toks.append(last[k])
            if k[:2] == "ps": toks += [w for w in readers.get(k, {}).values() if w[3] != me]
        for k in wr:
            if k in last and last[k][3] != q: toks.append(last[k])
            toks += list(readers.get(k, {}).values())
        waits(q, toks)
        ins = fn()
        if dma:
            s, v = DMAS[ndma[0]], 16
            ndma[0] += 1
        else:
            cnt[q] += 1
            s, v = "c" + q, cnt[q]
        ins.then_inc(T.sem[s], 16 if dma else 1)
        c = dict(clk[q])
        c[s] = v
        tok = (s, v, c, me)
        for k in rd:
            readers.setdefault(k, {})[s] = tok
        for k in wr:
            last[k] = tok
            readers[k] = {}

    V, S = g.vector, g.scalar

    def ts(out, i, s1, s2, o0, o1, rd, wr):
        if o1 is None: op("v", lambda: V.tensor_scalar(out, i, s1, None, o0), rd, wr)
        else: op("v", lambda: V.tensor_scalar(out, i, s1, s2, o0, o1), rd, wr)

    def tt(out, a, b, o, rd, wr):
        op("v", lambda: V.tensor_tensor(out, a, b, o), rd, wr)

    def cp(out, i, rd, wr):
        op("v", lambda: V.tensor_copy(out, i), rd, wr)

    def ms(ap, c, wr):
        op("v", lambda: V.memset(ap, c), (), wr)

    def act(out, i, f, rd, wr, bias=0.0, scale=1.0):
        op("s", lambda: S.activation(out, i, f, bias=bias, scale=scale), rd, wr)

    def qz(c, s, i, rd, wr):
        op("v", lambda: V.quantize_mx(c, s, i), rd, wr)

    def iota(out, pat, base, cm, wr, flag=True):
        op("g", lambda: g.iota(out, pat, base, cm, allow_small_or_imprecise_dtypes=flag), (), wr)

    def ld(q, out, i, wr, rd=()):
        op(q, lambda: Q[q].dma_start(out, i), rd, wr, dma=True)

    def ps(b, n=C):
        return T.ps[:, 512 * b:512 * b + n]

    def mm(b, n, lc, ls, rc, rs, rd, start=True, stop=True):
        op("t", lambda: g.tensor.matmul_mx(ps(b, n), lc, ls, rc, rs, start, stop), rd, "ps%d" % b)

    def kk(i):
        return T.kc[:, 128 * i:128 * i + 128], T.ks[:, 128 * i:128 * i + 128]

    def kz(k):
        if k < 4: i, n = T.un[:, 3 - k:3 - k + KW], "un"
        elif k < 8: i, n = T.kt[:, (k - 4) * KW:(k - 3) * KW], "kt%d" % k
        elif k > 15: i, n = T.kt[:, (k - 12) * KW:(k - 11) * KW], "kt%d" % k
        else:
            h, e = divmod(k - 8, 4)
            i, n = T.sp[:, (KW + 4) * h + e:(KW + 4) * h + e + KW], "sp%d" % h
        qz(*kk(k), i, n, "kc%d" % k)

    def scan(out, i, k, rd, wr, first=-4.0 * B96):
        op("v", lambda: V.tensor_tensor_scan(out, i, k, first, A.max, A.add), rd, wr)

    def send(src, dst, sem, peer, cols=slice(None), part=""):
        waits("g", [last[k + part] for k in src])
        rid, pid = topo.addr(peer, core)
        for a, b in zip(src, dst):
            o, i = (T[k][:, cols].bitcast(dt.uint8) if SCRATCH[k][2] == MXC else T[k][:, cols] for k in (b, a))
            g.remote_dma(o, i, T.sem[sem], T.sem.sent, pid, rid, topo.mask(core, peer))
        n = len(src) * len(topo.engines(core, peer))
        sent[0] += n
        due[sem] = n
        for k in dst:
            last[k + part] = (sem, n, {sem: n}, "r")

    peers = [T.cores[rank ^ (1 << t)] for t in range(2)]

    ld("y", T.xt0[:], T.x[:], "xt0")
    ld("s", T.ut[:], T.u[:], "ut")

    iota(T.pi[:, 0:1], [[1, 1]], 0, 1, "pi", False)
    iota(T.ij[:], [[1, C]], 0, 0, "ij")
    iota(T.rowog[:], [[1, 8], [0, 16]], 0, 0, "rowog")
    iota(T.ui[:, 0:16], [[16, 2], [32, 4], [0, 2]], 0, 0, "ui", False)
    iota(T.ui[:, 16:32], [[64, 2], [16, 4], [0, 2]], 1, 0, "ui", False)

    def col(i):
        return T.fc[:, i:i + 1]

    for i, x in ((13, TINY), (16, -TINY)):
        ms(col(i), x, "f%d" % i)
    ms(T.no[96:128, :], 0.0, "no7")
    ms(T.nr[:, 0:1], 0.0, "nr0")
    for i, (o, k) in enumerate(((A.bitwise_and, 15), (A.bitwise_and, 31), (A.arith_shift_right, 5))):
        ts(T.pj[:, i:i + 1], T.pi[:, 0:1], k, None, o, None, "pi", "pj")
    cp(col(0), T.pi[:, 0:1], "pi", "f0")
    cp(T.fc[:, 1:4], T.pj[:, 0:3], "pj", "f1")
    for t, w in enumerate((0.5, 1.0, 0.5, 0.0)):
        ms(T.kt[0:96, 3 * KW + t:4 * KW:4], w, "kt7")
    for i, j, a, b in ((7, 2, BIG, -0.5 * BIG), (11, 3, -2.0, 0.0), (12, 3, -2.0, -1.0), (8, 3, -1.0, 0.0)):
        ts(col(i), col(j), a, b, A.mult, A.add, "f1", "f%d" % i)
    ts(T.t1[:, 0:17], T.ij[:, 0:17], col(1), B16, A.is_equal, A.mult, ("ij", "f1"), "t1")
    for m in range(2):
        ts(T.mk[:, m:m + 1], col(2), 15.5, None, (A.is_lt, A.is_gt)[m], None, "f1", "mk")
    for i, x, o in ((4, 15.5, A.is_lt), (14, 15.5, A.is_gt), (10, 111.5, A.is_gt)):
        ts(col(i), col(0), x, None, o, None, "f0", "f%d" % i)
    tt(T.k16[:, 0:16], T.t1[:, 0:16], T.t1[:, 1:17], A.subtract, "t1", "k16")
    cp(T.ul[:], T.ui[:], "ui", "ul")
    for i, a in ((5, PLUS[2]), (9, PLUS[3])):
        ts(col(i), col(1), -18.0, a - 9.0, A.mult, A.add, "f1", "f%d" % i)
    ts(col(15), T.mk[:, 1:2], 512.0 * (PLUS[1] - PLUS[0]), B16 + 512.0 * PLUS[0], A.mult, A.add, "mk", "f15")
    ts(T.k16[:, 15:16], T.k16[:, 15:16], -2.0 * B16, None, A.add, None, "k16", "k16")
    ts(T.nid[:], T.ij[:, 0:C:16], col(1), col(14), A.add, A.mult, ("ij", "f1", "f14"), "nid")
    qz(T.uq[:], T.us[:], T.ut[:], "ut", ("uq", "us"))

    def upick(i, v):
        a, b = 128 * i, 128 * i + 128
        off = T.ul[:, 8 * i:8 * i + 8]
        if v: op("v", lambda: V.tensor_copy(T.up[:, a:b].bitcast(dt.uint32), T.uq[:, 0:128].bitcast(dt.uint32).indirect(off)), ("uq", "ul"), "up%d" % i)
        else: op("s", lambda: S.activation(T.ups[:, a:b], T.us[:, 0:128].indirect(off), F.Copy), ("us", "ul"), "ups%d" % i)

    for e in range(0, C, 32):
        act(T.hb[:, e:e + 32], T.ij[:, 0:32], F.Identity, ("ij", "f7"), "hb", bias=col(7), scale=-BIG)
    for x, n, c in ((T.t3, "t3", 11), (T.t4, "t4", 12)):
        act(x[:], T.rowog[:], F.Abs, ("rowog", "f%d" % c), n, bias=col(c))
    for e in (0, 64):
        act(T.t5[:, e:e + 64], T.rowog[:, 0:64], F.Abs, ("rowog", "f8"), "t5", bias=col(8))
    grown = [16, 32, 64, 128, 256]

    def weights(k, t, w, src, n):
        e = k - 4 if k < 8 else k - 12
        act(T.kt[:, e * KW + t:(e + 1) * KW:4], src[:], F.Relu, n, "kt%d" % k, bias=w, scale=-w)

    def longer():
        n = grown.pop(0)
        m = min(n, C - n)
        act(T.k16[:, n:n + m], T.k16[:, 0:m], F.Copy, "k16", "k16")

    def places(k):
        for t in range(4):
            weights(k, t, 512.0 if k == 5 and t % 2 else 256.0, *((T.t3, "t3") if t < 2 else (T.t4, "t4")))
            if t % 2: longer()

    places(4)
    for i in range(2):
        upick(i, True)
        upick(i, False)
    qz(T.xc0[:], T.xs0[:], T.xt0[:], "xt0", ("xc0", "xs0"))
    send(("xc0", "xs0"), ("lc0", "ls0"), "ax0", peers[0])
    places(5)
    for i in range(2, 4):
        upick(i, True)
        upick(i, False)
    longer()
    iota(T.tm2[:], [[0, KW + 4]], 512, 0, "tm2")

    def groups(h):
        w = T.sp[:, (KW + 4) * h:(KW + 4) * (h + 1)]
        op("g", lambda: g.affine_select(w, T.tm2[:], [[0, 129], [-16, 4]], A.is_ge, 0.0, -64 * h, 1), "tm2", "sp%d" % h)
        op("g", lambda: g.affine_select(w, w, [[0, 129], [16, 4]], A.is_ge, 0.0, 64 * h + 15, -1), "sp%d" % h, "sp%d" % h)

    groups(0)

    def late_constants(i):
        if i == 0:
            for k, ws in ((17, (0.5, 1.0, 0.0, 0.0)), (16, (0.5, 0.5, 0.5, 0.5))):
                for t, w in enumerate(ws):
                    weights(k, t, w, T.t5, "t5")
        if i == 1:
            ms(T.kt[96:128, 3 * KW:4 * KW], 0.0, "kt7")
            ts(T.t2[:, 0:97], T.ij[:, 0:97], col(0), B96, A.is_equal, A.mult, ("ij", "f0"), "t2")
            for m in range(2):
                ts(T.mk[:, m + 2:m + 3], col(2), 15.5, B16 + 96, (A.is_lt, A.is_gt)[m], A.mult, "f1", "mk2")
            ts(col(6), col(10), HIGH + B16 + 96, -HIGH, A.mult, A.add, "f10", "f6")
            tt(T.k96[:], T.t2[:, 0:96], T.t2[:, 1:97], A.subtract, "t2", "k96")
        if i == 2:
            ts(col(17), col(10), -HIGH - 4.0 * B96, HIGH, A.mult, A.add, "f10", "f17")
            ts(T.k96[:, 95:96], T.k96[:, 95:96], -B96 - 0.5, None, A.add, None, "k96", "k96")
        if i == 3:
            act(T.k7[:], T.k16[:], F.Copy, ("k16", "f10"), "k7", scale=col(10))
            act(col(18), T.k16[:, 15:16], F.Copy, ("k16", "f10"), "f18", scale=col(10))

    def last_constants():
        for t in range(1, 4):
            iota(T.cd[:, t:4 * C:4], [[0, C]], 0, 0, "cdz0")
        iota(T.ct[:, 3:4 * C:4], [[0, C]], 0, 0, "ctz")
        groups(1)
        for t in range(1, 4):
            iota(T.cd[:, 4 * C + t:8 * C:4], [[0, C]], 0, 0, "cdz1")
        iota(T.one[:], [[0, KW + 4]], 1, 0, "one")
        op("g", lambda: g.affine_select(T.un[:], T.one[:], [[-1, KW + 4]], A.is_equal, 0.0, 3, 4), "one", "un")
        for o, i, n in ((T.wk[:].bitcast(dt.uint8), T.wc[:], "wk"), (T.wp[:], T.ws[:], "wp"), (T.vt[:], T.v[:], "vt")):
            ld("y", o, i, n, "al0")

    ct, zt = T.ct, T.zt
    D01 = ("dd0", "dd1")
    K3 = ("key0.0", "key0.1", "key0.2")
    for t in range(2):
        peer = peers[t]
        dv = T.dd[:, 15:C:16]
        xc, xs = T["xc%d" % t], T["xs%d" % t]
        xn = ("xc%d" % t, "xs%d" % t)
        lc, ls = T["lc%d" % t], T["ls%d" % t]
        ln = ("lc%d" % t, "ls%d" % t)
        plus = PLUS[t]
        aw, al = "aw%d" % t, "al%d" % t

        def first(*ks):
            for i in ks if t == 0 else ():
                kz(i)

        banks = ((5, 7), (6, 0), (1, 3), (6, 7))

        def scores(k, e):
            c, s, n = (xc, xs, xn) if k < 2 else (lc, ls, ln)
            mm(banks[k][e], C, T.up[:, 128 * k:128 * k + 128], T.ups[:, 128 * k:128 * k + 128], c[:], s[:], n + ("up%d" % k, "ups%d" % k))

        def mask(k):
            tt(T.rm[:, C * k:C * k + C], ps(banks[k][0]), T.hb[:], A.max, ("ps%d" % banks[k][0], "hb"), "rm%d" % k)

        def turn(k):
            op("v", lambda: V.transpose(T.tr[:, C * k:C * k + C], T.rm[:, C * k:C * k + C]), "rm%d" % k, "tr%d" % k)

        def raw(k):
            op("v", lambda: V.transpose(T.tr[:, C * RAW[k]:C * RAW[k] + C], ps(banks[k][0])), "ps%d" % banks[k][0], "tr%d" % RAW[k])

        def hide(k):
            for a in range(0, 128, 32):
                op("g", lambda: g.affine_select(T.tr[a:a + 32, C * k:C * k + C], T.tr[a:a + 32, C * RAW[k]:C * RAW[k] + C], [[0, 9], [-1, 32]], A.is_ge, BIG, 0, 1),
                   "tr%d" % RAW[k], "tr%d" % k)

        def plane(k, b):
            if k < 2:
                w = [b in x for x in WORDS].index(True)
                return T.wa, 4 * C * w, 2 * k + WORDS[w].index(b), "a%d" % w
            w = [b in x for x in BWORDS].index(True)
            if w == 2: return T.wa, 4 * C * (6 - 2 * k), BWORDS[w].index(b), "a%d" % (6 - 2 * k)
            return T.wb, 4 * C * (2 * k - 4 + w), BWORDS[w].index(b), "b%d" % (2 * k - 4 + w)

        def diff(k, b):
            _, z, p, n = plane(k, b)
            z += 20 * C * (k > 1)
            bw = banks[k][1]
            act(T.ds[:, z + p:z + 4 * C:4], ps(bw), F.Identity, ("ps%d" % bw, "tr%d" % RAW[k]), "d%s.%d" % (n, p),
                bias=T.tr[:, C * RAW[k] + 32 * b:C * RAW[k] + 32 * b + 1], scale=-1.0)

        def sign(k, b):
            wt, z, p, n = plane(k, b)
            d = 20 * C * (k > 1)
            for lo, hi, c in ((0, 32 * b, 16), (32 * b, C, 13)):
                if hi > lo:
                    act(wt[:, z + 4 * lo + p:z + 4 * hi:4], T.ds[:, d + z + 4 * lo + p:d + z + 4 * hi:4], F.Sign, ("d%s.%d" % (n, p), "f13", "f16"),
                        "w%s.%d" % (n, p), bias=col(c))

        def chain(jobs):
            calls = []
            for i, j in enumerate(jobs):
                calls.append((diff, j))
                if i: calls.append((sign, jobs[i - 1]))
            return calls + [(sign, jobs[-1])]

        def run(calls, n=99):
            for f, j in calls[:n]:
                f(*j)
            del calls[:n]

        def block(k, *bs):
            for b in bs:
                wt, z, p, n = plane(k, b)
                bv = banks[k][0]
                rd, wr, o = ("ps%d" % bv, "tr%d" % k), "w%s.%d" % (n, p), C * k
                z += p
                if b == TIE:
                    tt(wt[:, z:z - p + 4 * C:4], ps(bv), T.tr[:, o:o + C], A.not_equal, rd, wr)
                    continue
                if t and k == 0: rd, o = (rd[0], "tr%d" % RAW[0]), C * RAW[0]
                sc = T.tr[:, o + 32 * b:o + 32 * b + 1]
                ts(wt[:, z:z + 128 * b - 3:4], ps(bv, 32 * b), sc, 2.0, A.is_lt, A.mult, rd, wr)
                ts(wt[:, z + 128 * b:z - p + 4 * C:4], T.ps[:, 512 * bv + 32 * b:512 * bv + C], sc, 2.0, A.is_le, A.mult, rd, wr)

        made, held = [0, 0, 0], []

        def word(ty, w):
            qn, pb, x, all_ = ("qa", 4, WORDS[w], 5) if ty == 0 else ("qb", (2, 4)[ty - 1], BWORDS[w], 3)
            wt, z, _, n = plane(ty + 1 if ty else 0, x[0])
            o = C * (w + 3 * (ty == 2))
            qc, qs, qn = T[qn][:, o:o + C], T[qn + "s"][:, o:o + C], "%s%d" % (qn, o)
            c = (4 if ty == 0 else 16) + (TIE in x)
            qz(qc, qs, wt[:, z:z + 4 * C], ["w%s.%d" % (n, p) for p in range(4)], qn)
            held.append((pb, C, *kk(c), qc, qs, (qn, "kc%d" % c), made[ty] == 0, made[ty] == all_ - 1))
            if ty < 2: mm(*held.pop())
            made[ty] += 1

        def release():
            while held:
                mm(*held.pop(0))

        def steps(e, i):
            o = C * e
            if i == 0 and e == 0: ts(T.bs[:, 0:C], ps(2), col(5), None, A.add, None, ("ps2", "f5"), "bt0")
            if i == 0 and e == 1: act(T.bs[:, C:2 * C], ps(4), F.Identity, ("ps4", "f9"), "bt1", bias=col(9))
            if i in (1, 2):
                a, b = PARTS[i - 1]
                op("v", lambda: V.tensor_scalar(T.cd[:, 4 * (o + a):4 * (o + b):4], T.bs[:, o:o + C].indirect(T.ox[:, a // 16:b // 16]), -9.0, 9.0, A.max, A.min),
                   ("bt%d" % e, "ox%d" % (i - 1)), "cd%d.%d" % (e, i - 1))
            if i in (3, 4):
                a, b = PARTS[i - 3]
                qz(T.qc[:, o + a:o + b], T.qcs[:, o + a:o + b], T.cd[:, 4 * (o + a):4 * (o + b)], ("cd%d.%d" % (e, i - 3), "cdz%d" % e), "qc%d.%d" % (e, i - 3))

        def table(k):
            o = C * (k // 4)
            mm((0, 3)[k % 2], C, *kk(8 + k), T.qc[:, o:o + C], T.qcs[:, o:o + C], ("qc%d.0" % (k // 4), "qc%d.1" % (k // 4), "kc%d" % (8 + k)))

        def keep(k):
            b = (0, 3)[k % 2]
            act(T.cw[:, C * k:C * k + C], ps(b), F.Copy, "ps%d" % b, "cw%d" % k)

        def picked(i, h):
            a, e = PARTS[h]
            if i == 0: op("s", lambda: S.activation(T.nv[:, a:e], T.of[:].indirect(T.nx[:, a // 16:e // 16]), F.Copy), ("of", "nx"), ("nv%d" % h, "nv"))
            if i == 1: scan(T.kr[:, a:e], T.nv[:, a:e], T.k16[:, a:e], ("nv%d" % h, "k16"), ("kr%d" % h, "kr"))
            if i == 2: ts(T.ox[:, a // 16:e // 16], T.kr[:, a + 15:e:16], B16, None, A.add, None, "kr%d" % h, "ox%d" % h)

        def gains(h):
            a, e = PARTS[h]
            mm((0, 4)[h], e - a, *kk(8), T.qc[:, a:e], T.qcs[:, a:e], ("qc0.%d" % h, "kc8"))

        for k, e in ((0, 0), (0, 1), (1, 0), (1, 1)):
            scores(k, e)
        raw(0)
        if t == 0:
            mask(0)
            mask(1)
            turn(0)
            turn(1)
            kz(4)
            run(chain([(0, 0), (0, 1), (0, 6), (1, 0), (1, 1), (0, 7), (0, 8), (1, 7), (1, 8)]))
            late_constants(0)
            block(0, TIE, 2, 3, 4, 5)
        else:
            hide(0)
            mask(1)
            block(0, 2)
            turn(1)
            run(chain([(0, 0), (0, 1), (0, 7), (1, 0), (1, 1), (0, 8), (1, 7), (1, 8)]))
            block(0, 3, 4, 5, 6)
        block(1, 2, 3)
        block(1, TIE)
        word(0, 0)
        block(1, 6)
        if t: block(1, 4)
        word(0, 3)
        first(5)
        if t:
            scores(2, 0)
            scores(2, 1)
            block(0, TIE)
            block(1, 5)
        else: block(1, 4, 5)
        word(0, 2)
        word(0, 1)
        word(0, 4)
        if t == 0:
            scores(2, 0)
            scores(2, 1)
            late_constants(1)
        else:
            raw(2)
            mask(2)
        scores(3, 0)
        scores(3, 1)
        scan(T.dd[:], ps(4), T.k16[:], ("ps4", "k16"), D01)
        if t == 0: raw(2)
        else: turn(2)
        ts(T[aw][:], dv, B16 + 512.0 * plus if t else col(15), 1.0 / 512, A.add, A.mult, D01 + ("f15",), aw)
        send((aw,), (al,), "aa%d" % t, peer)
        tt(T.to[0:1, :], T.ps[0:1, 4 * 512:4 * 512 + C], T.ij[0:1, :], A.subtract, ("ps4", "ij"), "to")
        op("g", lambda: g.partition_broadcast(T.key0[:], T.to[0:1, :], 128), "to", K3)
        run(chain([(2, b) for b in SCAL[2]]))
        ts(T.nf[:], dv, -1.0 / 512, 287.0 - B16 / 512 - plus, A.mult, A.add, D01, "nf")
        if t == 0:
            last_constants()
            mask(2)
            first(17, 16)
            turn(2)
        else: block(2, TIE)
        ts(T.ne[:], T.nf[:], col(4), None, A.mult, None, ("nf", "f4"), "ne")
        mask(3)
        tt(T.nf[:], T.ne[:], T.nid[:], A.add, ("ne", "nid"), "nf")
        if t == 0: block(2, TIE)
        block(2, 5)
        cp(T.nx[:], T.nf[:], "nf", "nx")
        turn(3)
        block(2, 4)
        word(1, 2)
        word(1, 0)
        block(3, TIE)
        if t: block(3, 5)
        op("v", lambda: V.tensor_copy(T.of[:].indirect(T[al][:]), T.ij[:]), ("ij", al), "of")
        late = chain([(3, b) for b in SCAL[3]])
        run(late, 3 if t else 1)
        picked(0, 0)
        picked(0, 1)
        run(late, 9 if t else 10)
        word(1, 1)
        if t: word(2, 2)
        first(8)
        picked(1, 0)
        if t == 0: late_constants(2)
        picked(1, 1)
        picked(2, 0)
        steps(0, 0)
        picked(2, 1)
        steps(0, 1)
        steps(0, 2)
        steps(0, 3)
        gains(0)
        steps(0, 4)
        gains(1)
        if t == 0: block(3, 5)
        first(7, 9)
        keys = ((T.key0, "key0"), (T.key1, "key1"))

        def grow(k, h):
            (x, xk), (y, yk) = keys[k % 2], keys[1 - k % 2]
            a, b = GROWS[h]
            if k == 0:
                bank, o = (4, 4 * 512 - H) if h else (0, 0)
                tt(y[:, a:b], T.ps[:, o + a:o + b], x[:, a:b], A.add, ("ps%d" % bank, "%s.%d" % (xk, h)), "%s.%d" % (yk, h))
                return
            l, n = (T.nl, "nl") if k < 7 else (T.nz, "nz")
            op("v", lambda: V.tensor_tensor(y[:, a:b], T.cw[:, C * k:C * k + C].indirect(l[:, a // 16:b // 16]), x[:, a:b], A.add),
               ("cw%d" % k, n + "%d" % min(h, 1), "%s.%d" % (xk, h)), "%s.%d" % (yk, h))

        def turns(h):
            a, b = PARTS[h]
            ts(T.nl[:, a // 16:b // 16], dv[:, a // 16:b // 16], B16 + 96, None, A.add, None, "%s%d" % (dn, h), "nl%d" % h)

        def unpack(b):
            mm((2, 7)[b % 2], C, *kk(b), lc[:], ls[:], ln + ("kc%d" % b,))
            act(T.ff[:, C * b:C * b + C], ps((2, 7)[b % 2]), F.Copy, "ps%d" % (2, 7)[b % 2], "ff%d" % b)

        def order(b):
            op("s", lambda: S.activation(T.fs[:, C * b:C * b + C], T.ff[:, C * b:C * b + C].indirect(T.ow[:]), F.Copy), ("ff%d" % b, "ow"), "fs%d" % b)

        def listed(i):
            if i == 0: scan(T.kr[:], T.of[:], T.k16[:], ("of", "k16"), ("kr", "kr0", "kr1"))
            if i == 1: ts(T.ow[:], T.kr[:, 15:C:16], B16, None, A.add, None, "kr", "ow")

        def spread(k):
            table(k)
            keep(k)

        def earlier(i):
            if i == 0: tt(T.nr[:, 1:19], T.ne[:], T.no[:], A.add, ("ne", "no", "no7"), "nr")
            if i == 1: tt(T.nf[:], T.nr[:, 1:19], T.nr[:, 0:18], A.subtract, ("nr", "nr0"), "nf")
            if i == 2:
                ts(T.k7[:, 15:C:16], T.nf[:], col(18), None, A.add, None, ("nf", "f18"), "k7")
                ts(col(19), T.nr[:, H // 16:H // 16 + 1], col(17), None, A.add, None, ("nr", "f17"), "f19")

        dn = "dd"
        zc, zs = T["zc%d" % t], T["zs%d" % t]

        def z_part(b, h, v):
            a, e = PARTS[h]
            o, i = zt[:, 4 * a + b:4 * e:4], T.fs[:, C * b:C * b + C].indirect(T.nz[:, a // 16:e // 16])
            rd, wr = ("fs%d" % b, "nz%d" % h), "zt%d.%d" % (b, h)
            if v: cp(o, i, rd, wr)
            else: op("s", lambda: S.activation(o, i, F.Copy), rd, wr)

        def z_codes(h):
            a, b = PARTS[h]
            qz(zc[:, a:b], zs[:, a:b], zt[:, 4 * a:4 * b], ["zt%d.%d" % (i, h) for i in range(4)], "zc")

        beside = {1: ([(spread, 1), (run, late)], [(word, 2, 0)], [(word, 2, 2)] * (1 - t) + [(first, 10), (spread, 2)]),
                  2: ([], [(word, 2, 1)], [(first, 11, 12), (spread, 3), (steps, 1, 0)]),
                  3: ([(late_constants, 3)], [(steps, 1, 1)], [(steps, 1, 2)]),
                  4: ([], [(steps, 1, 3), (steps, 1, 4), (spread, 4)], [(first, 13, 0), (spread, 5), (unpack, 0)]),
                  5: ([], [(listed, 0)], [(listed, 1), (first, 14, 1), (spread, 6), (unpack, 1)]),
                  6: ([(order, 0), (order, 1)], [(first, 2, 3)], [(unpack, 2), (unpack, 3)]),
                  7: ([(order, 2), (order, 3)], [(earlier, 1)], [(earlier, 2)])}
        if t:
            beside.update({2: ([], [(word, 2, 1)], [(listed, 0), (spread, 3), (steps, 1, 0)]),
                           3: ([(unpack, 0), (unpack, 1)], [(steps, 1, 1)], [(listed, 1), (steps, 1, 2)]),
                           4: ([(order, 0)], [(steps, 1, 3), (steps, 1, 4), (spread, 4)], [(spread, 5), (unpack, 2)]),
                           5: ([(order, 1), (order, 2)], [], [(spread, 6), (unpack, 3)]),
                           6: ([(order, 3)], [], [(spread, 7)]),
                           7: ([], [(earlier, 1)], [(earlier, 2)])})

        for k in range(1, 8):
            kr, kn = keys[k % 2]
            k0, k1, k2 = kn + ".0", kn + ".1", kn + ".2"

            def pick(b):
                scan(T.col[:, 96 * b:96 * b + 96], kr[:, 96 * b:96 * b + 96], T.k96[:], ((k0,), (k0, k1), (k2,))[b] + ("k96",), "col%d" % b)

            def less(b, h):
                a, e = PARTS[h]
                o, i, sc = ct[:, 4 * a + b:4 * e:4], kr[:, a:e], T.col[:, 96 * b + 95:96 * b + 96]
                rd, wr = ((k0,), (k1, k2))[h] + ("col%d" % b,), "ct%d.%d" % (b, h)
                if b == 1: ts(o, i, sc, None, A.is_lt, None, rd, wr)
                else: act(o, i, F.Sign, rd, wr, bias=sc, scale=-1.0)

            def fill(i):
                for f in beside[k][i]:
                    f[0](*f[1:])

            for h in range(3):
                grow(k - 1, h)
            for b in range(3):
                pick(b)
            if k == 7: earlier(0)
            for b in (0, 2):
                less(b, 0)
                less(b, 1)
            fill(0)
            fill(1)
            less(1, 0)
            less(1, 1)
            for h, (a, b) in enumerate(PARTS):
                qz(T.qt[:, a:b], T.qts[:, a:b], ct[:, 4 * a:4 * b], ["ct%d.%d" % (i, h) for i in range(3)] + ["ctz"], "qt%d" % h)
                mm((5, 1)[h], b - a, *kk(7), T.qt[:, a:b], T.qts[:, a:b], ("qt%d" % h, "kc7"))
            dx, dn = ((T.dd, "dd"), (T.de, "de"))[k % 2]
            dv = dx[:, 15:C:16]
            release()
            fill(2)
            release()
            for h, (a, b) in enumerate(PARTS):
                rd, wr = ("ps%d" % (5, 1)[h],), dn + "%d" % h
                if k < 7: scan(dx[:, a:b], ps((5, 1)[h], b - a), T.k16[:, a:b], rd + ("k16",), wr)
                else: scan(dx[:, a:b], ps((5, 1)[h], b - a), T.k7[:, a:b], rd + ("k7", "f17", "f19"), wr, col((17, 19)[h]))
            if k < 7:
                turns(0)
                turns(1)
                p0, m = 32 * (k // 2), k % 2
                p1 = p0 + 32
                nb, nn = ((T.ne, "ne"), (T.no, "no"))[m]
                act(nb[p0:p1, :], dv[p0:p1, :], F.Identity, (dn + "0", dn + "1", "mk", "mk2"), nn, bias=T.mk[p0:p1, 2 + m:3 + m], scale=T.mk[p0:p1, m:m + 1])
        for h, (a, b) in enumerate(PARTS):
            ts(T.nz[:, a // 16:b // 16], dv[:, a // 16:b // 16], col(6), None, A.add, None, (dn + "%d" % h, "f6"), "nz%d" % h)
        for h in range(2):
            for b in range(4):
                z_part(b, h, b < 2)
        z_codes(0)
        z_codes(1)
        for b in range(4):
            for h in range(2):
                w = 128 * (b + 4 * h)
                mm(2 * b + h, C, T.wk[:, w:w + 128], T.wp[:, w:w + 128], zc[:], zs[:], ("zc", "wk", "wp"))

        def copy(b):
            act(T.y1[:, C * b:C * b + C], ps(2 * b), F.Copy, "ps%d" % (2 * b), "y1%d" % b)

        def largest(b):
            tt(T.ym[:, C * b:C * b + C], ps(2 * b + 1), T.y1[:, C * b:C * b + C], A.max, ("ps%d" % (2 * b + 1), "y1%d" % b), "ym%d" % b)

        qn, bn = ("qc%d" % t, "qs%d" % t), ("bc%d" % t, "bs%d" % t)

        def put(b, h, v):
            a, e = BACK[h]
            o, i = T.yt[:, 4 * a + b:4 * e:4], T.ym[:, C * b:C * b + C].indirect(T.kw[:, a // 16:e // 16])
            rd, wr = ("ym%d" % b, "kw"), "yt%d.%d" % (b, h)
            if v: op("v", lambda: V.tensor_scalar(o, i, 0.03125, None, A.mult), rd, wr)
            else: op("s", lambda: S.activation(o, i, F.Copy, scale=0.03125), rd, wr)

        def y_codes(h):
            a, e = BACK[h]
            qz(T[qn[0]][:, a:e], T[qn[1]][:, a:e], T.yt[:, 4 * a:4 * e], ["yt%d.%d" % (b, h) for b in range(4)], [k + "/%d" % h for k in qn])
            send(qn, bn, "ay%d%d" % (t, h), peer, slice(a, e), "/%d" % h)

        op("v", lambda: V.tensor_copy(T.nv[:].indirect(T.nz[:]), T.ij[:]), ("ij", "nz0", "nz1"), ("nv", "nv0", "nv1"))
        copy(0)
        op("s", lambda: S.activation(T.kr[:], T.nv[:].indirect(T[al][:]), F.Copy), ("nv", al), "kr")
        largest(0)
        copy(1)
        scan(T.dd[:], T.kr[:], T.k16[:], ("kr", "k16"), D01)
        copy(2)
        copy(3)
        largest(1)
        ts(T.kw[:], T.dd[:, 15:C:16], B16, None, A.add, None, D01, "kw")
        largest(2)
        put(0, 0, False)
        put(1, 0, False)
        largest(3)
        put(0, 1, False)
        put(1, 1, False)
        put(2, 0, True)
        put(3, 0, True)
        put(2, 1, True)
        y_codes(0)
        put(3, 1, True)
        y_codes(1)
        for back in (False, True):
            for h, (a, e) in enumerate(BACK):
                c, s, n = (T[bn[0]], T[bn[1]], tuple(k + "/%d" % h for k in bn)) if back else (xc, xs, xn)
                for b in range(4):
                    mm(4 * h + b, e - a, *kk(b), c[:, a:e], s[:, a:e], n + ("kc%d" % b,), not back, back)
        first(15)
        if t == 1:
            qz(T.vq[:], T.vs[:], T.vt[:], "vt", "vq")
            for h in range(3):
                grow(7, h)
            tt(T.to[96:128, :], T.key0[96:128, :], T.ij[96:128, :], A.add, K3 + ("ij",), "to")
            ts(T.to[96:128, :], T.to[96:128, :], 1.0 / 512, 1152.0 + plus, A.mult, A.add, "to", "to")
            ld("y", T.tot[:], T.to[127:128, :], "tot", "to")
        xt = T["xt%d" % (t + 1)]
        nx = ("xc%d" % (t + 1), "xs%d" % (t + 1))

        def new(h, b):
            a, e = BACK[h]
            o, i, n = xt[:, 4 * a + b:4 * e:4], ps(4 * h + b, e - a), "ps%d" % (4 * h + b)
            if b % 2 == 0: act(o, i, F.Copy, n, "x%d.%d" % (b, h))
            else: cp(o, i, n, "x%d.%d" % (b, h))

        def x_codes(h):
            a, e = BACK[h]
            qz(T[nx[0]][:, a:e], T[nx[1]][:, a:e], xt[:, 4 * a:4 * e], ["x%d.%d" % (b, h) for b in range(4)], nx + ("xq%d" % h,))

        for b in range(4):
            new(0, b)
        for b in range(3):
            new(1, b)
        x_codes(0)
        new(1, 3)
        x_codes(1)
        if t == 0:
            send(nx, ("lc1", "ls1"), "ax1", peers[1])
    ld("y", T.oc[:], T.xc2[:].bitcast(dt.uint8), "oc", "xc2")
    for k in range(4):
        ld("s" if k % 2 else "y", T.osc[4 * k:4 * k + 4, :], T.xs2[32 * k:32 * k + 4, :], "osc%d" % k, "xs2")
    for h, (a, e) in enumerate(BACK):
        mm(h, e - a, T.vq[:], T.vs[:], T.xc2[:, a:e], T.xs2[:, a:e], ("xq%d" % h, "vq"))
        if h: cp(T.yo[:, a:e], ps(h, e - a), "ps%d" % h, "yo%d" % h)
        else: act(T.yo[:, a:e], ps(h, e - a), F.Copy, "ps%d" % h, "yo%d" % h)
        ld("sy"[h], T.y[:, a:e], T.yo[:, a:e], "y%d" % h, "yo%d" % h)
    for q in "vstg":
        g.wait_ge(T.sem["c" + q], cnt[q])
    for i in range(ndma[0]):
        g.wait_ge(T.sem[DMAS[i]], 16)
    g.wait_ge(T.sem.sent, sent[0])
    for s, n in due.items():
        g.wait_ge(T.sem[s], n)
